import numpy as np, ml_dtypes
CORES = [48,51,52,55]
N = 4
import mx_ref
BF = ml_dtypes.bfloat16
def cut(t, i, w=512):
    return t[:, w * i:w * i + w]
def pick(q, e):
    c = np.concatenate([q[0].reshape(128, -1, 4), np.zeros((128, 1, 4), np.uint8)], axis=1); s = np.concatenate([q[1], np.ones((16, 1), np.uint8)], axis=1)
    return (np.ascontiguousarray(c[:, e].reshape(128, -1)), np.ascontiguousarray(s[:, e]))
def join(*qs):
    return (np.concatenate([q[0] for q in qs], axis=1), np.concatenate([q[1] for q in qs], axis=1))
def put(q, e, v):
    c, s = q[0].reshape(128, -1, 4).copy(), q[1].copy(); c[:, e] = v[0].reshape(128, -1, 4); s[:, e] = v[1]
    return (c.reshape(128, -1), s)
def pk(c, s):
    return (np.ascontiguousarray(c), mx_ref.live(s))
def emit(q):
    return q[0], q[1]
def decode(q):
    o = []
    for b in range(4):
        e = np.zeros((128, 128, 4), np.float32); e[np.arange(128), np.arange(128), b] = 1
        o.append(mx_ref.matmul(mx_ref.quantize(e.reshape(128, 512).astype(BF)), q))
    return np.stack(o, axis=2).reshape(128, -1)
def f(rng, *shape):
    return mx_ref.flush((rng.standard_normal(shape, dtype=np.float32) * np.exp2(rng.integers(-2, 3, shape[:-1] + (1,)))).astype(BF))
def wide(rng, *shape, cols=0):
    v = rng.standard_normal(shape, dtype=np.float32) * np.exp2(rng.integers(-12, 13, shape)).astype(np.float32)
    if cols: v *= np.repeat(np.exp2(rng.integers(-cols, cols + 1, shape[:-2] + (1, shape[-1] // 4))) * (rng.random(shape[:-2] + (1, shape[-1] // 4)) > 0.0625), 4, axis=-1).astype(np.float32)
    return mx_ref.flush(v.astype(BF))
P, K, O = 256, 64, 2
def places(t, j):
    return (j + t * np.arange(N)[:, None]) % P
def checks(tab, u):
    return np.stack([mx_ref.matmul(mx_ref.quantize(np.ascontiguousarray(u[r])), tab[r])[:2] for r in range(N)], axis=1)
def judge(c, g, t):
    j = np.arange(P)
    p = (j + t) % N
    at = places(t, j)
    c, a = c[np.arange(N)[:, None], at], np.abs(g[np.arange(N)[:, None], at])
    s = c[p, j]
    for r in range(N):
        s = np.where(p == r, s, s - c[r])
    bad = np.argsort(-np.abs(s), kind="stable")[:K]
    a[p, j] = -1
    return bad, np.argmax(a, axis=0)[bad]
def rebuilt(tab, bad, lost, t):
    at = places(t, bad)
    v = decode(join(*[pick(tab[r], at[r]) for r in range(N)])).reshape(128, N, K, 4)
    new = np.zeros((128, K, 4), np.float32)
    for k in range(K):
        p = (bad[k] + t) % N
        x = v[:, p, k]
        for r in range(N):
            if r != p and r != lost[k]: x = x - v[:, r, k]
        new[:, k] = x
    return mx_ref.quantize(np.ascontiguousarray(new.reshape(128, -1).astype(BF)))
def data(rng):
    return f(rng, N, 128, 4 * P).astype(np.float32).reshape(N, 128, P, 4)
def striped(v):
    v = v.copy()
    for r in range(N):
        j = np.arange(r, P, N)
        v[r][:, j] = 0
        v[r][:, j] = np.sum(v[:, :, j], axis=0)
    return v
def harm(rng, v, stripes, size):
    for j in stripes:
        v[(j + rng.integers(1, N)) % N][:, j] = size * rng.standard_normal((128, 4))
def queries(rng):
    q = np.array(f(rng, 1, 128, 512))
    q[:, :, 8:] = 0
    return np.concatenate([q] * N)
def draw(rng, v, q=None):
    v = v.astype(np.float32).reshape(N, 128, 4 * P)
    v[np.abs(v) < np.float32(2.0 ** -16)] = 0
    return {"tb": v.astype(BF), "u": queries(rng) if q is None else q, "w": f(rng, N, 128, 512 * O)}
def setup_inputs(rng):
    v = striped(data(rng))
    harm(rng, v, rng.permutation(P)[:K + 6], 8)
    return draw(rng, v)
def setup_inputs_again(rng):
    v, q = striped(data(rng) * np.float32(2.0 ** -8)), queries(rng)
    s = np.where(q[0, :, 4:8].astype(np.float32) < 0, -1.0, 1.0)
    q[:, :, :4] = (np.abs(q[:, :, :4].astype(np.float32)) * s).astype(BF)
    q[:, :32, :4] = 0
    on = (np.arange(128) < 32)[:, None]
    at = N * rng.permutation(P // N)[:K // 2] + 2 * rng.integers(0, N // 2, K // 2) + np.arange(K // 2) % 2
    for j in at:
        p = int(j) % N
        m = (p + int(rng.integers(1, N))) % N
        if p % 2:
            m = ((p + 1) // 2 + N // 2 * int(rng.integers(0, 2))) % N
            if m == p: m = (m + N // 2) % N
        v[m][:, j] = 2.0 ** -4 * (1 + rng.random((128, 4))) * s * on
        v[p][:, j] = (2.0 ** 5 if p % 2 else -2.0 ** 5) * (1 + rng.random((128, 4))) * s
    return draw(rng, v, q)
def setup_inputs_one(rng):
    v, q = striped(data(rng)), queries(rng)
    s = np.where(q[0, :, :4].astype(np.float32) < 0, -1.0, 1.0)
    q[:, :, 4:8] = (np.abs(q[:, :, 4:8].astype(np.float32)) * s).astype(BF)
    m, i = int(rng.integers(0, N)), np.arange(P)
    at = rng.permutation(np.flatnonzero((i % N != m) & ((i - m + 1) % N != m)))[:2 * K]
    size = np.repeat([2.0 ** 16, 2.0 ** 11], K)
    v[m][:, at] = (1 + rng.random((128, 2 * K, 4))) * s[:, None] * size[:, None]
    return draw(rng, v, q)
def setup_inputs_spread(rng):
    q = (queries(rng).astype(np.float32) * np.float32(2.0 ** 20)).astype(BF)
    return draw(rng, wide(rng, N, 128, 4 * P, cols=6), q)
def setup_inputs_ties(rng):
    v, q = np.zeros((N, 128, P, 4), np.float32), queries(rng)
    s = np.where(q[0, :, 4:8].astype(np.float32) < 0, -1.0, 1.0)
    q[:, :32, :4] = 0
    on = (np.arange(128) < 32)[:, None]
    for p in range(N):
        at = p + N * rng.permutation(P // N)
        for g in range(P // N // 3):
            x = 2.0 ** -2 * rng.standard_normal((N, 128, 1, 4))
            a, b, m = (p + 1 + rng.permutation(N - 1)[:3]) % N
            x[p] *= 2.0 ** 22
            x[m] = x[p]
            x[a, :, 0] = np.where(on, 2.0 ** 23 * (1 + rng.random((128, 4))) * s, x[a, :, 0])
            x[b] = x[a] * rng.choice([-1.0, 1.0])
            v[:, :, at[3 * g:3 * g + 3]] = x * rng.choice([-1.0, 1.0], (3, 1))
    return draw(rng, v, q)
def setup_inputs_zero(rng):
    v = striped(data(rng))
    lo, hi = int(rng.integers(0, K // 4 + 1)), int(rng.integers(K // 2, P - K // 4 + 1))
    v[:, :, :hi] = 0
    v[:, :, hi + K // 4:] = 0
    for j in range(lo, lo + K // 4):
        m, n = (j + 1 + rng.permutation(N - 1)[:2]) % N
        v[m][:, j] = 4 * rng.standard_normal((128, 4))
        v[n][:, j] = -v[m][:, j]
    harm(rng, v, np.arange(hi, hi + K // 4), 8)
    return draw(rng, v)
def check_inputs(d):
    b = []
    for k, lo, hi in (("tb", -16, 24), ("u", -30, 30), ("w", -30, 30)):
        v = np.abs(d[k].astype(np.float32))
        if not (np.isfinite(v).all() and ((v == 0) | (v >= 2.0 ** lo) & (v <= 2.0 ** hi)).all()): b.append("a value of " + k)
    q = d["u"].astype(np.float32)
    if (q[:, :, 8:] != 0).any(): b.append("u has numbers behind its first 2 columns")
    if (q != q[:1]).any(): b.append("u isn't the same on all ranks")
    return b
def reference(tb, u, w):
    tab = [mx_ref.quantize(np.ascontiguousarray(tb[r])) for r in range(N)]
    bs = np.zeros((N, 4, K), np.float32)
    for t in range(2):
        c, g = checks(tab, u)
        bad, lost = judge(c, g, t)
        new = rebuilt(tab, bad, lost, t)
        at = places(t, bad)
        for r in range(N):
            e = np.flatnonzero(lost == r)
            tab[r] = put(tab[r], at[r, e], pick(new, e))
        bs[:, 2 * t] = bad
        bs[:, 2 * t + 1] = lost
    oc, osc, y = np.zeros((N, 128, 4 * P), np.uint8), np.zeros((N, 16, P), np.uint8), np.zeros((N, 128, O * P), np.float32)
    for r in range(N):
        oc[r], osc[r] = emit(tab[r])
        for o in range(O):
            y[r, :, o * P:o * P + P] = mx_ref.matmul(mx_ref.quantize(np.ascontiguousarray(cut(w[r], o))), tab[r])
    return {"oc": oc, "osc": osc, "bs": bs, "y": y}

@@ -1,0 +1,756 @@
+from concourse.bass import DstId, RemoteDMATransfer
+from concourse.mybir import dt, AluOpType as Op, AxisListType, ActivationFunctionType as Act
+
+N, P, K = 4, 256, 64
+R1, R2 = 352, 608
+BUILD = ((0, 2), (1, 3))
+TINY = 2.0 ** -110
+UNIT = 32768.0
+TUNE = dict(wake=150.0, fac=1.2, load=900.0, issue=60.0, rissue=250.0, hop=700.0, row=12.0, byte=0.06, tol=20.0, bias=60.0)
+
+F, B, I, U16, CODES = "float32", "bfloat16", "int32", "uint16", "float8_e4m3fn_x4"
+SCRATCH, LOG, _TOP = {}, {}, {}
+
+
+def _own(dtype, **kw):
+    for n, c in kw.items():
+        SCRATCH[n] = ("sbuf", [128, c], dtype)
+        LOG[n] = (n, 0, c, dtype)
+
+
+def _cube(**kw):
+    for n, (a, b) in kw.items():
+        SCRATCH[n] = ("sbuf", [128, a, b], F)
+        LOG[n] = (n, 0, a * b, F)
+
+
+def _slab(slab, dtype, **kw):
+    for n, c in kw.items():
+        at = _TOP.get(slab, 0)
+        LOG[n] = (slab, at, c, dtype)
+        _TOP[slab] = at + (c + 15) // 16 * 16
+        SCRATCH[slab] = ("sbuf", [128, _TOP[slab]], dtype)
+
+
+_own(B, onb=512, tbt=1040, ut=512, wt=1024, eb=2048, ub0=512, ub1=512, h0=512, h1=512)
+for _n, _c in dict(tq=256, tw=512, tx=768, uq=128, uc=128, ug=128, eq=512, wq=256, tz=256, sla=64, slb=64,
+                   laa=128, lab=128, psa=128, psb=128, ou=256).items():
+    _own(CODES, **{_n: _c})
+    _own("uint8", **{_n + "_s": _c})
+for _n in ("pa", "pu"):
+    SCRATCH[_n] = ("psum", [128, 2048], F)
+    LOG[_n] = (_n, 0, 2048, F)
+_own(F, l0=16, l1=16, xs=256, xd=128, ys=512, fr=640, ft=512)
+_cube(row0=(2, 128), row1=(2, 128), kt=(4, 32), mm0=(4, 64), mm1=(4, 64))
+_slab("fs", F, jc=2, jp0=2, jp1=2, jp2=2, jpb=2, cf=12, rr=16, rh=8, rk8=8, wm=16, nq=8, ca=8, cb=8, c1=8, c2=8, c3=8, c4=8,
+      s1=8, s2=8, s3=8, s4=8, s5=8, wl=8, wa=3, wb=1, wc=1, wd=3, wl1=6, ma=12, mb=12, m0=16, rho=4, csf=8, cso=2, gm=40, mrow=32,
+      kf=2, kg=2, tr=8, ofrf=4, va=128, vb=128, d0a=8, d0b=8, oh=512, prc=520, prg=390, rep=8, nrep=8, kra=12, krb=12, kro=16, kr0=16,
+      pm=130, src1=2, oho=128, sqc=8, gq=6, lr=128, bsf=256, junk=4096)
+for _t in "01":
+    _slab("fs", F, **{n + _t: c for n, c in dict(sq=16, sc=16, ex=64, sa=2, nd=2, dl=2, th=80, cm=544, po=2, mt=256, lw=4, ab=4, ac=4,
+                                                 ga=8, gx=2, gy=8, ge=8, gw=8, gn=2, pay=2, er=64).items()})
+    _slab("is_", I, **{n + _t: c for n, c in dict(wj=4, rk=6, fi=4, fj=4, fk=4, fa=8, fl=4, fm=4, fe=4, fo=8).items()})
+    _slab("us", U16, **{n + _t: c for n, c in dict(off=4, rfo=6, ofs=8, exo=4).items()})
+_slab("is_", I, bi=128, key=64, bj=256, ji=2, jj=2, pi=4, ci=12, csi=8, csj=8, tri32=8)
+_slab("us", U16, ofr=4, ofu=32, ofv=32, fou=16)
+
+SEMAPHORES = ["sv", "ss", "st", "sg", "dl_u", "dl_t0", "dl_t1", "dl_t2", "dl_w", "dl_x", "dl_x_s", "dl_m", "dl_m_s", "dl_n", "dl_n_s",
+              "dbs", "dy0", "dy1", "doc", "ls", "a0", "a1", "ha0", "ha1", "hb0", "hb1"]
+_QS = {"v": "sv", "s": "ss", "t": "st", "g": "sg"}
+_PLANS = {}
+
+
+def W(name, c0=0, c1=None, step=1, p0=0, p1=128):
+    return (name, c0, LOG[name][2] if c1 is None else c1, step, p0, p1)
+
+
+def C(name, a0, a1, b0, b1, p0=0, p1=128):
+    return (name, 0, LOG[name][2], 1, p0, p1, (a0, a1, b0, b1))
+
+
+def width(w):
+    if len(w) > 6:
+        a0, a1, b0, b1 = w[6]
+        return (a1 - a0) * (b1 - b0)
+    return len(range(w[1], w[2], w[3]))
+
+
+def meet(a, b):
+    if a[4] >= b[5] or b[4] >= a[5]:
+        return False
+    if a[0] in ("pa", "pu"):
+        return a[1] // 512 <= (b[2] - 1) // 512 and b[1] // 512 <= (a[2] - 1) // 512
+    if len(a) > 6 and len(b) > 6:
+        x, y = a[6], b[6]
+        return x[0] < y[1] and y[0] < x[1] and x[2] < y[3] and y[2] < x[3]
+    if a[1] >= b[2] or b[1] >= a[2]:
+        return False
+    return not (a[3] == b[3] and a[3] > 1 and (a[1] - b[1]) % a[3])
+
+
+def calls(r, cores, topo):
+    core = cores[r]
+    nodes = []
+    cyc = 0.83 * TUNE["fac"]
+
+    def node(rd, wr, fns, cost, sem=None, by=1, lag=0.0, after=(), to=(), cast=False):
+        nodes.append(dict(rd=rd, wr=wr, fns=fns, cost=cost, sem=sem, by=by, lag=lag, after=list(after), to=to, cast=cast, i=len(nodes)))
+        return nodes[-1]
+
+    def small(n):
+        return max(64, n) * cyc
+
+    def tt(out, a, b, op):
+        both = a[0] not in ("pa", "pu") and b[0] not in ("pa", "pu")
+        return node([a, b], [out], {"v": lambda e: e["v"].tensor_tensor(e["ap"](out), e["ap"](a), e["ap"](b), op)},
+                    {"v": small(width(out) * (2 if both else 1))})
+
+    def ts(out, a, s1, op0, s2=None, op1=None):
+        rd = [a] + [s for s in (s1, s2) if isinstance(s, tuple)]
+
+        def f(e):
+            x1, x2 = [e["ap"](s) if isinstance(s, tuple) else s for s in (s1, s2)]
+            if op1 is not None:
+                return e["v"].tensor_scalar(e["ap"](out), e["ap"](a), x1, x2, op0, op1)
+            return e["v"].tensor_scalar(e["ap"](out), e["ap"](a), x1, None, op0)
+        return node(rd, [out], {"v": f}, {"v": small(width(out))})
+
+    def cp(out, a, q="v"):
+        fns = {"v": lambda e: e["v"].tensor_copy(e["ap"](out), e["ap"](a)), "s": lambda e: e["s"].activation(e["ap"](out), e["ap"](a), Act.Copy)}
+        return node([a], [out], {x: fns[x] for x in q}, {x: small(width(out)) for x in q})
+
+    def red(out, a, op):
+        return node([a], [out], {"v": lambda e: e["v"].tensor_reduce(e["ap"](out), e["ap"](a), AxisListType.X, op)}, {"v": small(width(a))})
+
+    def fill(out, c):
+        return node([], [out], {"v": lambda e: e["v"].memset(e["ap"](out), c)}, {"v": small(width(out) * (0.5 if LOG[out[0]][3] in (B, U16) else 1))})
+
+    def turn(out, a):
+        return node([a], [out], {"v": lambda e: e["v"].transpose(e["ap"](out), e["ap"](a))}, {"v": small(width(a))})
+
+    def scan(out, d0, d1):
+        return node([d0, d1], [out], {"v": lambda e: e["v"].tensor_tensor_scan(e["ap"](out), e["ap"](d0), e["ap"](d1), 0.0, Op.mult, Op.subtract)},
+                    {"v": small(width(out))})
+
+    def act(out, a, f, off=None):
+        rd = [a] + [w for w in (off,) if w is not None]
+        n = width(out)
+        return node(rd, [out], {"s": lambda e: e["s"].activation(e["ap"](out), e["ap"](a) if off is None else e["ap"](a).indirect(e["ap"](off)), f)},
+                    {"s": small(n) if off is None else (65 + 1.56 * 0.83 * n) * TUNE["fac"]})
+
+    junk = [0]
+
+    def total(out, a, q="vs"):
+        n = width(a)
+        j = W("junk", junk[0], junk[0] + n)
+        junk[0] += n
+        fns = {"v": lambda e: e["v"].tensor_reduce(e["ap"](out), e["ap"](a), AxisListType.X, Op.add),
+               "s": lambda e: e["s"].activation(e["ap"](j), e["ap"](a), Act.Copy, accum_out=e["ap"](out))}
+        return node([a], [out, j], {x: fns[x] for x in q}, {x: small(n) + (20 if x == "s" else 0) for x in q})
+
+    def iota(out, pattern, base=0, cm=0):
+        kw = {} if LOG[out[0]][3] == I else {"allow_small_or_imprecise_dtypes": True}
+        return node([], [out], {"g": lambda e: e["g"].iota(e["ap"](out), pattern, base, cm, **kw)}, {"g": 130 * TUNE["fac"] + 2 * cyc * width(out)})
+
+    def quant(name, c0, src, s0, n):
+        q, s, x = W(name, c0, c0 + n), W(name + "_s", c0, c0 + n), W(src, s0, s0 + 4 * n)
+        return node([x], [q, s], {"v": lambda e: e["v"].quantize_mx(e["ap"](q), e["ap"](s), e["ap"](x))}, {"v": (12 + 0.88 * n) * TUNE["fac"]})
+
+    def mm(bank, lhs, l0, rhs, r0, n=128):
+        rd = [W(lhs, l0, l0 + 128), W(lhs + "_s", l0, l0 + 128), W(rhs, r0, r0 + n), W(rhs + "_s", r0, r0 + n)]
+        o = W("pu" if bank > 3 else "pa", 512 * (bank % 4), 512 * (bank % 4) + n)
+        return node(rd, [o], {"t": lambda e: e["t"].matmul_mx(e["ap"](o), e["ap"](rd[0]), e["ap"](rd[1]), e["ap"](rd[2]), e["ap"](rd[3]), True, True)},
+                    {"t": 1.3 * (n + 16) * cyc})
+
+    def pick(dst, d0, src, width_, off, o0, n):
+        o, a, f = W(dst, d0, d0 + n), W(src, 0, width_), W(off, o0, o0 + n // 16)
+        node([a, f], [o], {"v": lambda e: e["v"].tensor_copy(e["ap"](o).bitcast(dt.uint32), e["ap"](a).bitcast(dt.uint32).indirect(e["ap"](f)))},
+             {"v": (50 + 1.56 * 0.83 * n) * TUNE["fac"]})
+        act(W(dst + "_s", d0, d0 + n), W(src + "_s", 0, width_), Act.Copy, off=f)
+
+    def raw(e, w):
+        return e["ap"](w).bitcast(dt.uint8) if LOG[w[0]][3] == CODES else e["ap"](w)
+
+    def load(q, w, tensor, c0, c1, sem, first=()):
+        return node(list(first), [w], {q: lambda e: e[q].dma_start(e["ap"](w), e["T"][tensor][:, c0:c1])}, {q: TUNE["issue"]}, sem, 16, TUNE["load"])
+
+    def move(q, out, a, sem):
+        return node([a], [out], {q: lambda e: e[q].dma_start(raw(e, out), raw(e, a))}, {q: TUNE["issue"]}, sem, 16, TUNE["load"])
+
+    def store(q, dst, a, sem):
+        return node([a], [], {q: lambda e: e[q].dma_start(dst(e["T"]), raw(e, a))}, {q: TUNE["issue"]}, sem, 16, TUNE["load"])
+
+    peers = [c for c in cores if c != core]
+
+    def mask(engs):
+        m = 0
+        for e in engs:
+            m |= 1 << e
+        return m
+
+    def send(parts, sem, after=()):
+        def did(c):
+            a = topo.addr(c)
+            return DstId(rid=a[0], pnc=a[1])
+
+        def f(e):
+            return e["g"].remote_dma_fused([RemoteDMATransfer(dst_ids=[did(c) for c in cs], dma_engine_mask=mask(es), remote_sem=e["T"].sem[sem],
+                                                              srcs=[raw(e, a)], dsts=[raw(e, b)] * len(cs)) for a, b, cs, es in parts],
+                                           local_sem=e["T"].sem["ls"])
+        lag = 0.0
+        for a, b, cs, es in parts:
+            row = width(a) * {F: 4, CODES: 4}.get(LOG[a[0]][3], 1)
+            lag = max(lag, TUNE["hop"] + 128 // len(es) * len(cs) * (TUNE["row"] + row * TUNE["byte"]))
+        return node([p[0] for p in parts], [], {"g": f}, {"g": TUNE["rissue"]}, "ls", sum(len(p[3]) for p in parts), lag, after,
+                    [(cores.index(c), sem) for p in parts for c in p[2]], True)
+
+    def lands(sem, count, views):
+        return node([], views, {"r": None}, {"r": 0.0}, sem, count)
+
+    alle = topo.engines(core, peers[0])
+
+    load("y", W("ut", 0, 8), "u", 0, 8, "dl_u")
+    load("y", W("tbt", 0, 512), "tb", 0, 512, "dl_t0")
+    load("s", W("tbt", 512, 1024), "tb", 512, 1024, "dl_t1")
+
+    iota(W("pi", 0, 1), [[0, 1]], 0, 1)
+    iota(W("pi", 1, 2), [[0, 1]], 1, 1)
+    iota(W("pi", 2, 4), [[128, 2]], r, 1)
+    iota(W("jc"), [[128, 2]], 0, 1)
+    iota(W("rr"), [[1, 4], [0, 4]])
+    iota(W("rh"), [[1, 4], [0, 2]])
+    iota(W("rk8"), [[0, 2], [1, 4]])
+    iota(W("mrow"), [[1, 32]])
+    fill(W("ut", 8, 512), 0.0)
+    fill(W("onb"), 1.0)
+
+    def unit(b):
+        o = W("eb", 512 * b, 512 * b + 512)
+        node([W("onb")], [o], {"g": lambda e: e["g"].affine_select(e["ap"](o), e["ap"](W("onb")), [[-8, 128], [-1, 4]], Op.is_equal, 0.0, b, 8)},
+             {"g": 170 * TUNE["fac"] + 1024 * cyc})
+    for b in range(4):
+        unit(b)
+    for y in range(4):
+        iota(C("kt", y, y + 1, 0, 32), [[0, 2], [1, 16]], 16 * y)
+    iota(W("kf"), [[16, 2]])
+    iota(W("tr"), [[16, 8]], 512)
+    iota(W("ofrf"), [[2, 2], [0, 2]])
+
+    pp = W("pi", 0, 1)
+    ts(W("ci", 0, 2), W("pi", 0, 2), 3, Op.bitwise_and)
+    ts(W("ci", 2, 3), pp, 15, Op.bitwise_and)
+    ts(W("ci", 3, 4), pp, 4, Op.arith_shift_right, 1, Op.bitwise_and)
+    ts(W("ci", 4, 6), W("pi", 2, 4), 255, Op.bitwise_and)
+    ts(W("ci", 6, 7), pp, 31, Op.bitwise_and)
+    ts(W("ci", 7, 8), pp, 5, Op.arith_shift_right, 1, Op.bitwise_and)
+    ts(W("ci", 8, 9), pp, 6, Op.arith_shift_right)
+    fill(W("exo0", 0, 2), 14)
+    fill(W("exo0", 2, 4), 15)
+    fill(W("d0a"), 1.0)
+    fill(W("d0a", 0, 1), 0.0)
+    fill(W("d0a", 4, 5), -1.0)
+    cp(W("cf", 0, 9), W("ci", 0, 9))
+    q0, q1, xf, gf, i1 = W("cf", 0, 1), W("cf", 1, 2), W("cf", 2, 3), W("cf", 3, 4), W("cf", 4, 6)
+    ts(W("wm", 0, 8), W("rh"), q0, Op.is_equal)
+    ts(W("wm", 8, 16), W("rh"), q0, Op.not_equal)
+    fill(W("gm", 2, 3), 1.0)
+    ts(W("gm", 0, 2), W("cf", 7, 9), -1.0, Op.mult, 1.0, Op.add)
+    ts(W("gm", 3, 35), W("mrow"), W("cf", 6, 7), Op.is_ge)
+
+    quant("uq", 0, "ut", 0, 128)
+    quant("tq", 0, "tbt", 0, 128)
+    mm(0, "tq", 0, "uq", 0)
+    quant("tq", 128, "tbt", 512, 128)
+    mm(1, "tq", 128, "uq", 0)
+
+    def mine(l, bank):
+        for h in range(2):
+            o = 512 * (bank + h)
+            cp(W(l, 4 * r + 2 * h, 4 * r + 2 * h + 1), W("pa", o, o + 1), "s")
+            act(W(l, 4 * r + 2 * h + 1, 4 * r + 2 * h + 2), W("pa", o + 1, o + 2), Act.Abs)
+        v = W(l, 4 * r, 4 * r + 4)
+        send([(v, v, peers, alle)], "a" + l[1])
+
+    mine("l0", 0)
+    lands("a0", 3 * len(alle), [W("l0", 4 * o, 4 * o + 4) for o in range(N) if o != r])
+
+    if r:
+        load("y", W("tbt", 1024, 1040), "tb", 0, 16, "dl_t2")
+        quant("tz", 0, "tbt", 4 * r, 256)
+        mm(2, "tz", 0, "uq", 0)
+        mm(3, "tz", 128, "uq", 0)
+        mine("l1", 2)
+    lands("a1", len(alle) * (3 if r == 0 else 2), [W("l1", 4 * o, 4 * o + 4) for o in range(1, N) if o != r])
+
+    u1, u2, u3 = 4096 / UNIT, 1024 / UNIT, 256 / UNIT
+    ts(W("nq"), W("rk8"), q0, Op.not_equal)
+    ts(W("ca"), W("rk8"), q0, Op.min)
+    ts(W("cb"), W("rk8"), q0, Op.max)
+    ts(W("s4"), W("rk8"), u1, Op.mult, 3 * u3 - 0.5, Op.add)
+    ts(W("c1"), W("ca"), 0.0, Op.is_equal, u2, Op.mult)
+    ts(W("c2"), W("cb"), 1.0, Op.is_equal, 1.0, Op.add)
+    ts(W("c3"), W("cb"), 3.0, Op.is_equal, -u3, Op.mult)
+    ts(W("c4"), W("ca"), 2.0, Op.is_equal, 1.0, Op.add)
+    tt(W("s1"), W("c1"), W("c2"), Op.mult)
+    tt(W("s2"), W("c3"), W("c4"), Op.mult)
+    tt(W("s3"), W("s1"), W("s4"), Op.add)
+    tt(W("s5"), W("s3"), W("s2"), Op.add)
+    tt(W("wl"), W("s5"), W("nq"), Op.mult)
+    ts(W("jp1"), W("jc"), 1.0 / UNIT, Op.mult, 0.5, Op.add)
+    tt(W("jp0"), W("jc"), W("jp1"), Op.add)
+
+    ts(W("ofu"), W("mrow"), 0.0, Op.is_ge, q0, Op.mult)
+    ts(W("ofv"), W("ofu"), 4.0, Op.add)
+    ready = [quant("tw", 320, "tbt", 0, 128)]
+    act(W("ub0"), W("ut"), Act.Copy, off=W("ofu"))
+    act(W("ub1"), W("ut"), Act.Copy, off=W("ofv"))
+    iota(W("va"), [[0, 2], [1, 64]], R1)
+    iota(W("vb"), [[0, 2], [1, 64]], R2)
+    iota(W("fr", 0, 512), [[16, 16], [0, 2], [1, 16]])
+    fill(W("fr", 512, 640), 0.0)
+    ts(W("kg"), W("kf"), xf, Op.add)
+    ts(W("ofr"), W("ofrf"), gf, Op.add)
+    ts(W("tri32"), W("tr"), xf, Op.add)
+    when = 0 if r in BUILD[0] else 1
+    quant("eq", 0, "eb", 0, 512)
+    quant(("psa", "psb")[when], 0, "tbt", 0, 128)
+    cp(W(("h0", "h1")[when]), W("tbt", 0, 512), "vs")
+    for x in ("", "_s"):
+        move("y", W("tw" + x, 0, 256), W("tq" + x), "dl_m" + x)
+    quant("uc", 0, "ub0", 0, 128)
+    quant("ug", 0, "ub1", 0, 128)
+    load("y", W("wt"), "w", 0, 1024, "dl_w", [W("l0")])
+    for x in ("", "_s"):
+        move("y", W("tx" + x, 0, 256), W("tq" + x), "dl_n" + x)
+    quant("wq", 0, "wt", 0, 256)
+
+    ts(W("ma"), W("rr", 0, 12), q1, Op.is_lt)
+    ts(W("mb"), W("rr", 0, 12), q1, Op.is_ge)
+    ts(W("m0"), W("rr"), q1, Op.is_equal)
+    cp(W("rho", 0, 1), q1)
+    tt(W("rho", 1, 4), W("rr", 0, 12, 4), W("mb", 0, 12, 4), Op.add)
+    r1, r2, r3 = W("rho", 1, 2), W("rho", 2, 3), W("rho", 3, 4)
+    ts(W("wa"), W("rho", 1, 4), u1, Op.mult, -0.5, Op.add)
+    ts(W("wb"), r1, u2, Op.mult)
+    ts(W("wc"), r3, u3, Op.mult)
+    ts(W("wd", 0, 1), r2, u2, Op.mult, W("wa", 0, 1), Op.add)
+    ts(W("wd", 1, 3), W("wa", 1, 3), W("wb"), Op.add)
+    for h in range(2):
+        ts(W("wl1", 3 * h, 3 * h + 2), W("wd", 0, 2), W("wc"), Op.add)
+        ts(W("wl1", 3 * h + 2, 3 * h + 3), r2, u3, Op.mult, W("wd", 2, 3), Op.add)
+    fill(W("d0b"), 1.0)
+    fill(W("d0b", 0, 8, 4), 0.0)
+    fill(W("d0b", 1, 8, 4), -1.0)
+    fill(W("exo1", 0, 2), 3)
+    fill(W("exo1", 2, 4), 7)
+    for h in range(2):
+        ts(W("csi", 4 * h, 4 * h + 4), W("rho"), 4097.0, Op.mult, W("jc", h, h + 1), Op.add)
+    ts(W("csj"), W("csi"), 3 * 4096 + 255, Op.bitwise_and)
+    cp(W("csf"), W("csj"))
+    ts(W("cso"), i1, 4096.0 * r, Op.add)
+    ts(W("ji"), W("jc"), 1.0, Op.add)
+    ts(W("jj"), W("ji"), 255, Op.bitwise_and)
+    ts(W("jp2"), W("jj"), 1.0 / UNIT, Op.mult, 0.5, Op.add)
+    cp(W("pm", 64, 130, 65), W("cf", 4, 6), "vs")
+
+    cp(W("l1", 0, 4), W("l0", 0, 4), "vs")
+    tt(W("krb"), W("l1", 4, 16), W("mb"), Op.mult)
+    tt(W("kra"), W("l1", 0, 12), W("ma"), Op.mult)
+    tt(W("kr0"), W("l1"), W("m0"), Op.mult)
+    tt(W("kro", 4, 16), W("kra"), W("krb"), Op.add)
+    for h in range(2):
+        red(W("kro", 2 * h, 2 * h + 1), W("kr0", 2 * h, 16, 4), Op.add)
+
+    def count(t):
+        n = str(t)
+        src, off = (W("sc0"), W("exo0")) if t == 0 else (W("sc1", 0, 8), W("exo1"))
+        s2 = W("sc0", 14, 16) if t == 0 else W("sc1", 3, 8, 4)
+        rn, th, cm = "row" + n, "th" + n, "cm" + n
+        act(W("ex" + n), src, Act.Abs, off=off)
+        act(W("sa" + n), s2, Act.Abs)
+        for h in range(2):
+            turn(C(rn, h, h + 1, 0, 32), W("ex" + n, 32 * h, 32 * h + 32))
+        for h in range(2):
+            s = W("sa" + n, h, h + 1)
+            ts(W("nd" + n, h, h + 1), s, 1.5 * 2.0 ** -24, Op.mult, s, Op.add)
+            ts(W("dl" + n, h, h + 1), W("nd" + n, h, h + 1), TINY, Op.max, W("sa" + n, h, h + 1), Op.subtract)
+        for a in range(2):
+            cp(C(rn, 0, 2, 64, 96, 64 * a, 64 * a + 64), C(rn, 0, 2, 0, 32, 64 - 64 * a, 128 - 64 * a), "vs")
+        for x in (1, 3):
+            for a in range(4):
+                b = a ^ x
+                cp(C(rn, 0, 2, 32 * x, 32 * x + 32, 32 * a, 32 * a + 32), C(rn, 0, 2, 0, 32, 32 * b, 32 * b + 32), "vs")
+        for h in range(2):
+            ts(W(th, 40 * h, 40 * h + 35), W("gm", 0, 35), W("dl" + n, h, h + 1), Op.mult, W("sa" + n, h, h + 1), Op.add)
+        for h in range(2):
+            tt(W(cm, 272 * h + 232, 272 * h + 264), C(rn, h, h + 1, 0, 32), W(th, 40 * h + 3, 40 * h + 35), Op.is_ge)
+            ts(W(cm, 272 * h + 200, 272 * h + 232), C(rn, h, h + 1, 32, 64), W(th, 40 * h, 40 * h + 1), Op.is_ge)
+            other = W(th, 2, 3) if h == 0 else W("sa" + n, 1, 2)
+            ts(W(cm, 272 * h, 272 * h + 128), C(rn, 1 - h, 2 - h, 0, 128), other, Op.is_ge)
+            ts(W(cm, 272 * h + 128, 272 * h + 192), C(rn, h, h + 1, 64, 128), W(th, 40 * h + 1, 40 * h + 2), Op.is_ge)
+            total(W(cm, 272 * h + 192, 272 * h + 193), W(cm, 272 * h + 200, 272 * h + 264))
+            total(W("po" + n, h, h + 1), W(cm, 272 * h, 272 * h + 193))
+
+    def listed(t):
+        m, mt, lw, b, c = [x + str(t) for x in ("mm", "mt", "lw", "ab", "ac")]
+        for h in range(2):
+            ts(C(m, 0, 4, 32 * h, 32 * h + 32), C("kt", 0, 4, 0, 32), W("po%d" % t, h, h + 1), Op.is_equal, W("pay%d" % t, h, h + 1), Op.mult)
+        for y in range(4):
+            turn(W(mt, 64 * y, 64 * y + 64), C(m, y, y + 1, 0, 64))
+        for y in range(4):
+            total(W(lw, y, y + 1), W(mt, 64 * y, 64 * y + 64))
+        for k in range(4):
+            tt(W(b, 0, 4, 1, 32 * k, 32 * k + 32), W(lw, 0, 4, 1, 32 * k, 32 * k + 32), W(lw, 0, 4, 1, 32 * (k ^ 1), 32 * (k ^ 1) + 32), Op.add)
+        for k in range(2):
+            tt(W(c, 0, 4, 1, 64 * k, 64 * k + 64), W(b, 0, 4, 1, 64 * k, 64 * k + 64), W(b, 0, 4, 1, 64 - 64 * k, 128 - 64 * k), Op.add)
+        return W(c, 0, 4)
+
+    def lost(t, n, wl, base):
+        k = n // 2
+        s = str(t)
+
+        def size(h):
+            return W("gy0", h, 8, 2) if t == 0 else W("ga1", k * h, k * h + k)
+        for h in range(2):
+            red(W("gx" + s, h, h + 1), size(h), Op.max)
+        for h in range(2):
+            ts(W("ge" + s, k * h, k * h + k), size(h), W("gx" + s, h, h + 1), Op.is_equal)
+        tt(W("gw" + s, 0, n), W("ge" + s, 0, n), W(wl), Op.mult)
+        for h in range(2):
+            red(W("gn" + s, h, h + 1), W("gw" + s, k * h, k * h + k), Op.min)
+        tt(W("pay" + s), W("gn" + s), W(base), Op.add)
+
+    def gather(t, lists):
+        n = "ab"[t]
+        src, width_ = (("tq", 256), ("tw", 448))[t]
+        off = "off%d" % t
+        cp(W(off), lists)
+        sl, la = "sl" + n, "la" + n
+        bs = BUILD[t]
+        if r in bs:
+            d = bs.index(r)
+            o = 1 - d
+            pick(sl, 32 * o, src, width_, off, 2 * o, 32)
+            to = cores[bs[o]]
+            for s in ("", "_s"):
+                send([(W(sl + s, 32 * o, 32 * o + 32), W(la + s, 32 * r, 32 * r + 32), [to], topo.engines(core, to))], "ha%d" % t, ready)
+            pick(la, 32 * r, src, width_, off, 2 * d, 32)
+            cnt = 0
+            for i in range(N):
+                if i != r:
+                    cnt += 2 * len(topo.engines(cores[i], core)) // (1 if i in bs else 2)
+            lands("ha%d" % t, cnt, [W(la + s, 32 * i, 32 * i + 32) for s in ("", "_s") for i in range(N) if i != r])
+        else:
+            pick(sl, 0, src, width_, off, 0, 64)
+            for s in ("", "_s"):
+                send([(W(sl + s, 32 * d, 32 * d + 32), W(la + s, 32 * r, 32 * r + 32), [cores[bs[d]]], topo.engines(core, cores[bs[d]])[d::2])
+                      for d in range(2)], "ha%d" % t, ready)
+
+    def numbers(t, w):
+        ts(W("wj%d" % t), w, UNIT, Op.mult)
+
+    def buildlist(t):
+        s, d = str(t), BUILD[t].index(r)
+        v = W("wj" + s, 2 * d, 2 * d + 2)
+        ts(W("rk" + s, 0, 2), v, 3, Op.bitwise_and)
+        ts(W("rk" + s, 2, 4), v, 10, Op.arith_shift_right, 3, Op.bitwise_and)
+        ts(W("rk" + s, 4, 6), v, 8, Op.arith_shift_right, 3, Op.bitwise_and)
+        for y in range(2):
+            ts(W("rfo" + s, y, 6, 2), W("rk" + s, y, 6, 2), 32.0, Op.mult, W("kg", y, y + 1), Op.add)
+
+    def build(t):
+        s, n, d = str(t), "ab"[t], BUILD[t].index(r)
+        la, ps, hh = "la" + n, "ps" + n, "h" + s
+        pick(ps, 0, la, 128, "rfo" + s, 0, 96)
+        for b in range(4):
+            mm(4 + b, "eq", 128 * b, ps, 0)
+        at = 96 if d == 0 else 0
+        for b in range(4):
+            cp(W("xs", 64 * b, 64 * b + 64), W("pu", 512 * b + 32, 512 * b + 96), "s")
+            tt(W("xd", 32 * b, 32 * b + 32), W("pu", 512 * b, 512 * b + 32), W("xs", 64 * b, 64 * b + 32), Op.subtract)
+            tt(W(hh, 4 * at + b, 4 * at + 128, 4), W("xd", 32 * b, 32 * b + 32), W("xs", 64 * b + 32, 64 * b + 64), Op.subtract)
+        dst, base = ("tw", 256) if t == 0 else ("tx", 512)
+        quant(dst, base + 128 * d, hh, 0, 128)
+        c = base + 96 + 32 * d
+        for x in ("", "_s"):
+            v = W(dst + x, c, c + 32)
+            send([(v, v, peers, alle)], "hb%d" % t)
+
+    def built(t):
+        dst, base = ("tw", 256) if t == 0 else ("tx", 512)
+        lands("hb%d" % t, sum(2 * len(topo.engines(cores[b], core)) for b in BUILD[t] if b != r),
+              [W(dst + x, base + 96 + 32 * d, base + 128 + 32 * d) for x in ("", "_s") for d in range(2) if BUILD[t][d] != r])
+
+    def mapped(t):
+        s = str(t)
+        i, a = W("fi" + s), W("wj" + s)
+        ts(W("fl" + s), a, 12, Op.arith_shift_right, 3, Op.bitwise_and)
+        if t and r != 1:
+            ts(W("fj" + s), a, float(r - 1), Op.add)
+            a = W("fj" + s)
+        ts(i, a, 255, Op.bitwise_and)
+        ts(W("fk" + s), a, 240, Op.bitwise_and)
+        ts(W("fm" + s), W("fl" + s), float(r), Op.not_equal, 4096.0, Op.mult)
+        tt(W("fe" + s), i, W("fk" + s), Op.add)
+        tt(W("fa" + s, 0, 4), W("fe" + s), W("fm" + s), Op.add)
+        ts(W("fa" + s, 4, 8), W("fa" + s, 0, 4), 16.0, Op.add)
+        tt(W("fo" + s), W("fa" + s), W("tri32"), Op.min)
+        cp(W("ofs" + s), W("fo" + s))
+
+    def enter(t):
+        win, off, src = W("fr"), W("ofs%d" % t), W("va" if t == 0 else "vb")
+        node([off, src], [win], {"v": lambda e: e["v"].tensor_copy(e["ap"](win).indirect(e["ap"](off)), e["ap"](src))},
+             {"v": (50 + 3 * 0.83 * 128) * TUNE["fac"]})
+
+    def listrow(t, w):
+        s = str(t)
+        act(W("er" + s), w, Act.Copy, off=W("ofr"))
+        turn(W("lr", 64 * t, 64 * t + 64), W("er" + s))
+        ts(W("bi", 64 * t, 64 * t + 64), W("lr", 64 * t, 64 * t + 64), UNIT, Op.mult, -1.0 * t, Op.add)
+
+    def stripes(t):
+        o = 128 * t
+        b = W("bi", 64 * t, 64 * t + 64, 1, 0, 1)
+        ts(W("bj", o, o + 64, 1, 0, 1), b, 255, Op.bitwise_and)
+        ts(W("bj", o + 64, o + 128, 1, 0, 1), b, 12, Op.arith_shift_right, 3, Op.bitwise_and)
+        cp(W("bsf", o, o + 128, 1, 0, 1), W("bj", o, o + 128, 1, 0, 1))
+
+    for m in range(2):
+        tt(W("sq0", 8 * m, 8 * m + 8), W("l0", 0, 16, 2), W("wm", 8 * m, 8 * m + 8), Op.mult)
+    for h in range(2):
+        scan(W("sc0", h, 16, 2), W("d0a"), W("sq0", h, 16, 2))
+    tt(W("gy0"), W("l0", 1, 16, 2), W("wm", 8, 16), Op.mult)
+    lost(0, 8, "wl", "jp0")
+    count(0)
+    w0 = listed(0)
+    gather(0, w0)
+    numbers(0, w0)
+    if r in BUILD[0]:
+        buildlist(0)
+        build(0)
+    built(0)
+    listrow(0, w0)
+    ts(W("key"), W("bi", 0, 64), 3 * 4096 + 255, Op.bitwise_and)
+    mapped(0)
+    enter(0)
+    for e in range(8):
+        ts(W("oh", 64 * e, 64 * e + 64), W("key"), W("csf", e, e + 1), Op.is_equal)
+    for e in range(8):
+        total(W("rep", e, e + 1), W("oh", 64 * e, 64 * e + 64))
+    for h in range(2):
+        ts(W("oho", 64 * h, 64 * h + 64), W("key"), W("cso", h, h + 1), Op.is_equal)
+        tt(W("pm", 65 * h, 65 * h + 64), W("oho", 64 * h, 64 * h + 64), W("va", 0, 64), Op.mult)
+        red(W("src1", h, h + 1), W("pm", 65 * h, 65 * h + 65), Op.max)
+    ts(W("nrep"), W("rep"), -1.0, Op.mult, 1.0, Op.add)
+    tt(W("jpb"), W("src1"), W("jp2"), Op.add)
+    for h in range(2):
+        tt(W("prc", 260 * h + 64, 260 * h + 260, 65), W("kro", 2 * h, 16, 4), W("nrep", 4 * h, 4 * h + 4), Op.mult)
+        tt(W("prg", 195 * h + 64, 195 * h + 195, 65), W("kro", 4 + 2 * h + 1, 16, 4), W("nrep", 4 * h + 1, 4 * h + 4), Op.mult)
+
+    mm(0, "uc", 0, "tw", 320)
+    mm(1, "ug", 0, "tw", 320)
+    for e in range(8):
+        tt(W("prc", 65 * e, 65 * e + 64), W("pa", 32, 96), W("oh", 64 * e, 64 * e + 64), Op.mult)
+        total(W("sqc", e, e + 1), W("prc", 65 * e, 65 * e + 65))
+    scan(W("sc1", 0, 8), W("d0b"), W("sqc"))
+    for e in range(6):
+        o = 64 * (4 * (e // 3) + e % 3 + 1)
+        tt(W("prg", 65 * e, 65 * e + 64), W("pa", 544, 608), W("oh", o, o + 64), Op.mult)
+        total(W("gq", e, e + 1), W("prg", 65 * e, 65 * e + 65))
+    act(W("ga1", 0, 6), W("gq"), Act.Abs)
+    lost(1, 6, "wl1", "jpb")
+    count(1)
+    w1 = listed(1)
+    gather(1, w1)
+    numbers(1, w1)
+    if r in BUILD[1]:
+        buildlist(1)
+        build(1)
+    mapped(1)
+    built(1)
+    for x in ("", "_s"):
+        move("y", W("tx" + x, R1, R1 + 64), W("tw" + x, R1, R1 + 64), "dl_x" + x)
+    enter(1)
+    turn(W("ft"), W("fr", 0, 512))
+    cp(W("fou"), W("ft", 0, 512, 32))
+    listrow(1, w1)
+    for t in range(2):
+        stripes(t)
+    store("y", lambda T: T.bs[:, :], W("bsf", 0, 256, 1, 0, 1), "dbs")
+
+    for c in range(2):
+        pick("ou", 128 * c, "tx", 672, "fou", 8 * c, 128)
+        for o in range(2):
+            mm(2 * c + o, "wq", 128 * o, "ou", 128 * c)
+
+    def scales(k):
+        store("y", lambda T: T.osc[4 * k:4 * k + 4, 0:256], W("ou_s", 0, 256, 1, 32 * k, 32 * k + 4), "doc")
+
+    def block(c, o):
+        a, b = 256 * o + 128 * c, 256 * o + 128 * c + 128
+        cp(W("ys", a, b), W("pa", 512 * (2 * c + o), 512 * (2 * c + o) + 128), "vs"[o])
+        store("ys"[o], lambda T: T.y[:, a:b], W("ys", a, b), "dy%d" % o)
+
+    store("y", lambda T: T.oc[:, 0:1024], W("ou"), "doc")
+    for k in range(4):
+        scales(k)
+    for c in range(2):
+        for o in range(2):
+            block(c, o)
+    return nodes
+
+
+def arrange(plans):
+    wake = TUNE["wake"]
+    flat, base = [], []
+    for r, ns in enumerate(plans):
+        base.append(len(flat))
+        for n in ns:
+            flat.append((r, n))
+    pred = [set() for _ in flat]
+    for r, ns in enumerate(plans):
+        log = {}
+        for n in ns:
+            me = base[r] + n["i"]
+            qs = list(n["fns"])
+            for ws, isw in ((n["rd"], False), (n["wr"], True)):
+                for w in ws:
+                    for w2, isw2, j, qs2 in log.get(w[0], ()):
+                        if (isw or isw2 or (w[0] in ("pa", "pu") and (len(qs) > 1 or qs != qs2))) and meet(w, w2):
+                            pred[me].add(j)
+            for ws, isw in ((n["rd"], False), (n["wr"], True)):
+                for w in ws:
+                    log.setdefault(w[0], []).append((w, isw, me, qs))
+            for a in n["after"]:
+                pred[me].add(base[r] + a["i"])
+            pred[me].discard(me)
+    sends = {}
+    for k, (r, n) in enumerate(flat):
+        for to in n["to"]:
+            sends.setdefault(to, []).append(k)
+    for k, (r, n) in enumerate(flat):
+        if "r" in n["fns"]:
+            pred[k].update(sends.get((r, n["sem"]), ()))
+    succ = [[] for _ in flat]
+    for k, ps in enumerate(pred):
+        for j in ps:
+            succ[j].append(k)
+
+    def after(j, k):
+        return flat[j][1]["lag"] + (0.0 if "r" in flat[k][1]["fns"] else wake)
+    left = [len(s) for s in succ]
+    way = [0.0] * len(flat)
+    todo = [k for k in range(len(flat)) if not left[k]]
+    while todo:
+        k = todo.pop()
+        n = flat[k][1]
+        way[k] = min(n["cost"].values()) + max([n["lag"]] + [after(k, j) + way[j] for j in succ[k]])
+        for j in pred[k]:
+            left[j] -= 1
+            if not left[j]:
+                todo.append(j)
+
+    count = [len(p) for p in pred]
+    when, free, ready, best, out = [0.0] * len(flat), {}, {}, {}, []
+
+    def choose(q):
+        f = free.get(q, 0.0)
+        top, at = None, 0.0
+        for k in sorted(ready[q], key=lambda k: (-way[k], k)):
+            s = max(f, when[k])
+            if top is None or (s < at and s + flat[k][1]["cost"][q[1]] <= at + TUNE["tol"]):
+                top, at = k, s
+        best[q] = (at, top)
+        if top is None:
+            del best[q]
+
+    def put(k):
+        for q in flat[k][1]["fns"]:
+            ready.setdefault((flat[k][0], q), set()).add(k)
+            choose((flat[k][0], q))
+    for k in range(len(flat)):
+        if not count[k]:
+            put(k)
+
+    def ends(q):
+        n = flat[best[q][1]][1]
+        return best[q][0] + n["cost"][q[1]] + (TUNE["bias"] if q[1] == "v" and len(n["fns"]) > 1 else 0.0), best[q][1]
+    while best:
+        q = min(best, key=ends)
+        at, k = best[q]
+        r, n = flat[k]
+        out.append((r, n, q[1]))
+        end = at + n["cost"][q[1]]
+        free[q] = end if q[1] != "r" else 0.0
+        for x in n["fns"]:
+            ready[(r, x)].discard(k)
+            choose((r, x))
+        for j in succ[k]:
+            when[j] = max(when[j], end + after(k, j))
+            count[j] -= 1
+            if not count[j]:
+                put(j)
+    return out
+
+
+def rank_program(g, core, T, topo):
+    r = T.rank_of(core)
+    if r is None:
+        return
+    cores = list(T.cores)
+    if "order" not in _PLANS:
+        _PLANS["order"] = arrange([calls(i, cores, topo) for i in range(N)])
+    queue = {"v": g.vector, "s": g.scalar, "t": g.tensor, "g": g, "y": g.sync}
+    total, known, snap, log = {}, {q: {} for q in queue}, {}, {}
+
+    def ap(w):
+        n, c0, c1, st, p0, p1 = w[:6]
+        if len(w) > 6:
+            a0, a1, b0, b1 = w[6]
+            return T[n][p0:p1, a0, b0:b1] if a1 == a0 + 1 else T[n][p0:p1, a0:a1, b0:b1]
+        n, at = LOG[n][:2]
+        c0, c1 = c0 + at, c1 + at
+        return T[n][p0:p1, c0:c1] if st == 1 else T[n][p0:p1, c0:c1:st]
+
+    env = dict(queue, T=T, ap=ap)
+
+    def wait(q, tok):
+        s, v = tok
+        if known[q].get(s, 0) >= v:
+            return
+        queue[q].wait_ge(T.sem[s], v)
+        known[q][s] = v
+        for a, b in snap.get(tok, {}).items():
+            if known[q].get(a, 0) < b:
+                known[q][a] = b
+
+    tokens = {}
+    for rank, n, q in _PLANS["order"]:
+        if rank != r:
+            continue
+        s = n["sem"] or _QS[q]
+        if q != "r":
+            need = {}
+            for ws, isw in ((n["rd"], False), (n["wr"], True)):
+                for w in ws:
+                    for w2, isw2, tok, q2 in log.get(w[0], ()):
+                        if (isw or isw2 or (w[0] in ("pa", "pu") and q != q2)) and meet(w, w2):
+                            need[tok[0]] = max(need.get(tok[0], 0), tok[1])
+            for a in n["after"]:
+                tok = tokens[a["i"]]
+                need[tok[0]] = max(need.get(tok[0], 0), tok[1])
+            for x in sorted(need):
+                wait(q, (x, need[x]))
+            ins = n["fns"][q](env)
+            total[s] = total.get(s, 0) + n["by"]
+            if not n["cast"]:
+                ins.then_inc(T.sem[s], n["by"])
+                snap[(s, total[s])] = dict(known[q])
+        else:
+            total[s] = n["by"]
+        tok = tokens[n["i"]] = (s, total[s])
+        for ws, isw in ((n["rd"], False), (n["wr"], True)):
+            for w in ws:
+                log.setdefault(w[0], []).append((w, isw, tok, q))
+    for s in sorted(total):
+        wait("g", (s, total[s]))

@@ -3,10 +3,12 @@ from concourse.mybir import dt, AluOpType as Op, AxisListType, ActivationFunctio
 
 N, P, K = 4, 256, 64
 R1, R2 = 352, 608
+M0 = 96
 BUILD = ((0, 2), (1, 3))
 TINY = 2.0 ** -110
+BIG = 4096.0
 UNIT = 32768.0
-TUNE = dict(wake=150.0, fac=1.2, load=900.0, issue=60.0, rissue=250.0, hop=700.0, row=12.0, byte=0.06, tol=20.0, bias=60.0)
+TUNE = dict(wake=150.0, fac=1.2, load=900.0, issue=60.0, rissue=250.0, hop=700.0, row=12.0, byte=0.06, tol=0.0, bias=20.0)
 
 F, B, I, U16, CODES = "float32", "bfloat16", "int32", "uint16", "float8_e4m3fn_x4"
 SCRATCH, LOG, _TOP = {}, {}, {}
@@ -32,7 +34,7 @@ def _slab(slab, dtype, **kw):
         SCRATCH[slab] = ("sbuf", [128, _TOP[slab]], dtype)
 
 
-_own(B, onb=512, tbt=1040, ut=512, wt=1024, eb=2048, ub0=512, ub1=512, h0=512, h1=512)
+_own(B, onb=512, tbt=1040, ut=512, wt=1024, eb=2048, ub0=512, ub1=512, h0=512, h1=512, mp=1024)
 for _n, _c in dict(tq=256, tw=512, tx=768, uq=128, uc=128, ug=128, eq=512, wq=256, tz=256, sla=64, slb=64,
                    laa=128, lab=128, psa=128, psb=128, ou=256).items():
     _own(CODES, **{_n: _c})
@@ -40,22 +42,23 @@ for _n, _c in dict(tq=256, tw=512, tx=768, uq=128, uc=128, ug=128, eq=512, wq=25
 for _n in ("pa", "pu"):
     SCRATCH[_n] = ("psum", [128, 2048], F)
     LOG[_n] = (_n, 0, 2048, F)
-_own(F, l0=16, l1=16, xs=256, xd=128, ys=512, fr=640, ft=512)
-_cube(row0=(2, 128), row1=(2, 128), kt=(4, 32), mm0=(4, 64), mm1=(4, 64))
-_slab("fs", F, jc=2, jp0=2, jp1=2, jp2=2, jpb=2, cf=12, rr=16, rh=8, rk8=8, wm=16, nq=8, ca=8, cb=8, c1=8, c2=8, c3=8, c4=8,
-      s1=8, s2=8, s3=8, s4=8, s5=8, wl=8, wa=3, wb=1, wc=1, wd=3, wl1=6, ma=12, mb=12, m0=16, rho=4, csf=8, cso=2, gm=40, mrow=32,
-      kf=2, kg=2, tr=8, ofrf=4, va=128, vb=128, d0a=8, d0b=8, oh=512, prc=520, prg=390, rep=8, nrep=8, kra=12, krb=12, kro=16, kr0=16,
-      pm=130, src1=2, oho=128, sqc=8, gq=6, lr=128, bsf=256, junk=4096)
+_own(F, l0=16, l1=16, xs=256, xd=128, yb0=1024, yb1=1024, winc=160, wing=160)
+_cube(row0=(4, 64), row1=(4, 64), kt=(4, 32), mm0=(4, 64), mm1=(4, 64))
+_slab("fs", F, jc=2, jp0=2, jp2=2, jpb=2, cf=12, rr=16, rh=8, wm=16, nq=4, ca=4, cb=4, c1=4, c2=4, c3=4, c4=4,
+      s1=4, s2=4, s3=4, s4=4, s5=4, wl=4, wlb0=8, wlb1=6, wa=3, wb=1, wc=1, wd=3, wl1=3, ma=12, mb=12, m0=16, rho=4, gm=40, mrow=32,
+      kf=16, kg=16, ofrf=4, d0a=8, kra=12, krb=12, kr0=16, kk=10, o1f=8, sra=2, srb=2, src1=2, cg=128, gg=96, gs=96,
+      fa=16, fb=16, fc=16, yn=256, lr=128, bsf=256, one=48, ga=8, gb=8, junk=4096)
+_slab("hs", B, i16=256, dg=256, d0g=256, d0c=64, va=64, vb=64, mg=160, ms=160, fm=256, fn=256)
 for _t in "01":
-    _slab("fs", F, **{n + _t: c for n, c in dict(sq=16, sc=16, ex=64, sa=2, nd=2, dl=2, th=80, cm=544, po=2, mt=256, lw=4, ab=4, ac=4,
-                                                 ga=8, gx=2, gy=8, ge=8, gw=8, gn=2, pay=2, er=64).items()})
-    _slab("is_", I, **{n + _t: c for n, c in dict(wj=4, rk=6, fi=4, fj=4, fk=4, fa=8, fl=4, fm=4, fe=4, fo=8).items()})
-    _slab("us", U16, **{n + _t: c for n, c in dict(off=4, rfo=6, ofs=8, exo=4).items()})
-_slab("is_", I, bi=128, key=64, bj=256, ji=2, jj=2, pi=4, ci=12, csi=8, csj=8, tri32=8)
-_slab("us", U16, ofr=4, ofu=32, ofv=32, fou=16)
+    _slab("fs", F, **{n + _t: c for n, c in dict(sq=16, sc=128, ex=64, dl=2, th=80, cm=544, po=2, mt=256, lw=4, ab=4, ac=4,
+                                                 gx=2, gy=8, ge=8, gw=8, pay=2, er=64).items()})
+    _slab("is_", I, **{n + _t: c for n, c in dict(wj=4, wk=2, rk=6, fi=4).items()})
+    _slab("us", U16, **{n + _t: c for n, c in dict(off=4, rfo=6, ofs=4).items()})
+_slab("is_", I, bi=128, bk=64, bj=256, pi=4, ci=12, csi=8, csj=8, csk=8)
+_slab("us", U16, ofr=4, ofu=32, ofv=32, fou=16, ko=10, o1=8, o2=6)
 
-SEMAPHORES = ["sv", "ss", "st", "sg", "dl_u", "dl_t0", "dl_t1", "dl_t2", "dl_w", "dl_x", "dl_x_s", "dl_m", "dl_m_s", "dl_n", "dl_n_s",
-              "dbs", "dy0", "dy1", "doc", "ls", "a0", "a1", "ha0", "ha1", "hb0", "hb1"]
+SEMAPHORES = ["sv", "ss", "st", "sg", "dl_u", "dl_t0", "dl_t1", "dl_t2", "dl_w", "dl_z", "dl_x", "dl_x_s", "dl_m", "dl_m_s", "dl_n", "dl_n_s",
+              "dbs", "dy0", "dy1", "doc", "dos", "ls", "a0", "a1", "ha0", "ha1", "hb0", "hb1"]
 _QS = {"v": "sv", "s": "ss", "t": "st", "g": "sg"}
 _PLANS = {}
 
@@ -97,13 +100,25 @@ def calls(r, cores, topo):
         nodes.append(dict(rd=rd, wr=wr, fns=fns, cost=cost, sem=sem, by=by, lag=lag, after=list(after), to=to, cast=cast, i=len(nodes)))
         return nodes[-1]
 
-    def small(n):
+    def small(n, *ws):
+        if ws and all(LOG[w[0]][3] in (B, U16) for w in ws):
+            n = n / 2
         return max(64, n) * cyc
 
     def tt(out, a, b, op):
         both = a[0] not in ("pa", "pu") and b[0] not in ("pa", "pu")
         return node([a, b], [out], {"v": lambda e: e["v"].tensor_tensor(e["ap"](out), e["ap"](a), e["ap"](b), op)},
                     {"v": small(width(out) * (2 if both else 1))})
+
+    def own(out, win, off):
+        n = width(out)
+        b = W("dg", 0, n)
+        return node([win, off, b], [out], {"v": lambda e: e["v"].tensor_tensor(e["ap"](out), e["ap"](win).indirect(e["ap"](off)), e["ap"](b), Op.mult)},
+                    {"v": (50 + 2 * 0.83 * n) * TUNE["fac"]})
+
+    def strew(win, off, src):
+        node([off, src], [win], {"v": lambda e: e["v"].tensor_copy(e["ap"](win).indirect(e["ap"](off)), e["ap"](src))},
+             {"v": (50 + 3.5 * 0.83 * width(src)) * TUNE["fac"]})
 
     def ts(out, a, s1, op0, s2=None, op1=None):
         rd = [a] + [s for s in (s1, s2) if isinstance(s, tuple)]
@@ -113,7 +128,7 @@ def calls(r, cores, topo):
             if op1 is not None:
                 return e["v"].tensor_scalar(e["ap"](out), e["ap"](a), x1, x2, op0, op1)
             return e["v"].tensor_scalar(e["ap"](out), e["ap"](a), x1, None, op0)
-        return node(rd, [out], {"v": f}, {"v": small(width(out))})
+        return node(rd, [out], {"v": f}, {"v": small(width(out), out, a)})
 
     def cp(out, a, q="v"):
         fns = {"v": lambda e: e["v"].tensor_copy(e["ap"](out), e["ap"](a)), "s": lambda e: e["s"].activation(e["ap"](out), e["ap"](a), Act.Copy)}
@@ -123,14 +138,18 @@ def calls(r, cores, topo):
         return node([a], [out], {"v": lambda e: e["v"].tensor_reduce(e["ap"](out), e["ap"](a), AxisListType.X, op)}, {"v": small(width(a))})
 
     def fill(out, c):
-        return node([], [out], {"v": lambda e: e["v"].memset(e["ap"](out), c)}, {"v": small(width(out) * (0.5 if LOG[out[0]][3] in (B, U16) else 1))})
+        return node([], [out], {"v": lambda e: e["v"].memset(e["ap"](out), c)}, {"v": small(width(out), out)})
 
     def turn(out, a):
         return node([a], [out], {"v": lambda e: e["v"].transpose(e["ap"](out), e["ap"](a))}, {"v": small(width(a))})
 
-    def scan(out, d0, d1):
-        return node([d0, d1], [out], {"v": lambda e: e["v"].tensor_tensor_scan(e["ap"](out), e["ap"](d0), e["ap"](d1), 0.0, Op.mult, Op.subtract)},
-                    {"v": small(width(out))})
+    def scan(out, d0, d1, op=Op.subtract):
+        return node([d0, d1], [out], {"v": lambda e: e["v"].tensor_tensor_scan(e["ap"](out), e["ap"](d0), e["ap"](d1), 0.0, Op.mult, op)},
+                    {"v": small(width(out), out, d0, d1)})
+
+    def spread(out, s):
+        a = W("one", 0, 32)
+        return node([a, s], [out], {"s": lambda e: e["s"].activation(e["ap"](out), e["ap"](a), Act.Abs, scale=e["ap"](s))}, {"s": small(width(out))})
 
     def act(out, a, f, off=None):
         rd = [a] + [w for w in (off,) if w is not None]
@@ -177,8 +196,8 @@ def calls(r, cores, topo):
     def move(q, out, a, sem):
         return node([a], [out], {q: lambda e: e[q].dma_start(raw(e, out), raw(e, a))}, {q: TUNE["issue"]}, sem, 16, TUNE["load"])
 
-    def store(q, dst, a, sem):
-        return node([a], [], {q: lambda e: e[q].dma_start(dst(e["T"]), raw(e, a))}, {q: TUNE["issue"]}, sem, 16, TUNE["load"])
+    def store(q, dst, a, sem, more=0.0):
+        return node([a], [], {q: lambda e: e[q].dma_start(dst(e["T"]), raw(e, a))}, {q: TUNE["issue"]}, sem, 16, TUNE["load"] + more)
 
     peers = [c for c in cores if c != core]
 
@@ -213,16 +232,15 @@ def calls(r, cores, topo):
     load("y", W("tbt", 0, 512), "tb", 0, 512, "dl_t0")
     load("s", W("tbt", 512, 1024), "tb", 512, 1024, "dl_t1")
 
-    iota(W("pi", 0, 1), [[0, 1]], 0, 1)
-    iota(W("pi", 1, 2), [[0, 1]], 1, 1)
+    iota(W("pi", 0, 2), [[1, 2]], 0, 1)
     iota(W("pi", 2, 4), [[128, 2]], r, 1)
     iota(W("jc"), [[128, 2]], 0, 1)
     iota(W("rr"), [[1, 4], [0, 4]])
     iota(W("rh"), [[1, 4], [0, 2]])
-    iota(W("rk8"), [[0, 2], [1, 4]])
     iota(W("mrow"), [[1, 32]])
     fill(W("ut", 8, 512), 0.0)
     fill(W("onb"), 1.0)
+    fill(W("one"), 1.0)
 
     def unit(b):
         o = W("eb", 512 * b, 512 * b + 512)
@@ -230,10 +248,8 @@ def calls(r, cores, topo):
              {"g": 170 * TUNE["fac"] + 1024 * cyc})
     for b in range(4):
         unit(b)
-    for y in range(4):
-        iota(C("kt", y, y + 1, 0, 32), [[0, 2], [1, 16]], 16 * y)
-    iota(W("kf"), [[16, 2]])
-    iota(W("tr"), [[16, 8]], 512)
+    iota(C("kt", 0, 4, 0, 32), [[16, 4], [0, 2], [1, 16]])
+    iota(W("kf"), [[16, 16]])
     iota(W("ofrf"), [[2, 2], [0, 2]])
 
     pp = W("pi", 0, 1)
@@ -244,8 +260,6 @@ def calls(r, cores, topo):
     ts(W("ci", 6, 7), pp, 31, Op.bitwise_and)
     ts(W("ci", 7, 8), pp, 5, Op.arith_shift_right, 1, Op.bitwise_and)
     ts(W("ci", 8, 9), pp, 6, Op.arith_shift_right)
-    fill(W("exo0", 0, 2), 14)
-    fill(W("exo0", 2, 4), 15)
     fill(W("d0a"), 1.0)
     fill(W("d0a", 0, 1), 0.0)
     fill(W("d0a", 4, 5), -1.0)
@@ -266,8 +280,7 @@ def calls(r, cores, topo):
     def mine(l, bank):
         for h in range(2):
             o = 512 * (bank + h)
-            cp(W(l, 4 * r + 2 * h, 4 * r + 2 * h + 1), W("pa", o, o + 1), "s")
-            act(W(l, 4 * r + 2 * h + 1, 4 * r + 2 * h + 2), W("pa", o + 1, o + 2), Act.Abs)
+            cp(W(l, 4 * r + 2 * h, 4 * r + 2 * h + 2), W("pa", o, o + 2), "vs")
         v = W(l, 4 * r, 4 * r + 4)
         send([(v, v, peers, alle)], "a" + l[1])
 
@@ -282,35 +295,40 @@ def calls(r, cores, topo):
         mine("l1", 2)
     lands("a1", len(alle) * (3 if r == 0 else 2), [W("l1", 4 * o, 4 * o + 4) for o in range(1, N) if o != r])
 
-    u1, u2, u3 = 4096 / UNIT, 1024 / UNIT, 256 / UNIT
-    ts(W("nq"), W("rk8"), q0, Op.not_equal)
-    ts(W("ca"), W("rk8"), q0, Op.min)
-    ts(W("cb"), W("rk8"), q0, Op.max)
-    ts(W("s4"), W("rk8"), u1, Op.mult, 3 * u3 - 0.5, Op.add)
+    u1, u2, u3, uj = 4096 / UNIT, 4 / UNIT, 1 / UNIT, 16 / UNIT
+    rk = W("mrow", 0, 4)
+    ts(W("nq"), rk, q0, Op.is_equal, BIG, Op.mult)
+    ts(W("ca"), rk, q0, Op.min)
+    ts(W("cb"), rk, q0, Op.max)
+    ts(W("s4"), rk, u1, Op.mult, 3 * u3, Op.add)
     ts(W("c1"), W("ca"), 0.0, Op.is_equal, u2, Op.mult)
     ts(W("c2"), W("cb"), 1.0, Op.is_equal, 1.0, Op.add)
     ts(W("c3"), W("cb"), 3.0, Op.is_equal, -u3, Op.mult)
     ts(W("c4"), W("ca"), 2.0, Op.is_equal, 1.0, Op.add)
     tt(W("s1"), W("c1"), W("c2"), Op.mult)
     tt(W("s2"), W("c3"), W("c4"), Op.mult)
-    tt(W("s3"), W("s1"), W("s4"), Op.add)
-    tt(W("s5"), W("s3"), W("s2"), Op.add)
-    tt(W("wl"), W("s5"), W("nq"), Op.mult)
-    ts(W("jp1"), W("jc"), 1.0 / UNIT, Op.mult, 0.5, Op.add)
-    tt(W("jp0"), W("jc"), W("jp1"), Op.add)
+    tt(W("s3"), W("s4"), W("nq"), Op.add)
+    tt(W("s5"), W("s1"), W("s2"), Op.add)
+    tt(W("wl"), W("s5"), W("s3"), Op.add)
+    ts(W("jp0"), W("jc"), 1.0 + uj, Op.mult)
+    for h in range(2):
+        ts(W("wlb0", 4 * h, 4 * h + 4), W("wl"), W("jp0", h, h + 1), Op.add)
 
     ts(W("ofu"), W("mrow"), 0.0, Op.is_ge, q0, Op.mult)
     ts(W("ofv"), W("ofu"), 4.0, Op.add)
     ready = [quant("tw", 320, "tbt", 0, 128)]
     act(W("ub0"), W("ut"), Act.Copy, off=W("ofu"))
     act(W("ub1"), W("ut"), Act.Copy, off=W("ofv"))
-    iota(W("va"), [[0, 2], [1, 64]], R1)
-    iota(W("vb"), [[0, 2], [1, 64]], R2)
-    iota(W("fr", 0, 512), [[16, 16], [0, 2], [1, 16]])
-    fill(W("fr", 512, 640), 0.0)
+    before = r == BUILD[1][1]
+    old = R2 - 64 if before else R2 + 64
+    lift = old - M0
+    iota(W("va"), [[1, 64]], M0)
+    iota(W("vb"), [[1, 64]], R2 - lift)
+    iota(W("i16"), [[0, 16], [1, 16]])
+    ts(W("dg"), W("i16"), xf, Op.is_equal)
+    ts(W("d0g"), W("i16"), 0.0, Op.not_equal)
     ts(W("kg"), W("kf"), xf, Op.add)
     ts(W("ofr"), W("ofrf"), gf, Op.add)
-    ts(W("tri32"), W("tr"), xf, Op.add)
     when = 0 if r in BUILD[0] else 1
     quant("eq", 0, "eb", 0, 512)
     quant(("psa", "psb")[when], 0, "tbt", 0, 128)
@@ -319,10 +337,15 @@ def calls(r, cores, topo):
         move("y", W("tw" + x, 0, 256), W("tq" + x), "dl_m" + x)
     quant("uc", 0, "ub0", 0, 128)
     quant("ug", 0, "ub1", 0, 128)
+    for a, b in ((0, 504), (504, 1008), (1008, 1024)):
+        load("y", W("mp", a, b), "u", 8, 8 + b - a, "dl_z", [W("l0")])
     load("y", W("wt"), "w", 0, 1024, "dl_w", [W("l0")])
     for x in ("", "_s"):
         move("y", W("tx" + x, 0, 256), W("tq" + x), "dl_n" + x)
     quant("wq", 0, "wt", 0, 256)
+    for o in range(2):
+        mm(2 + o, "wq", 128 * o, "tq", 0, 256)
+        cp(W("yb%d" % o, 256 * r, 256 * r + 256), W("pa", 512 * (2 + o), 512 * (2 + o) + 256), "s")
 
     ts(W("ma"), W("rr", 0, 12), q1, Op.is_lt)
     ts(W("mb"), W("rr", 0, 12), q1, Op.is_ge)
@@ -330,71 +353,68 @@ def calls(r, cores, topo):
     cp(W("rho", 0, 1), q1)
     tt(W("rho", 1, 4), W("rr", 0, 12, 4), W("mb", 0, 12, 4), Op.add)
     r1, r2, r3 = W("rho", 1, 2), W("rho", 2, 3), W("rho", 3, 4)
-    ts(W("wa"), W("rho", 1, 4), u1, Op.mult, -0.5, Op.add)
+    ts(W("wa"), W("rho", 1, 4), u1, Op.mult)
     ts(W("wb"), r1, u2, Op.mult)
     ts(W("wc"), r3, u3, Op.mult)
     ts(W("wd", 0, 1), r2, u2, Op.mult, W("wa", 0, 1), Op.add)
     ts(W("wd", 1, 3), W("wa", 1, 3), W("wb"), Op.add)
-    for h in range(2):
-        ts(W("wl1", 3 * h, 3 * h + 2), W("wd", 0, 2), W("wc"), Op.add)
-        ts(W("wl1", 3 * h + 2, 3 * h + 3), r2, u3, Op.mult, W("wd", 2, 3), Op.add)
-    fill(W("d0b"), 1.0)
-    fill(W("d0b", 0, 8, 4), 0.0)
-    fill(W("d0b", 1, 8, 4), -1.0)
-    fill(W("exo1", 0, 2), 3)
-    fill(W("exo1", 2, 4), 7)
+    ts(W("wl1", 0, 2), W("wd", 0, 2), W("wc"), Op.add)
+    ts(W("wl1", 2, 3), r2, u3, Op.mult, W("wd", 2, 3), Op.add)
+    fill(W("d0c"), 1.0)
+    fill(W("d0c", 16, 17), -1.0)
     for h in range(2):
         ts(W("csi", 4 * h, 4 * h + 4), W("rho"), 4097.0, Op.mult, W("jc", h, h + 1), Op.add)
-    ts(W("csj"), W("csi"), 3 * 4096 + 255, Op.bitwise_and)
-    cp(W("csf"), W("csj"))
-    ts(W("cso"), i1, 4096.0 * r, Op.add)
-    ts(W("ji"), W("jc"), 1.0, Op.add)
-    ts(W("jj"), W("ji"), 255, Op.bitwise_and)
-    ts(W("jp2"), W("jj"), 1.0 / UNIT, Op.mult, 0.5, Op.add)
-    cp(W("pm", 64, 130, 65), W("cf", 4, 6), "vs")
+    ts(W("csj"), W("csi"), 255, Op.bitwise_and)
+    ts(W("csk"), W("csi"), 4, Op.arith_shift_right, 768, Op.bitwise_and)
+    tt(W("kk", 0, 8), W("csj"), W("csk"), Op.add)
+    ts(W("kk", 8, 10), i1, 256.0 * r, Op.add)
+    cp(W("ko"), W("kk"))
+    ts(W("jp2"), i1, uj, Op.mult)
+    fill(W("winc", 0, M0), 0.0)
+    fill(W("wing", 0, M0), 0.0)
 
     cp(W("l1", 0, 4), W("l0", 0, 4), "vs")
     tt(W("krb"), W("l1", 4, 16), W("mb"), Op.mult)
     tt(W("kra"), W("l1", 0, 12), W("ma"), Op.mult)
     tt(W("kr0"), W("l1"), W("m0"), Op.mult)
-    tt(W("kro", 4, 16), W("kra"), W("krb"), Op.add)
     for h in range(2):
-        red(W("kro", 2 * h, 2 * h + 1), W("kr0", 2 * h, 16, 4), Op.add)
+        tt(W("winc", 4 * h + 1, 4 * h + 4), W("kra", 2 * h, 12, 4), W("krb", 2 * h, 12, 4), Op.add)
+        tt(W("gb", 4 * h + 1, 4 * h + 4), W("kra", 2 * h + 1, 12, 4), W("krb", 2 * h + 1, 12, 4), Op.add)
+        act(W("wing", 4 * h + 1, 4 * h + 4), W("gb", 4 * h + 1, 4 * h + 4), Act.Abs)
+        total(W("winc", 4 * h, 4 * h + 1), W("kr0", 2 * h, 16, 4))
 
     def count(t):
         n = str(t)
-        src, off = (W("sc0"), W("exo0")) if t == 0 else (W("sc1", 0, 8), W("exo1"))
-        s2 = W("sc0", 14, 16) if t == 0 else W("sc1", 3, 8, 4)
         rn, th, cm = "row" + n, "th" + n, "cm" + n
-        act(W("ex" + n), src, Act.Abs, off=off)
-        act(W("sa" + n), s2, Act.Abs)
+        sa = [W("ex" + n, 32 * h, 32 * h + 1) for h in range(2)]
         for h in range(2):
-            turn(C(rn, h, h + 1, 0, 32), W("ex" + n, 32 * h, 32 * h + 32))
-        for h in range(2):
-            s = W("sa" + n, h, h + 1)
-            ts(W("nd" + n, h, h + 1), s, 1.5 * 2.0 ** -24, Op.mult, s, Op.add)
-            ts(W("dl" + n, h, h + 1), W("nd" + n, h, h + 1), TINY, Op.max, W("sa" + n, h, h + 1), Op.subtract)
+            at = 64 * h + 63 if t else 14 + h
+            spread(W("ex" + n, 32 * h, 32 * h + 32), W("sc" + n, at, at + 1))
+        turn(C(rn, 0, 1, 0, 64), W("ex" + n))
+        ts(W("dl" + n), W("ex" + n, 0, 64, 32), 1.5 * 2.0 ** -24, Op.mult, TINY, Op.max)
         for a in range(2):
-            cp(C(rn, 0, 2, 64, 96, 64 * a, 64 * a + 64), C(rn, 0, 2, 0, 32, 64 - 64 * a, 128 - 64 * a), "vs")
+            cp(C(rn, 2, 3, 0, 64, 64 * a, 64 * a + 64), C(rn, 0, 1, 0, 64, 64 - 64 * a, 128 - 64 * a), "vs")
         for x in (1, 3):
             for a in range(4):
                 b = a ^ x
-                cp(C(rn, 0, 2, 32 * x, 32 * x + 32, 32 * a, 32 * a + 32), C(rn, 0, 2, 0, 32, 32 * b, 32 * b + 32), "vs")
+                cp(C(rn, x, x + 1, 0, 64, 32 * a, 32 * a + 32), C(rn, 0, 1, 0, 64, 32 * b, 32 * b + 32), "vs" if x == 1 else "s")
         for h in range(2):
-            ts(W(th, 40 * h, 40 * h + 35), W("gm", 0, 35), W("dl" + n, h, h + 1), Op.mult, W("sa" + n, h, h + 1), Op.add)
+            ts(W(th, 40 * h, 40 * h + 35), W("gm", 0, 35), W("dl" + n, h, h + 1), Op.mult, sa[h], Op.add)
         for h in range(2):
-            tt(W(cm, 272 * h + 232, 272 * h + 264), C(rn, h, h + 1, 0, 32), W(th, 40 * h + 3, 40 * h + 35), Op.is_ge)
-            ts(W(cm, 272 * h + 200, 272 * h + 232), C(rn, h, h + 1, 32, 64), W(th, 40 * h, 40 * h + 1), Op.is_ge)
-            other = W(th, 2, 3) if h == 0 else W("sa" + n, 1, 2)
-            ts(W(cm, 272 * h, 272 * h + 128), C(rn, 1 - h, 2 - h, 0, 128), other, Op.is_ge)
-            ts(W(cm, 272 * h + 128, 272 * h + 192), C(rn, h, h + 1, 64, 128), W(th, 40 * h + 1, 40 * h + 2), Op.is_ge)
-            total(W(cm, 272 * h + 192, 272 * h + 193), W(cm, 272 * h + 200, 272 * h + 264))
-            total(W("po" + n, h, h + 1), W(cm, 272 * h, 272 * h + 193))
+            o = 272 * h
+            other = W(th, 2, 3) if h == 0 else sa[1]
+            ts(W(cm, o, o + 128), C(rn, 0, 4, 32 - 32 * h, 64 - 32 * h), other, Op.is_ge)
+            tt(W(cm, o + 200, o + 232), C(rn, 0, 1, 32 * h, 32 * h + 32), W(th, 40 * h + 3, 40 * h + 35), Op.is_ge)
+            ts(W(cm, o + 232, o + 264), C(rn, 1, 2, 32 * h, 32 * h + 32), W(th, 40 * h, 40 * h + 1), Op.is_ge)
+            ts(W(cm, o + 128, o + 192), C(rn, 2, 4, 32 * h, 32 * h + 32), W(th, 40 * h + 1, 40 * h + 2), Op.is_ge)
+            total(W(cm, o + 192, o + 193), W(cm, o + 200, o + 264))
+            total(W("po" + n, h, h + 1), W(cm, o, o + 193))
 
     def listed(t):
         m, mt, lw, b, c = [x + str(t) for x in ("mm", "mt", "lw", "ab", "ac")]
-        for h in range(2):
-            ts(C(m, 0, 4, 32 * h, 32 * h + 32), C("kt", 0, 4, 0, 32), W("po%d" % t, h, h + 1), Op.is_equal, W("pay%d" % t, h, h + 1), Op.mult)
+        for y in (0, 2):
+            for h in range(2):
+                ts(C(m, y, y + 2, 32 * h, 32 * h + 32), C("kt", y, y + 2, 0, 32), W("po%d" % t, h, h + 1), Op.is_equal, W("pay%d" % t, h, h + 1), Op.mult)
         for y in range(4):
             turn(W(mt, 64 * y, 64 * y + 64), C(m, y, y + 1, 0, 64))
         for y in range(4):
@@ -405,20 +425,19 @@ def calls(r, cores, topo):
             tt(W(c, 0, 4, 1, 64 * k, 64 * k + 64), W(b, 0, 4, 1, 64 * k, 64 * k + 64), W(b, 0, 4, 1, 64 - 64 * k, 128 - 64 * k), Op.add)
         return W(c, 0, 4)
 
-    def lost(t, n, wl, base):
-        k = n // 2
+    def lost(t):
+        k = 4 - t
         s = str(t)
-
-        def size(h):
-            return W("gy0", h, 8, 2) if t == 0 else W("ga1", k * h, k * h + k)
         for h in range(2):
-            red(W("gx" + s, h, h + 1), size(h), Op.max)
+            if t == 0:
+                size, top = W("gy0", h, 8, 2), W("gx0", h, h + 1)
+                red(top, size, Op.max)
+            else:
+                size, top = W("gs", 48 * h + 15, 48 * h + 48, 16), W("gs", 48 * h + 47, 48 * h + 48)
+            ts(W("ge" + s, k * h, k * h + k), size, top, Op.not_equal, BIG, Op.mult)
+        tt(W("gw" + s, 0, 2 * k), W("ge" + s, 0, 2 * k), W("wlb" + s), Op.add)
         for h in range(2):
-            ts(W("ge" + s, k * h, k * h + k), size(h), W("gx" + s, h, h + 1), Op.is_equal)
-        tt(W("gw" + s, 0, n), W("ge" + s, 0, n), W(wl), Op.mult)
-        for h in range(2):
-            red(W("gn" + s, h, h + 1), W("gw" + s, k * h, k * h + k), Op.min)
-        tt(W("pay" + s), W("gn" + s), W(base), Op.add)
+            red(W("pay" + s, h, h + 1), W("gw" + s, k * h, k * h + k), Op.min)
 
     def gather(t, lists):
         n = "ab"[t]
@@ -449,12 +468,16 @@ def calls(r, cores, topo):
     def numbers(t, w):
         ts(W("wj%d" % t), w, UNIT, Op.mult)
 
-    def buildlist(t):
+    def buildlist(t, w):
         s, d = str(t), BUILD[t].index(r)
-        v = W("wj" + s, 2 * d, 2 * d + 2)
-        ts(W("rk" + s, 0, 2), v, 3, Op.bitwise_and)
-        ts(W("rk" + s, 2, 4), v, 10, Op.arith_shift_right, 3, Op.bitwise_and)
-        ts(W("rk" + s, 4, 6), v, 8, Op.arith_shift_right, 3, Op.bitwise_and)
+        v = vq = W("wj" + s, 2 * d, 2 * d + 2)
+        up = t * (1 - r) % N
+        if up:
+            vq = W("wk" + s)
+            ts(vq, W(w[0], 2 * d, 2 * d + 2), UNIT, Op.mult, 16.0 * up, Op.add)
+        ts(W("rk" + s, 0, 2), vq, 4, Op.arith_shift_right, 3, Op.bitwise_and)
+        ts(W("rk" + s, 2, 4), v, 2, Op.arith_shift_right, 3, Op.bitwise_and)
+        ts(W("rk" + s, 4, 6), v, 3, Op.bitwise_and)
         for y in range(2):
             ts(W("rfo" + s, y, 6, 2), W("rk" + s, y, 6, 2), 32.0, Op.mult, W("kg", y, y + 1), Op.add)
 
@@ -483,35 +506,34 @@ def calls(r, cores, topo):
 
     def mapped(t):
         s = str(t)
-        i, a = W("fi" + s), W("wj" + s)
-        ts(W("fl" + s), a, 12, Op.arith_shift_right, 3, Op.bitwise_and)
-        if t and r != 1:
-            ts(W("fj" + s), a, float(r - 1), Op.add)
-            a = W("fj" + s)
-        ts(i, a, 255, Op.bitwise_and)
-        ts(W("fk" + s), a, 240, Op.bitwise_and)
-        ts(W("fm" + s), W("fl" + s), float(r), Op.not_equal, 4096.0, Op.mult)
-        tt(W("fe" + s), i, W("fk" + s), Op.add)
-        tt(W("fa" + s, 0, 4), W("fe" + s), W("fm" + s), Op.add)
-        ts(W("fa" + s, 4, 8), W("fa" + s, 0, 4), 16.0, Op.add)
-        tt(W("fo" + s), W("fa" + s), W("tri32"), Op.min)
-        cp(W("ofs" + s), W("fo" + s))
+        ts(W("fi" + s), W("wj" + s), 4, Op.arith_shift_right, 1023, Op.bitwise_and)
+        cp(W("ofs" + s), W("fi" + s))
+        strew(W("mp"), W("ofs" + s), W("va" if t == 0 else "vb"))
 
-    def enter(t):
-        win, off, src = W("fr"), W("ofs%d" % t), W("va" if t == 0 else "vb")
-        node([off, src], [win], {"v": lambda e: e["v"].tensor_copy(e["ap"](win).indirect(e["ap"](off)), e["ap"](src))},
-             {"v": (50 + 3 * 0.83 * 128) * TUNE["fac"]})
+    def placed(out, a, b, m, up, home):
+        ts(a, m, 1000.0, Op.mult, float(up), Op.min)
+        tt(b, a, m, Op.add)
+        tt(out, b, home, Op.max)
 
-    def listrow(t, w):
-        s = str(t)
+    def products(t, src, c0, at):
+        for o in range(2):
+            bank = 2 - 2 * t + o
+            mm(bank, "wq", 128 * o, src, c0)
+            v = W("yn", 128 * t + 64 * o, 128 * t + 64 * o + 64)
+            cp(v, W("pa", 512 * bank + at, 512 * bank + at + 64), "vs")
+            strew(W("yb%d" % o), W("ofs%d" % t), v)
+
+    def stripes(t, w):
+        s, o = str(t), 128 * t
         act(W("er" + s), w, Act.Copy, off=W("ofr"))
         turn(W("lr", 64 * t, 64 * t + 64), W("er" + s))
-        ts(W("bi", 64 * t, 64 * t + 64), W("lr", 64 * t, 64 * t + 64), UNIT, Op.mult, -1.0 * t, Op.add)
-
-    def stripes(t):
-        o = 128 * t
-        b = W("bi", 64 * t, 64 * t + 64, 1, 0, 1)
-        ts(W("bj", o, o + 64, 1, 0, 1), b, 255, Op.bitwise_and)
+        a = W("lr", 64 * t, 64 * t + 64, 1, 0, 1)
+        b = c = W("bi", 64 * t, 64 * t + 64, 1, 0, 1)
+        ts(b, a, UNIT, Op.mult)
+        if t * r:
+            c = W("bk", 0, 64, 1, 0, 1)
+            ts(c, a, UNIT, Op.mult, 16.0 * (256 - r), Op.add)
+        ts(W("bj", o, o + 64, 1, 0, 1), c, 4, Op.arith_shift_right, 255, Op.bitwise_and)
         ts(W("bj", o + 64, o + 128, 1, 0, 1), b, 12, Op.arith_shift_right, 3, Op.bitwise_and)
         cp(W("bsf", o, o + 128, 1, 0, 1), W("bj", o, o + 128, 1, 0, 1))
 
@@ -519,84 +541,75 @@ def calls(r, cores, topo):
         tt(W("sq0", 8 * m, 8 * m + 8), W("l0", 0, 16, 2), W("wm", 8 * m, 8 * m + 8), Op.mult)
     for h in range(2):
         scan(W("sc0", h, 16, 2), W("d0a"), W("sq0", h, 16, 2))
-    tt(W("gy0"), W("l0", 1, 16, 2), W("wm", 8, 16), Op.mult)
-    lost(0, 8, "wl", "jp0")
+    act(W("ga"), W("l0", 1, 16, 2), Act.Abs)
+    tt(W("gy0"), W("ga"), W("wm", 8, 16), Op.mult)
+    lost(0)
     count(0)
     w0 = listed(0)
     gather(0, w0)
     numbers(0, w0)
     if r in BUILD[0]:
-        buildlist(0)
+        buildlist(0, w0)
         build(0)
     built(0)
-    listrow(0, w0)
-    ts(W("key"), W("bi", 0, 64), 3 * 4096 + 255, Op.bitwise_and)
     mapped(0)
-    enter(0)
-    for e in range(8):
-        ts(W("oh", 64 * e, 64 * e + 64), W("key"), W("csf", e, e + 1), Op.is_equal)
-    for e in range(8):
-        total(W("rep", e, e + 1), W("oh", 64 * e, 64 * e + 64))
+    own(W("mg"), W("mp"), W("ko"))
+    scan(W("ms"), W("d0g", 0, 160), W("mg"), Op.add)
+    tt(W("o1f"), W("ms", 15, 128, 16), W("mrow", 0, 8), Op.max)
+    cp(W("o1"), W("o1f"))
     for h in range(2):
-        ts(W("oho", 64 * h, 64 * h + 64), W("key"), W("cso", h, h + 1), Op.is_equal)
-        tt(W("pm", 65 * h, 65 * h + 64), W("oho", 64 * h, 64 * h + 64), W("va", 0, 64), Op.mult)
-        red(W("src1", h, h + 1), W("pm", 65 * h, 65 * h + 65), Op.max)
-    ts(W("nrep"), W("rep"), -1.0, Op.mult, 1.0, Op.add)
+        cp(W("o2", 3 * h, 3 * h + 3), W("o1f", 4 * h + 1, 4 * h + 4))
+    placed(W("src1"), W("sra"), W("srb"), W("ms", 143, 160, 16), R1 - M0, i1)
     tt(W("jpb"), W("src1"), W("jp2"), Op.add)
     for h in range(2):
-        tt(W("prc", 260 * h + 64, 260 * h + 260, 65), W("kro", 2 * h, 16, 4), W("nrep", 4 * h, 4 * h + 4), Op.mult)
-        tt(W("prg", 195 * h + 64, 195 * h + 195, 65), W("kro", 4 + 2 * h + 1, 16, 4), W("nrep", 4 * h + 1, 4 * h + 4), Op.mult)
+        ts(W("wlb1", 3 * h, 3 * h + 3), W("wl1"), W("jpb", h, h + 1), Op.add)
 
     mm(0, "uc", 0, "tw", 320)
     mm(1, "ug", 0, "tw", 320)
-    for e in range(8):
-        tt(W("prc", 65 * e, 65 * e + 64), W("pa", 32, 96), W("oh", 64 * e, 64 * e + 64), Op.mult)
-        total(W("sqc", e, e + 1), W("prc", 65 * e, 65 * e + 65))
-    scan(W("sc1", 0, 8), W("d0b"), W("sqc"))
-    for e in range(6):
-        o = 64 * (4 * (e // 3) + e % 3 + 1)
-        tt(W("prg", 65 * e, 65 * e + 64), W("pa", 544, 608), W("oh", o, o + 64), Op.mult)
-        total(W("gq", e, e + 1), W("prg", 65 * e, 65 * e + 65))
-    act(W("ga1", 0, 6), W("gq"), Act.Abs)
-    lost(1, 6, "wl1", "jpb")
+    cp(W("winc", M0, M0 + 64), W("pa", 32, 96), "vs")
+    act(W("wing", M0, M0 + 64), W("pa", 544, 608), Act.Abs)
+    for h in range(2):
+        own(W("cg", 64 * h, 64 * h + 64), W("winc"), W("o1", 4 * h, 4 * h + 4))
+        scan(W("sc1", 64 * h, 64 * h + 64), W("d0c"), W("cg", 64 * h, 64 * h + 64))
+    own(W("gg"), W("wing"), W("o2"))
+    for h in range(2):
+        scan(W("gs", 48 * h, 48 * h + 48), W("one"), W("gg", 48 * h, 48 * h + 48), Op.max)
+    lost(1)
     count(1)
     w1 = listed(1)
     gather(1, w1)
     numbers(1, w1)
     if r in BUILD[1]:
-        buildlist(1)
+        buildlist(1, w1)
         build(1)
-    mapped(1)
     built(1)
     for x in ("", "_s"):
-        move("y", W("tx" + x, R1, R1 + 64), W("tw" + x, R1, R1 + 64), "dl_x" + x)
-    enter(1)
-    turn(W("ft"), W("fr", 0, 512))
-    cp(W("fou"), W("ft", 0, 512, 32))
-    listrow(1, w1)
-    for t in range(2):
-        stripes(t)
+        move("y", W("tx" + x, old, old + 64), W("tw" + x, R1, R1 + 64), "dl_x" + x)
+    products(0, "tw", 320, 32)
+    mapped(1)
+    tt(W("fm"), W("mp", 256 * r, 256 * r + 256), W("dg"), Op.mult)
+    scan(W("fn"), W("d0g"), W("fm"), Op.add)
+    placed(W("fc"), W("fa"), W("fb"), W("fn", 15, 256, 16), lift, W("kg"))
+    cp(W("fou"), W("fc"))
+    stripes(0, w0)
+    stripes(1, w1)
     store("y", lambda T: T.bs[:, :], W("bsf", 0, 256, 1, 0, 1), "dbs")
 
+    products(1, "tx", min(old, R2), 64 if before else 0)
     for c in range(2):
-        pick("ou", 128 * c, "tx", 672, "fou", 8 * c, 128)
-        for o in range(2):
-            mm(2 * c + o, "wq", 128 * o, "ou", 128 * c)
+        pick("ou", 128 * c, "tx", max(old, R2) + 64, "fou", 8 * c, 128)
 
     def scales(k):
-        store("y", lambda T: T.osc[4 * k:4 * k + 4, 0:256], W("ou_s", 0, 256, 1, 32 * k, 32 * k + 4), "doc")
+        store("ys"[k % 2], lambda T: T.osc[4 * k:4 * k + 4, 0:256], W("ou_s", 0, 256, 1, 32 * k, 32 * k + 4), ("doc", "dos")[k % 2])
 
-    def block(c, o):
-        a, b = 256 * o + 128 * c, 256 * o + 128 * c + 128
-        cp(W("ys", a, b), W("pa", 512 * (2 * c + o), 512 * (2 * c + o) + 128), "vs"[o])
-        store("ys"[o], lambda T: T.y[:, a:b], W("ys", a, b), "dy%d" % o)
+    def block(o):
+        store("ys"[o], lambda T: T.y[:, 256 * o:256 * o + 256], W("yb%d" % o, 256 * r, 256 * r + 256), "dy%d" % o, 200.0 - 200.0 * o)
 
-    store("y", lambda T: T.oc[:, 0:1024], W("ou"), "doc")
+    store("y", lambda T: T.oc[:, 0:1024], W("ou"), "doc", 100.0)
+    block(0)
     for k in range(4):
         scales(k)
-    for c in range(2):
-        for o in range(2):
-            block(c, o)
+    block(1)
     return nodes
 
 

@@ -1,14 +1,20 @@
 from concourse.bass import DstId, RemoteDMATransfer
-from concourse.mybir import dt, AluOpType as Op, AxisListType, ActivationFunctionType as Act
+from concourse.mybir import dt, AluOpType as Op, ActivationFunctionType as Act
 
 N, P, K = 4, 256, 64
 R1, R2 = 352, 608
-M0 = 96
+M0 = 128
 BUILD = ((0, 2), (1, 3))
-TINY = 2.0 ** -110
-BIG = 4096.0
+STEP = 1.5 * 2.0 ** -24
+TINY = 2.0 ** -100
+HUGE = 2.0 ** 90
 UNIT = 32768.0
-TUNE = dict(wake=150.0, fac=1.2, load=900.0, issue=60.0, rissue=250.0, hop=700.0, row=12.0, byte=0.06, tol=0.0, bias=20.0)
+TUNE = dict(wake=150.0, fac=1.2, load=900.0, issue=60.0, rissue=250.0, hop=700.0, row=12.0, byte=0.06, tol=0.0, bias=20.0, pe=1.3, gat=1.56)
+LEAN = {'0onb0.0.0': 6000, '0eb0.0.0': 5760, '0eq0.0.0': 5110, '0eq128.0.0': 5000, '0ng00.0.0': -380, '1xs64.0.0': -690, '1onb0.0.0': 180,
+        '1o20.0.0': -940, '1bsf0.0.0': 210, '1tw0.0.0': -110, '1d0c0.0.0': -390, '1kk8.0.0': -300, '0ko0.0.0': 260, '0sc336.0.0': 300,
+        '0c20.0.0': -130, '0row10.32.67': 300, '1yn64.0.0': 120, '0cm0128.0.0': -240, '0l02.0.0': -100, '1dv15.0.0': -540, '0wj00.0.0': -450,
+        '0rho1.0.0': 80, '0hm0.0.0': 390, '0row00.0.67': 60, '0rfo01.0.0': 230, '1row00.0.67': 220, '0bi0.0.0': -680, '1gx0.0.0': -20,
+        '0s20.0.0': -430, '0cg64.0.0': 120, '1fou0.0.0': 1260, '0bj64.0.0': 470, '0mm00.0.38': 650}
 
 F, B, I, U16, CODES = "float32", "bfloat16", "int32", "uint16", "float8_e4m3fn_x4"
 SCRATCH, LOG, _TOP = {}, {}, {}
@@ -20,10 +26,10 @@ def _own(dtype, **kw):
         LOG[n] = (n, 0, c, dtype)
 
 
-def _cube(**kw):
+def _cube(dtype, **kw):
     for n, (a, b) in kw.items():
-        SCRATCH[n] = ("sbuf", [128, a, b], F)
-        LOG[n] = (n, 0, a * b, F)
+        SCRATCH[n] = ("sbuf", [128, a, b], dtype)
+        LOG[n] = (n, 0, a * b, dtype)
 
 
 def _slab(slab, dtype, **kw):
@@ -34,7 +40,7 @@ def _slab(slab, dtype, **kw):
         SCRATCH[slab] = ("sbuf", [128, _TOP[slab]], dtype)
 
 
-_own(B, onb=512, tbt=1040, ut=512, wt=1024, eb=2048, ub0=512, ub1=512, h0=512, h1=512, mp=1024)
+_own(B, onb=516, tbt=1040, ut=512, wt=1024, eb=516, ub0=512, ub1=512, h0=512, h1=512, mp=1024)
 for _n, _c in dict(tq=256, tw=512, tx=768, uq=128, uc=128, ug=128, eq=512, wq=256, tz=256, sla=64, slb=64,
                    laa=128, lab=128, psa=128, psb=128, ou=256).items():
     _own(CODES, **{_n: _c})
@@ -42,23 +48,26 @@ for _n, _c in dict(tq=256, tw=512, tx=768, uq=128, uc=128, ug=128, eq=512, wq=25
 for _n in ("pa", "pu"):
     SCRATCH[_n] = ("psum", [128, 2048], F)
     LOG[_n] = (_n, 0, 2048, F)
-_own(F, l0=16, l1=16, xs=256, xd=128, yb0=1024, yb1=1024, winc=160, wing=160)
-_cube(row0=(4, 64), row1=(4, 64), kt=(4, 32), mm0=(4, 64), mm1=(4, 64))
-_slab("fs", F, jc=2, jp0=2, jp2=2, jpb=2, cf=12, rr=16, rh=8, wm=16, nq=4, ca=4, cb=4, c1=4, c2=4, c3=4, c4=4,
-      s1=4, s2=4, s3=4, s4=4, s5=4, wl=4, wlb0=8, wlb1=6, wa=3, wb=1, wc=1, wd=3, wl1=3, ma=12, mb=12, m0=16, rho=4, gm=40, mrow=32,
-      kf=16, kg=16, ofrf=4, d0a=8, kra=12, krb=12, kr0=16, kk=10, o1f=8, sra=2, srb=2, src1=2, cg=128, gg=96, gs=96,
-      fa=16, fb=16, fc=16, yn=256, lr=128, bsf=256, one=48, ga=8, gb=8, junk=4096)
-_slab("hs", B, i16=256, dg=256, d0g=256, d0c=64, va=64, vb=64, mg=160, ms=160, fm=256, fn=256)
+_own(F, l0=16, l1=16, l2=15, xs=256, xd=128, yb0=1024, yb1=1024, winc=192, wing=192, uf=8)
+_cube(F, row0=(4, 64), row1=(4, 64), kt=(4, 32), mm0=(4, 64), mm1=(4, 64))
+_cube(B, md=(16, 32))
+_slab("fs", F, jc=2, jp0=2, jp2=2, jpb=2, cf=12, rh=8, wm=16, ca=4, cb=4, c1=4, c2=4, c3=4, c4=4,
+      s1=4, s2=4, s4=4, s5=4, wl=4, wa=3, wb=1, wc=1, wd=3, wl1=3, mb=4, mk=64, rho=4, gm=40, mrow=32,
+      kf=16, kg=16, ofrf=4, kk=10, o1f=8, sra=2, srb=2, src1=2, cg=224, gg=96, gs=144,
+      fa=16, fb=16, fc=16, yn=256, lr=128, bsf=256, ga=12, r6=12, cq=12, cap=12, gy=12, d0m=12, gx=12,
+      sq=82, sc=448, d0c=97)
+_slab("hs", B, i16=160, dg=160, d0g=160, va=64, vb=64, mg=160, ms=160, fn=512)
 for _t in "01":
-    _slab("fs", F, **{n + _t: c for n, c in dict(sq=16, sc=128, ex=64, dl=2, th=80, cm=544, po=2, mt=256, lw=4, ab=4, ac=4,
-                                                 gx=2, gy=8, ge=8, gw=8, pay=2, er=64).items()})
+    _slab("fs", F, **{n + _t: c for n, c in dict(rw=64, sa=2, mx=2, th=80, mt=256, zz=256, ac=4, ng=10, dv=10, pay=10,
+                                                 er=64, po=128, pe=2).items()})
+    _slab("hs", B, **{n + _t: c for n, c in dict(cm=512, cj=256).items()})
     _slab("is_", I, **{n + _t: c for n, c in dict(wj=4, wk=2, rk=6, fi=4).items()})
     _slab("us", U16, **{n + _t: c for n, c in dict(off=4, rfo=6, ofs=4).items()})
-_slab("is_", I, bi=128, bk=64, bj=256, pi=4, ci=12, csi=8, csj=8, csk=8)
-_slab("us", U16, ofr=4, ofu=32, ofv=32, fou=16, ko=10, o1=8, o2=6)
+_slab("is_", I, bi=128, bk=64, bj=256, pi=4, ci=12, csi=8, csj=8, csk=8, dj=64, dk=64)
+_slab("us", U16, ofr=4, fou=16, ko=10, o1=8, o2=6, hm=8)
 
 SEMAPHORES = ["sv", "ss", "st", "sg", "dl_u", "dl_t0", "dl_t1", "dl_t2", "dl_w", "dl_z", "dl_x", "dl_x_s", "dl_m", "dl_m_s", "dl_n", "dl_n_s",
-              "dbs", "dy0", "dy1", "doc", "dos", "ls", "a0", "a1", "ha0", "ha1", "hb0", "hb1"]
+              "dl_p", "dl_p_s", "dl_k", "dl_k_s", "dbs", "dy0", "dy1", "doc", "dos", "ls", "a0", "a1", "ha0", "ha1", "hb0", "hb1"]
 _QS = {"v": "sv", "s": "ss", "t": "st", "g": "sg"}
 _PLANS = {}
 
@@ -97,7 +106,8 @@ def calls(r, cores, topo):
     cyc = 0.83 * TUNE["fac"]
 
     def node(rd, wr, fns, cost, sem=None, by=1, lag=0.0, after=(), to=(), cast=False):
-        nodes.append(dict(rd=rd, wr=wr, fns=fns, cost=cost, sem=sem, by=by, lag=lag, after=list(after), to=to, cast=cast, i=len(nodes)))
+        kind = 2 if len(rd) > 1 and rd[0][4] != rd[1][4] else 1 if rd else 0
+        nodes.append(dict(kind=kind, rd=rd, wr=wr, fns=fns, cost=cost, sem=sem, by=by, lag=lag, after=list(after), to=to, cast=cast, i=len(nodes)))
         return nodes[-1]
 
     def small(n, *ws):
@@ -114,11 +124,17 @@ def calls(r, cores, topo):
         n = width(out)
         b = W("dg", 0, n)
         return node([win, off, b], [out], {"v": lambda e: e["v"].tensor_tensor(e["ap"](out), e["ap"](win).indirect(e["ap"](off)), e["ap"](b), Op.mult)},
-                    {"v": (50 + 2 * 0.83 * n) * TUNE["fac"]})
+                    {"v": (50 + max(2, TUNE["gat"]) * 0.83 * n) * TUNE["fac"]})
+
+    def take(out, win, off, q):
+        n = TUNE["gat"] * 0.83 * width(out)
+        fns = {"v": lambda e: e["v"].tensor_copy(e["ap"](out), e["ap"](win).indirect(e["ap"](off))),
+               "s": lambda e: e["s"].activation(e["ap"](out), e["ap"](win).indirect(e["ap"](off)), Act.Copy)}
+        return node([win, off], [out], {x: fns[x] for x in q}, {x: (n + (50 if x == "v" else 65)) * TUNE["fac"] for x in q})
 
     def strew(win, off, src):
         node([off, src], [win], {"v": lambda e: e["v"].tensor_copy(e["ap"](win).indirect(e["ap"](off)), e["ap"](src))},
-             {"v": (50 + 3.5 * 0.83 * width(src)) * TUNE["fac"]})
+             {"v": (50 + TUNE["gat"] * 2.3 * 0.83 * width(src)) * TUNE["fac"]})
 
     def ts(out, a, s1, op0, s2=None, op1=None):
         rd = [a] + [s for s in (s1, s2) if isinstance(s, tuple)]
@@ -134,38 +150,33 @@ def calls(r, cores, topo):
         fns = {"v": lambda e: e["v"].tensor_copy(e["ap"](out), e["ap"](a)), "s": lambda e: e["s"].activation(e["ap"](out), e["ap"](a), Act.Copy)}
         return node([a], [out], {x: fns[x] for x in q}, {x: small(width(out)) for x in q})
 
-    def red(out, a, op):
-        return node([a], [out], {"v": lambda e: e["v"].tensor_reduce(e["ap"](out), e["ap"](a), AxisListType.X, op)}, {"v": small(width(a))})
-
-    def fill(out, c):
-        return node([], [out], {"v": lambda e: e["v"].memset(e["ap"](out), c)}, {"v": small(width(out), out)})
+    def fill(out, c, q="v"):
+        fns = {"v": lambda e: e["v"].memset(e["ap"](out), c),
+               "g": lambda e: e["g"].iota(e["ap"](out), [[0, width(out)]], int(c), 0, allow_small_or_imprecise_dtypes=True)}
+        return node([], [out], {x: fns[x] for x in q}, {x: small(width(out), out) if x == "v" else 130 * TUNE["fac"] + 2 * cyc * width(out) for x in q})
 
     def turn(out, a):
-        return node([a], [out], {"v": lambda e: e["v"].transpose(e["ap"](out), e["ap"](a))}, {"v": small(width(a))})
+        return node([a], [out], {"v": lambda e: e["v"].transpose(e["ap"](out), e["ap"](a))}, {"v": small(width(a), out, a)})
 
-    def scan(out, d0, d1, op=Op.subtract):
-        return node([d0, d1], [out], {"v": lambda e: e["v"].tensor_tensor_scan(e["ap"](out), e["ap"](d0), e["ap"](d1), 0.0, Op.mult, op)},
+    def scan(out, d0, d1, op=Op.subtract, op0=Op.mult, first=0.0):
+        col = isinstance(first, tuple)
+        return node([d0, d1] + [first] * col, [out],
+                    {"v": lambda e: e["v"].tensor_tensor_scan(e["ap"](out), e["ap"](d0), e["ap"](d1), e["ap"](first) if col else first, op0, op)},
                     {"v": small(width(out), out, d0, d1)})
 
     def spread(out, s):
-        a = W("one", 0, 32)
-        return node([a, s], [out], {"s": lambda e: e["s"].activation(e["ap"](out), e["ap"](a), Act.Abs, scale=e["ap"](s))}, {"s": small(width(out))})
+        a = W("onb", 0, width(out))
+        return node([a, s], [out], {"s": lambda e: e["s"].activation(e["ap"](out), e["ap"](a), Act.Copy, scale=e["ap"](s))}, {"s": small(width(out))})
 
     def act(out, a, f, off=None):
         rd = [a] + [w for w in (off,) if w is not None]
         n = width(out)
         return node(rd, [out], {"s": lambda e: e["s"].activation(e["ap"](out), e["ap"](a) if off is None else e["ap"](a).indirect(e["ap"](off)), f)},
-                    {"s": small(n) if off is None else (65 + 1.56 * 0.83 * n) * TUNE["fac"]})
+                    {"s": small(n) if off is None else (65 + TUNE["gat"] * 0.83 * n) * TUNE["fac"]})
 
-    junk = [0]
-
-    def total(out, a, q="vs"):
-        n = width(a)
-        j = W("junk", junk[0], junk[0] + n)
-        junk[0] += n
-        fns = {"v": lambda e: e["v"].tensor_reduce(e["ap"](out), e["ap"](a), AxisListType.X, Op.add),
-               "s": lambda e: e["s"].activation(e["ap"](j), e["ap"](a), Act.Copy, accum_out=e["ap"](out))}
-        return node([a], [out, j], {x: fns[x] for x in q}, {x: small(n) + (20 if x == "s" else 0) for x in q})
+    def total(out, a, spare):
+        return node([a], [out, spare], {"s": lambda e: e["s"].activation(e["ap"](spare), e["ap"](a), Act.Copy, accum_out=e["ap"](out))},
+                    {"s": small(width(a)) + 20})
 
     def iota(out, pattern, base=0, cm=0):
         kw = {} if LOG[out[0]][3] == I else {"allow_small_or_imprecise_dtypes": True}
@@ -179,12 +190,12 @@ def calls(r, cores, topo):
         rd = [W(lhs, l0, l0 + 128), W(lhs + "_s", l0, l0 + 128), W(rhs, r0, r0 + n), W(rhs + "_s", r0, r0 + n)]
         o = W("pu" if bank > 3 else "pa", 512 * (bank % 4), 512 * (bank % 4) + n)
         return node(rd, [o], {"t": lambda e: e["t"].matmul_mx(e["ap"](o), e["ap"](rd[0]), e["ap"](rd[1]), e["ap"](rd[2]), e["ap"](rd[3]), True, True)},
-                    {"t": 1.3 * (n + 16) * cyc})
+                    {"t": TUNE["pe"] * (n + 16) * cyc})
 
     def pick(dst, d0, src, width_, off, o0, n):
         o, a, f = W(dst, d0, d0 + n), W(src, 0, width_), W(off, o0, o0 + n // 16)
         node([a, f], [o], {"v": lambda e: e["v"].tensor_copy(e["ap"](o).bitcast(dt.uint32), e["ap"](a).bitcast(dt.uint32).indirect(e["ap"](f)))},
-             {"v": (50 + 1.56 * 0.83 * n) * TUNE["fac"]})
+             {"v": (50 + TUNE["gat"] * 0.83 * n) * TUNE["fac"]})
         act(W(dst + "_s", d0, d0 + n), W(src + "_s", 0, width_), Act.Copy, off=f)
 
     def raw(e, w):
@@ -193,8 +204,8 @@ def calls(r, cores, topo):
     def load(q, w, tensor, c0, c1, sem, first=()):
         return node(list(first), [w], {q: lambda e: e[q].dma_start(e["ap"](w), e["T"][tensor][:, c0:c1])}, {q: TUNE["issue"]}, sem, 16, TUNE["load"])
 
-    def move(q, out, a, sem):
-        return node([a], [out], {q: lambda e: e[q].dma_start(raw(e, out), raw(e, a))}, {q: TUNE["issue"]}, sem, 16, TUNE["load"])
+    def move(q, out, a, sem, first=()):
+        return node([a] + list(first), [out], {q: lambda e: e[q].dma_start(raw(e, out), raw(e, a))}, {q: TUNE["issue"]}, sem, 16, TUNE["load"])
 
     def store(q, dst, a, sem, more=0.0):
         return node([a], [], {q: lambda e: e[q].dma_start(dst(e["T"]), raw(e, a))}, {q: TUNE["issue"]}, sem, 16, TUNE["load"] + more)
@@ -235,19 +246,12 @@ def calls(r, cores, topo):
     iota(W("pi", 0, 2), [[1, 2]], 0, 1)
     iota(W("pi", 2, 4), [[128, 2]], r, 1)
     iota(W("jc"), [[128, 2]], 0, 1)
-    iota(W("rr"), [[1, 4], [0, 4]])
     iota(W("rh"), [[1, 4], [0, 2]])
     iota(W("mrow"), [[1, 32]])
     fill(W("ut", 8, 512), 0.0)
     fill(W("onb"), 1.0)
-    fill(W("one"), 1.0)
-
-    def unit(b):
-        o = W("eb", 512 * b, 512 * b + 512)
-        node([W("onb")], [o], {"g": lambda e: e["g"].affine_select(e["ap"](o), e["ap"](W("onb")), [[-8, 128], [-1, 4]], Op.is_equal, 0.0, b, 8)},
-             {"g": 170 * TUNE["fac"] + 1024 * cyc})
-    for b in range(4):
-        unit(b)
+    node([W("onb")], [W("eb")], {"g": lambda e: e["g"].affine_select(e["ap"](W("eb")), e["ap"](W("onb")), [[-1, 516]], Op.is_equal, 0.0, 3, 4)},
+         {"g": 170 * TUNE["fac"] + 1032 * cyc})
     iota(C("kt", 0, 4, 0, 32), [[16, 4], [0, 2], [1, 16]])
     iota(W("kf"), [[16, 16]])
     iota(W("ofrf"), [[2, 2], [0, 2]])
@@ -260,16 +264,23 @@ def calls(r, cores, topo):
     ts(W("ci", 6, 7), pp, 31, Op.bitwise_and)
     ts(W("ci", 7, 8), pp, 5, Op.arith_shift_right, 1, Op.bitwise_and)
     ts(W("ci", 8, 9), pp, 6, Op.arith_shift_right)
-    fill(W("d0a"), 1.0)
-    fill(W("d0a", 0, 1), 0.0)
-    fill(W("d0a", 4, 5), -1.0)
+    fill(W("d0c"), 1.0)
+    fill(W("d0c", 16, 17), -1.0, "g")
     cp(W("cf", 0, 9), W("ci", 0, 9))
     q0, q1, xf, gf, i1 = W("cf", 0, 1), W("cf", 1, 2), W("cf", 2, 3), W("cf", 3, 4), W("cf", 4, 6)
     ts(W("wm", 0, 8), W("rh"), q0, Op.is_equal)
     ts(W("wm", 8, 16), W("rh"), q0, Op.not_equal)
-    fill(W("gm", 2, 3), 1.0)
-    ts(W("gm", 0, 2), W("cf", 7, 9), -1.0, Op.mult, 1.0, Op.add)
-    ts(W("gm", 3, 35), W("mrow"), W("cf", 6, 7), Op.is_ge)
+    ts(W("gm", 0, 2), W("cf", 7, 9), -STEP, Op.mult, STEP, Op.add)
+    ts(W("gm", 2, 34), W("mrow"), W("cf", 6, 7), Op.is_ge, STEP, Op.mult)
+    fill(W("sq", 16, 80), 0.0, "g")
+    fill(W("sq", 80, 82), -TINY)
+    iota(W("r6"), [[0, 2], [1, 6]])
+    ts(W("cq"), W("r6"), q0, Op.is_equal, -2 * HUGE, Op.mult)
+    ts(W("cap"), W("cq"), HUGE, Op.add)
+    fill(W("cap", 4, 12, 6), 0.0, "g")
+    fill(W("ga"), HUGE)
+    fill(W("d0m"), 1.0, "g")
+    fill(W("d0m", 0, 12, 6), -1.0, "g")
 
     quant("uq", 0, "ut", 0, 128)
     quant("tq", 0, "tbt", 0, 128)
@@ -277,14 +288,14 @@ def calls(r, cores, topo):
     quant("tq", 128, "tbt", 512, 128)
     mm(1, "tq", 128, "uq", 0)
 
-    def mine(l, bank):
+    def mine(l, bank, sem):
         for h in range(2):
             o = 512 * (bank + h)
             cp(W(l, 4 * r + 2 * h, 4 * r + 2 * h + 2), W("pa", o, o + 2), "vs")
         v = W(l, 4 * r, 4 * r + 4)
-        send([(v, v, peers, alle)], "a" + l[1])
+        send([(v, v, peers, alle)], sem)
 
-    mine("l0", 0)
+    mine("l0", 0, "a0")
     lands("a0", 3 * len(alle), [W("l0", 4 * o, 4 * o + 4) for o in range(N) if o != r])
 
     if r:
@@ -292,12 +303,11 @@ def calls(r, cores, topo):
         quant("tz", 0, "tbt", 4 * r, 256)
         mm(2, "tz", 0, "uq", 0)
         mm(3, "tz", 128, "uq", 0)
-        mine("l1", 2)
+        mine("l1", 2, "a1")
     lands("a1", len(alle) * (3 if r == 0 else 2), [W("l1", 4 * o, 4 * o + 4) for o in range(1, N) if o != r])
 
     u1, u2, u3, uj = 4096 / UNIT, 4 / UNIT, 1 / UNIT, 16 / UNIT
     rk = W("mrow", 0, 4)
-    ts(W("nq"), rk, q0, Op.is_equal, BIG, Op.mult)
     ts(W("ca"), rk, q0, Op.min)
     ts(W("cb"), rk, q0, Op.max)
     ts(W("s4"), rk, u1, Op.mult, 3 * u3, Op.add)
@@ -307,51 +317,50 @@ def calls(r, cores, topo):
     ts(W("c4"), W("ca"), 2.0, Op.is_equal, 1.0, Op.add)
     tt(W("s1"), W("c1"), W("c2"), Op.mult)
     tt(W("s2"), W("c3"), W("c4"), Op.mult)
-    tt(W("s3"), W("s4"), W("nq"), Op.add)
     tt(W("s5"), W("s1"), W("s2"), Op.add)
-    tt(W("wl"), W("s5"), W("s3"), Op.add)
+    tt(W("wl"), W("s5"), W("s4"), Op.add)
     ts(W("jp0"), W("jc"), 1.0 + uj, Op.mult)
+    fill(W("dv0", 4, 6), 0.0, "g")
     for h in range(2):
-        ts(W("wlb0", 4 * h, 4 * h + 4), W("wl"), W("jp0", h, h + 1), Op.add)
+        tt(W("dv0", 6 * h, 6 * h + 3), W("wl", 0, 3), W("wl", 1, 4), Op.subtract)
+    ts(W("dv0", 3, 10, 6), W("jp0"), W("wl", 3, 4), Op.add)
 
-    ts(W("ofu"), W("mrow"), 0.0, Op.is_ge, q0, Op.mult)
-    ts(W("ofv"), W("ofu"), 4.0, Op.add)
-    ready = [quant("tw", 320, "tbt", 0, 128)]
-    act(W("ub0"), W("ut"), Act.Copy, off=W("ofu"))
-    act(W("ub1"), W("ut"), Act.Copy, off=W("ofv"))
+    cp(W("uf"), W("ut", 0, 8), "s")
+    for x in range(8):
+        spread(W("ub%d" % (x // 4), x % 4, 512, 4), W("uf", x, x + 1))
     before = r == BUILD[1][1]
     old = R2 - 64 if before else R2 + 64
     lift = old - M0
     iota(W("va"), [[1, 64]], M0)
     iota(W("vb"), [[1, 64]], R2 - lift)
-    iota(W("i16"), [[0, 16], [1, 16]])
+    iota(W("i16"), [[0, 10], [1, 16]])
     ts(W("dg"), W("i16"), xf, Op.is_equal)
     ts(W("d0g"), W("i16"), 0.0, Op.not_equal)
     ts(W("kg"), W("kf"), xf, Op.add)
     ts(W("ofr"), W("ofrf"), gf, Op.add)
     when = 0 if r in BUILD[0] else 1
-    quant("eq", 0, "eb", 0, 512)
-    quant(("psa", "psb")[when], 0, "tbt", 0, 128)
+    for b in range(4):
+        quant("eq", 128 * b, "eb", 3 - b, 128)
     cp(W(("h0", "h1")[when]), W("tbt", 0, 512), "vs")
     for x in ("", "_s"):
-        move("y", W("tw" + x, 0, 256), W("tq" + x), "dl_m" + x)
+        move("y", W(("psa", "psb")[when] + x, 96, 128), W("tq" + x, 0, 32), "dl_p" + x, [W("l0")])
+        move("y", W("tw" + x, 0, 256), W("tq" + x), "dl_m" + x, [W("l0")])
+        move("y", W("tw" + x, 288, 352), W("tq" + x, 0, 64), "dl_k" + x, [W("l0")])
     quant("uc", 0, "ub0", 0, 128)
     quant("ug", 0, "ub1", 0, 128)
     for a, b in ((0, 504), (504, 1008), (1008, 1024)):
         load("y", W("mp", a, b), "u", 8, 8 + b - a, "dl_z", [W("l0")])
     load("y", W("wt"), "w", 0, 1024, "dl_w", [W("l0")])
     for x in ("", "_s"):
-        move("y", W("tx" + x, 0, 256), W("tq" + x), "dl_n" + x)
+        move("y", W("tx" + x, 0, 256), W("tq" + x), "dl_n" + x, [W("l0")])
     quant("wq", 0, "wt", 0, 256)
     for o in range(2):
         mm(2 + o, "wq", 128 * o, "tq", 0, 256)
         cp(W("yb%d" % o, 256 * r, 256 * r + 256), W("pa", 512 * (2 + o), 512 * (2 + o) + 256), "s")
 
-    ts(W("ma"), W("rr", 0, 12), q1, Op.is_lt)
-    ts(W("mb"), W("rr", 0, 12), q1, Op.is_ge)
-    ts(W("m0"), W("rr"), q1, Op.is_equal)
-    cp(W("rho", 0, 1), q1)
-    tt(W("rho", 1, 4), W("rr", 0, 12, 4), W("mb", 0, 12, 4), Op.add)
+    ts(W("mb", 0, 3), W("mrow", 0, 3), q1, Op.is_ge)
+    cp(W("rho", 0, 1), q1, "vs")
+    tt(W("rho", 1, 4), W("mrow", 0, 3), W("mb", 0, 3), Op.add)
     r1, r2, r3 = W("rho", 1, 2), W("rho", 2, 3), W("rho", 3, 4)
     ts(W("wa"), W("rho", 1, 4), u1, Op.mult)
     ts(W("wb"), r1, u2, Op.mult)
@@ -360,8 +369,13 @@ def calls(r, cores, topo):
     ts(W("wd", 1, 3), W("wa", 1, 3), W("wb"), Op.add)
     ts(W("wl1", 0, 2), W("wd", 0, 2), W("wc"), Op.add)
     ts(W("wl1", 2, 3), r2, u3, Op.mult, W("wd", 2, 3), Op.add)
-    fill(W("d0c"), 1.0)
-    fill(W("d0c", 16, 17), -1.0)
+    fill(W("dv1", 3, 5), 0.0, "g")
+    for h in range(2):
+        tt(W("dv1", 5 * h, 5 * h + 2), W("wl1", 0, 2), W("wl1", 1, 3), Op.subtract)
+        fill(W("cg", 112 * h + 64, 112 * h + 96), 0.0, "g")
+    fill(W("cg", 96, 224, 112), -TINY)
+    fill(W("gs", 63, 144, 80), -1.0, "g")
+    fill(W("gs", 79, 80), 1.0, "g")
     for h in range(2):
         ts(W("csi", 4 * h, 4 * h + 4), W("rho"), 4097.0, Op.mult, W("jc", h, h + 1), Op.add)
     ts(W("csj"), W("csi"), 255, Op.bitwise_and)
@@ -370,80 +384,70 @@ def calls(r, cores, topo):
     ts(W("kk", 8, 10), i1, 256.0 * r, Op.add)
     cp(W("ko"), W("kk"))
     ts(W("jp2"), i1, uj, Op.mult)
-    fill(W("winc", 0, M0), 0.0)
-    fill(W("wing", 0, M0), 0.0)
-
-    cp(W("l1", 0, 4), W("l0", 0, 4), "vs")
-    tt(W("krb"), W("l1", 4, 16), W("mb"), Op.mult)
-    tt(W("kra"), W("l1", 0, 12), W("ma"), Op.mult)
-    tt(W("kr0"), W("l1"), W("m0"), Op.mult)
     for h in range(2):
-        tt(W("winc", 4 * h + 1, 4 * h + 4), W("kra", 2 * h, 12, 4), W("krb", 2 * h, 12, 4), Op.add)
-        tt(W("gb", 4 * h + 1, 4 * h + 4), W("kra", 2 * h + 1, 12, 4), W("krb", 2 * h + 1, 12, 4), Op.add)
-        act(W("wing", 4 * h + 1, 4 * h + 4), W("gb", 4 * h + 1, 4 * h + 4), Act.Abs)
-        total(W("winc", 4 * h, 4 * h + 1), W("kr0", 2 * h, 16, 4))
+        ts(W("hm", 4 * h, 4 * h + 4), W("rho"), 4.0, Op.mult, 2.0 * h, Op.add)
+    cp(W("l1", 0, 4), W("l0", 0, 4), "vs")
+    cp(W("l2"), W("l1", 1, 16), "s")
+    own(W("winc", 0, M0), W("l1"), W("hm"))
+    own(W("wing", 0, M0), W("l2"), W("hm"))
 
     def count(t):
         n = str(t)
-        rn, th, cm = "row" + n, "th" + n, "cm" + n
-        sa = [W("ex" + n, 32 * h, 32 * h + 1) for h in range(2)]
+        rw, rn, th, cm = "rw" + n, "row" + n, "th" + n, "cm" + n
+        at = 224 * t + 64
+        sa = [W("sa" + n, h, h + 1) for h in range(2)]
+        act(W("sa" + n), W("sc", at, at + 160, 112), Act.Abs)
+        act(W("mx" + n), W("sc", at + 32, at + 160, 112), Act.Abs)
         for h in range(2):
-            at = 64 * h + 63 if t else 14 + h
-            spread(W("ex" + n, 32 * h, 32 * h + 32), W("sc" + n, at, at + 1))
-        turn(C(rn, 0, 1, 0, 64), W("ex" + n))
-        ts(W("dl" + n), W("ex" + n, 0, 64, 32), 1.5 * 2.0 ** -24, Op.mult, TINY, Op.max)
-        for a in range(2):
-            cp(C(rn, 2, 3, 0, 64, 64 * a, 64 * a + 64), C(rn, 0, 1, 0, 64, 64 - 64 * a, 128 - 64 * a), "vs")
+            o = 112 * h + at
+            turn(W(rw, 32 * h, 32 * h + 32), W("sc", o, o + 32))
+        act(C(rn, 0, 1, 0, 64), W(rw), Act.Abs)
         for x in (1, 3):
             for a in range(4):
                 b = a ^ x
-                cp(C(rn, x, x + 1, 0, 64, 32 * a, 32 * a + 32), C(rn, 0, 1, 0, 64, 32 * b, 32 * b + 32), "vs" if x == 1 else "s")
+                act(C(rn, x, x + 1, 0, 64, 32 * a, 32 * a + 32), W(rw, 0, 64, 1, 32 * b, 32 * b + 32), Act.Abs)
+        for a in range(2):
+            cp(C(rn, 2, 3, 0, 64, 64 * a, 64 * a + 64), C(rn, 0, 1, 0, 64, 64 - 64 * a, 128 - 64 * a), "vs")
         for h in range(2):
-            ts(W(th, 40 * h, 40 * h + 35), W("gm", 0, 35), W("dl" + n, h, h + 1), Op.mult, sa[h], Op.add)
+            ts(W(th, 40 * h, 40 * h + 34), W("gm", 0, 34), W("mx" + n, h, h + 1), Op.mult, sa[h], Op.add)
         for h in range(2):
-            o = 272 * h
-            other = W(th, 2, 3) if h == 0 else sa[1]
-            ts(W(cm, o, o + 128), C(rn, 0, 4, 32 - 32 * h, 64 - 32 * h), other, Op.is_ge)
-            tt(W(cm, o + 200, o + 232), C(rn, 0, 1, 32 * h, 32 * h + 32), W(th, 40 * h + 3, 40 * h + 35), Op.is_ge)
-            ts(W(cm, o + 232, o + 264), C(rn, 1, 2, 32 * h, 32 * h + 32), W(th, 40 * h, 40 * h + 1), Op.is_ge)
-            ts(W(cm, o + 128, o + 192), C(rn, 2, 4, 32 * h, 32 * h + 32), W(th, 40 * h + 1, 40 * h + 2), Op.is_ge)
-            total(W(cm, o + 192, o + 193), W(cm, o + 200, o + 264))
-            total(W("po" + n, h, h + 1), W(cm, o, o + 193))
+            o = 256 * h
+            tt(W(cm, o, o + 32), C(rn, 0, 1, 32 * h, 32 * h + 32), W(th, 40 * h + 2, 40 * h + 34), Op.is_ge)
+            ts(W(cm, o + 32, o + 64), C(rn, 1, 2, 32 * h, 32 * h + 32), W(th, 40 * h, 40 * h + 1), Op.is_ge)
+            for x in (0, 2):
+                ts(W(cm, o + 64 + 32 * x, o + 128 + 32 * x), C(rn, x, x + 2, 32 - 32 * h, 64 - 32 * h), sa[h], (Op.is_gt, Op.is_ge)[h])
+            ts(W(cm, o + 192, o + 256), C(rn, 2, 4, 32 * h, 32 * h + 32), W(th, 40 * h + 1, 40 * h + 2), Op.is_ge)
+            near = W("pe" + n, h, h + 1)
+            total(near, W(cm, o, o + 128), W("cj" + n, 128 * h, 128 * h + 128))
+            scan(W("po" + n, 64 * h, 64 * h + 64), W(cm, o + 128, o + 192), W(cm, o + 192, o + 256), Op.add, Op.add, near)
 
     def listed(t):
-        m, mt, lw, b, c = [x + str(t) for x in ("mm", "mt", "lw", "ab", "ac")]
-        for y in (0, 2):
-            for h in range(2):
-                ts(C(m, y, y + 2, 32 * h, 32 * h + 32), C("kt", y, y + 2, 0, 32), W("po%d" % t, h, h + 1), Op.is_equal, W("pay%d" % t, h, h + 1), Op.mult)
+        m, mt, z, c, po, pay = [x + str(t) for x in ("mm", "mt", "zz", "ac", "po", "pay")]
+        for h in range(2):
+            at = (3 + 6 * h, 2 + 5 * h)[t]
+            for y in (0, 2):
+                ts(C(m, y, y + 2, 32 * h, 32 * h + 32), C("kt", y, y + 2, 0, 32), W(po, 64 * h + 63, 64 * h + 64), Op.is_equal, W(pay, at, at + 1), Op.mult)
         for y in range(4):
             turn(W(mt, 64 * y, 64 * y + 64), C(m, y, y + 1, 0, 64))
         for y in range(4):
-            total(W(lw, y, y + 1), W(mt, 64 * y, 64 * y + 64))
-        for k in range(4):
-            tt(W(b, 0, 4, 1, 32 * k, 32 * k + 32), W(lw, 0, 4, 1, 32 * k, 32 * k + 32), W(lw, 0, 4, 1, 32 * (k ^ 1), 32 * (k ^ 1) + 32), Op.add)
+            o = 64 * y
+            scan(W(z, o, o + 64, 1, 0, 64), W(mt, o, o + 64, 1, 0, 64), W(mt, o, o + 64, 1, 64, 128), Op.add, Op.add)
         for k in range(2):
-            tt(W(c, 0, 4, 1, 64 * k, 64 * k + 64), W(b, 0, 4, 1, 64 * k, 64 * k + 64), W(b, 0, 4, 1, 64 - 64 * k, 128 - 64 * k), Op.add)
+            tt(W(c, 0, 4, 1, 32 * k, 32 * k + 32), W(z, 63, 256, 64, 0, 32), W(z, 63, 256, 64, 32, 64), Op.add)
+        for k in range(2):
+            cp(W("off%d" % t, 0, 4, 1, 64 * k, 64 * k + 64), W(c, 0, 4, 1, 0, 64))
+        cp(W(c, 0, 4, 1, 64, 128), W(c, 0, 4, 1, 0, 64), "s")
         return W(c, 0, 4)
 
-    def lost(t):
-        k = 4 - t
-        s = str(t)
-        for h in range(2):
-            if t == 0:
-                size, top = W("gy0", h, 8, 2), W("gx0", h, h + 1)
-                red(top, size, Op.max)
-            else:
-                size, top = W("gs", 48 * h + 15, 48 * h + 48, 16), W("gs", 48 * h + 47, 48 * h + 48)
-            ts(W("ge" + s, k * h, k * h + k), size, top, Op.not_equal, BIG, Op.mult)
-        tt(W("gw" + s, 0, 2 * k), W("ge" + s, 0, 2 * k), W("wlb" + s), Op.add)
-        for h in range(2):
-            red(W("pay" + s, h, h + 1), W("gw" + s, k * h, k * h + k), Op.min)
+    def lost(t, later, sooner):
+        n, s = width(later), str(t)
+        tt(W("ng" + s, 0, n), later, sooner, Op.is_le)
+        scan(W("pay" + s, 0, n), W("dv" + s, 0, n), W("ng" + s, 0, n), Op.mult, Op.add)
 
-    def gather(t, lists):
+    def gather(t):
         n = "ab"[t]
         src, width_ = (("tq", 256), ("tw", 448))[t]
         off = "off%d" % t
-        cp(W(off), lists)
         sl, la = "sl" + n, "la" + n
         bs = BUILD[t]
         if r in bs:
@@ -452,7 +456,7 @@ def calls(r, cores, topo):
             pick(sl, 32 * o, src, width_, off, 2 * o, 32)
             to = cores[bs[o]]
             for s in ("", "_s"):
-                send([(W(sl + s, 32 * o, 32 * o + 32), W(la + s, 32 * r, 32 * r + 32), [to], topo.engines(core, to))], "ha%d" % t, ready)
+                send([(W(sl + s, 32 * o, 32 * o + 32), W(la + s, 32 * r, 32 * r + 32), [to], topo.engines(core, to))], "ha%d" % t)
             pick(la, 32 * r, src, width_, off, 2 * d, 32)
             cnt = 0
             for i in range(N):
@@ -463,7 +467,7 @@ def calls(r, cores, topo):
             pick(sl, 0, src, width_, off, 0, 64)
             for s in ("", "_s"):
                 send([(W(sl + s, 32 * d, 32 * d + 32), W(la + s, 32 * r, 32 * r + 32), [cores[bs[d]]], topo.engines(core, cores[bs[d]])[d::2])
-                      for d in range(2)], "ha%d" % t, ready)
+                      for d in range(2)], "ha%d" % t)
 
     def numbers(t, w):
         ts(W("wj%d" % t), w, UNIT, Op.mult)
@@ -527,57 +531,62 @@ def calls(r, cores, topo):
         s, o = str(t), 128 * t
         act(W("er" + s), w, Act.Copy, off=W("ofr"))
         turn(W("lr", 64 * t, 64 * t + 64), W("er" + s))
-        a = W("lr", 64 * t, 64 * t + 64, 1, 0, 1)
-        b = c = W("bi", 64 * t, 64 * t + 64, 1, 0, 1)
+        top = 1 if t else 128
+        a = W("lr", 64 * t, 64 * t + 64, 1, 0, top)
+        b = c = W("bi", 64 * t, 64 * t + 64, 1, 0, top)
         ts(b, a, UNIT, Op.mult)
         if t * r:
             c = W("bk", 0, 64, 1, 0, 1)
             ts(c, a, UNIT, Op.mult, 16.0 * (256 - r), Op.add)
-        ts(W("bj", o, o + 64, 1, 0, 1), c, 4, Op.arith_shift_right, 255, Op.bitwise_and)
-        ts(W("bj", o + 64, o + 128, 1, 0, 1), b, 12, Op.arith_shift_right, 3, Op.bitwise_and)
+        ts(W("bj", o, o + 64, 1, 0, top), c, 4, Op.arith_shift_right, 255, Op.bitwise_and)
+        ts(W("bj", o + 64, o + 128, 1, 0, top), b, 12, Op.arith_shift_right, 3, Op.bitwise_and)
         cp(W("bsf", o, o + 128, 1, 0, 1), W("bj", o, o + 128, 1, 0, 1))
 
     for m in range(2):
-        tt(W("sq0", 8 * m, 8 * m + 8), W("l0", 0, 16, 2), W("wm", 8 * m, 8 * m + 8), Op.mult)
+        tt(W("sq", 8 * m, 8 * m + 8), W("l0", 0, 16, 2), W("wm", 8 * m, 8 * m + 8), Op.mult)
     for h in range(2):
-        scan(W("sc0", h, 16, 2), W("d0a"), W("sq0", h, 16, 2))
-    act(W("ga"), W("l0", 1, 16, 2), Act.Abs)
-    tt(W("gy0"), W("ga"), W("wm", 8, 16), Op.mult)
-    lost(0)
+        scan(W("sc", 112 * h + 56, 112 * h + 97), W("d0c", 12, 53), W("sq", h, 82, 2))
+        act(W("ga", 6 * h, 6 * h + 4), W("l0", 2 * h + 1, 16, 4), Act.Abs)
+    tt(W("gy"), W("ga"), W("cap"), Op.min)
+    scan(W("gx"), W("d0m"), W("gy"), Op.max, Op.mult, HUGE)
+    lost(0, W("gx", 1, 11), W("gx", 0, 10))
     count(0)
     w0 = listed(0)
-    gather(0, w0)
+    gather(0)
     numbers(0, w0)
     if r in BUILD[0]:
         buildlist(0, w0)
         build(0)
     built(0)
     mapped(0)
+    stripes(0, w0)
+    tt(W("dj"), W("bj", 0, 64), W("bj", 64, 128), Op.subtract)
+    ts(W("dk"), W("dj"), 127, Op.bitwise_and)
+    ts(W("mk"), W("dk"), W("jc", 0, 1), Op.is_equal)
     own(W("mg"), W("mp"), W("ko"))
     scan(W("ms"), W("d0g", 0, 160), W("mg"), Op.add)
-    tt(W("o1f"), W("ms", 15, 128, 16), W("mrow", 0, 8), Op.max)
+    tt(W("o1f"), W("ms", 15, 128, 16), W("kg", 0, 8), Op.max)
     cp(W("o1"), W("o1f"))
     for h in range(2):
         cp(W("o2", 3 * h, 3 * h + 3), W("o1f", 4 * h + 1, 4 * h + 4))
     placed(W("src1"), W("sra"), W("srb"), W("ms", 143, 160, 16), R1 - M0, i1)
     tt(W("jpb"), W("src1"), W("jp2"), Op.add)
-    for h in range(2):
-        ts(W("wlb1", 3 * h, 3 * h + 3), W("wl1"), W("jpb", h, h + 1), Op.add)
+    ts(W("dv1", 2, 10, 5), W("jpb"), W("wl1", 2, 3), Op.add)
 
-    mm(0, "uc", 0, "tw", 320)
-    mm(1, "ug", 0, "tw", 320)
-    cp(W("winc", M0, M0 + 64), W("pa", 32, 96), "vs")
-    act(W("wing", M0, M0 + 64), W("pa", 544, 608), Act.Abs)
+    mm(0, "uc", 0, "tw", 288)
+    mm(1, "ug", 0, "tw", 288)
+    tt(W("winc", M0, M0 + 64), W("pa", 64, 128), W("mk"), Op.mult)
+    tt(W("wing", M0, M0 + 64), W("pa", 576, 640), W("mk"), Op.mult)
     for h in range(2):
-        own(W("cg", 64 * h, 64 * h + 64), W("winc"), W("o1", 4 * h, 4 * h + 4))
-        scan(W("sc1", 64 * h, 64 * h + 64), W("d0c"), W("cg", 64 * h, 64 * h + 64))
-    own(W("gg"), W("wing"), W("o2"))
+        take(W("cg", 112 * h, 112 * h + 64), W("winc"), W("o1", 4 * h, 4 * h + 4), "vs"[h])
+        scan(W("sc", 112 * h + 224, 112 * h + 321), W("d0c"), W("cg", 112 * h, 112 * h + 97))
+    act(W("gg"), W("wing"), Act.Abs, off=W("o2"))
     for h in range(2):
-        scan(W("gs", 48 * h, 48 * h + 48), W("one"), W("gg", 48 * h, 48 * h + 48), Op.max)
-    lost(1)
+        scan(W("gs", 80 * h, 80 * h + 48), W("d0c", 17, 65), W("gg", 48 * h, 48 * h + 48), Op.max)
+    lost(1, W("gs", 31, 144, 16), W("gs", 15, 128, 16))
     count(1)
     w1 = listed(1)
-    gather(1, w1)
+    gather(1)
     numbers(1, w1)
     if r in BUILD[1]:
         buildlist(1, w1)
@@ -585,13 +594,13 @@ def calls(r, cores, topo):
     built(1)
     for x in ("", "_s"):
         move("y", W("tx" + x, old, old + 64), W("tw" + x, R1, R1 + 64), "dl_x" + x)
-    products(0, "tw", 320, 32)
+    products(0, "tw", 288, 64)
     mapped(1)
-    tt(W("fm"), W("mp", 256 * r, 256 * r + 256), W("dg"), Op.mult)
-    scan(W("fn"), W("d0g"), W("fm"), Op.add)
-    placed(W("fc"), W("fa"), W("fb"), W("fn", 15, 256, 16), lift, W("kg"))
+    for x in (0, 16):
+        cp(C("md", 0, 16, x, x + 16), W("mp", 256 * r, 256 * r + 256), "s")
+    turn(W("fn"), C("md", 0, 16, 0, 32))
+    placed(W("fc"), W("fa"), W("fb"), W("fn", 0, 512, 32), lift, W("kg"))
     cp(W("fou"), W("fc"))
-    stripes(0, w0)
     stripes(1, w1)
     store("y", lambda T: T.bs[:, :], W("bsf", 0, 256, 1, 0, 1), "dbs")
 
@@ -613,8 +622,12 @@ def calls(r, cores, topo):
     return nodes
 
 
-def arrange(plans):
-    wake = TUNE["wake"]
+def tag(r, n):
+    w = (n["wr"] + n["rd"])[0]
+    return "%d%s%d.%d.%d" % (r % 2, w[0], w[1], w[4], sum(w[6]) if len(w) > 6 else 0)
+
+
+def graph(plans):
     flat, base = [], []
     for r, ns in enumerate(plans):
         base.append(len(flat))
@@ -648,6 +661,12 @@ def arrange(plans):
     for k, ps in enumerate(pred):
         for j in ps:
             succ[j].append(k)
+    return flat, pred, succ, [tag(r, n) for r, n in flat]
+
+
+def arrange(g, lean):
+    flat, pred, succ, tags = g
+    wake = TUNE["wake"]
 
     def after(j, k):
         return flat[j][1]["lag"] + (0.0 if "r" in flat[k][1]["fns"] else wake)
@@ -663,14 +682,15 @@ def arrange(plans):
             if not left[j]:
                 todo.append(j)
 
+    way = [x + lean.get(t, 0) for x, t in zip(way, tags)]
     count = [len(p) for p in pred]
-    when, free, ready, best, out = [0.0] * len(flat), {}, {}, {}, []
+    when, free, ready, best, out, cross = [0.0] * len(flat), {}, {}, {}, [], {}
 
     def choose(q):
         f = free.get(q, 0.0)
         top, at = None, 0.0
         for k in sorted(ready[q], key=lambda k: (-way[k], k)):
-            s = max(f, when[k])
+            s = max(f, when[k], cross.get(q, 0.0) if flat[k][1]["kind"] == 1 else 0.0)
             if top is None or (s < at and s + flat[k][1]["cost"][q[1]] <= at + TUNE["tol"]):
                 top, at = k, s
         best[q] = (at, top)
@@ -695,6 +715,8 @@ def arrange(plans):
         out.append((r, n, q[1]))
         end = at + n["cost"][q[1]]
         free[q] = end if q[1] != "r" else 0.0
+        if q[1] == "v" and n["kind"] == 2:
+            cross[q] = end + wake
         for x in n["fns"]:
             ready[(r, x)].discard(k)
             choose((r, x))
@@ -706,16 +728,7 @@ def arrange(plans):
     return out
 
 
-def rank_program(g, core, T, topo):
-    r = T.rank_of(core)
-    if r is None:
-        return
-    cores = list(T.cores)
-    if "order" not in _PLANS:
-        _PLANS["order"] = arrange([calls(i, cores, topo) for i in range(N)])
-    queue = {"v": g.vector, "s": g.scalar, "t": g.tensor, "g": g, "y": g.sync}
-    total, known, snap, log = {}, {q: {} for q in queue}, {}, {}
-
+def viewer(T):
     def ap(w):
         n, c0, c1, st, p0, p1 = w[:6]
         if len(w) > 6:
@@ -724,8 +737,19 @@ def rank_program(g, core, T, topo):
         n, at = LOG[n][:2]
         c0, c1 = c0 + at, c1 + at
         return T[n][p0:p1, c0:c1] if st == 1 else T[n][p0:p1, c0:c1:st]
+    return ap
 
-    env = dict(queue, T=T, ap=ap)
+
+def rank_program(g, core, T, topo):
+    r = T.rank_of(core)
+    if r is None:
+        return
+    cores = list(T.cores)
+    if "order" not in _PLANS:
+        _PLANS["order"] = arrange(graph([calls(i, cores, topo) for i in range(N)]), LEAN)
+    queue = {"v": g.vector, "s": g.scalar, "t": g.tensor, "g": g, "y": g.sync}
+    total, known, snap, log = {}, {q: {} for q in queue}, {}, {}
+    env = dict(queue, T=T, ap=viewer(T))
 
     def wait(q, tok):
         s, v = tok
@@ -737,7 +761,7 @@ def rank_program(g, core, T, topo):
             if known[q].get(a, 0) < b:
                 known[q][a] = b
 
-    tokens = {}
+    tokens, cross = {}, 0
     for rank, n, q in _PLANS["order"]:
         if rank != r:
             continue
@@ -752,10 +776,14 @@ def rank_program(g, core, T, topo):
             for a in n["after"]:
                 tok = tokens[a["i"]]
                 need[tok[0]] = max(need.get(tok[0], 0), tok[1])
+            if q == "v" and n["kind"] == 1 and cross:
+                need["sv"] = max(need.get("sv", 0), cross)
             for x in sorted(need):
                 wait(q, (x, need[x]))
             ins = n["fns"][q](env)
             total[s] = total.get(s, 0) + n["by"]
+            if q == "v" and n["kind"] == 2:
+                cross = total[s]
             if not n["cast"]:
                 ins.then_inc(T.sem[s], n["by"])
                 snap[(s, total[s])] = dict(known[q])

@@ -2,19 +2,20 @@ from concourse.bass import DstId, RemoteDMATransfer
 from concourse.mybir import dt, AluOpType as Op, ActivationFunctionType as Act
 
 N, P, K = 4, 256, 64
-R1, R2 = 352, 608
+R1, R2 = 352, 512
 M0 = 128
 BUILD = ((0, 2), (1, 3))
 STEP = 1.5 * 2.0 ** -24
 TINY = 2.0 ** -100
 HUGE = 2.0 ** 90
 UNIT = 32768.0
-TUNE = dict(wake=150.0, fac=1.2, load=900.0, issue=60.0, rissue=250.0, hop=700.0, row=12.0, byte=0.06, tol=0.0, bias=20.0, pe=1.3, gat=1.56)
-LEAN = {'0onb0.0.0': 6000, '0eb0.0.0': 5760, '0eq0.0.0': 5110, '0eq128.0.0': 5000, '0ng00.0.0': -380, '1xs64.0.0': -690, '1onb0.0.0': 180,
-        '1o20.0.0': -940, '1bsf0.0.0': 210, '1tw0.0.0': -110, '1d0c0.0.0': -390, '1kk8.0.0': -300, '0ko0.0.0': 260, '0sc336.0.0': 300,
-        '0c20.0.0': -130, '0row10.32.67': 300, '1yn64.0.0': 120, '0cm0128.0.0': -240, '0l02.0.0': -100, '1dv15.0.0': -540, '0wj00.0.0': -450,
-        '0rho1.0.0': 80, '0hm0.0.0': 390, '0row00.0.67': 60, '0rfo01.0.0': 230, '1row00.0.67': 220, '0bi0.0.0': -680, '1gx0.0.0': -20,
-        '0s20.0.0': -430, '0cg64.0.0': 120, '1fou0.0.0': 1260, '0bj64.0.0': 470, '0mm00.0.38': 650}
+TUNE = dict(wake=165.0, fac=1.25, load=800.0, issue=60.0, rissue=250.0, hop=500.0, row=15.0, byte=0.03, first=0.0, eng=15.0, tol=0.0, bias=20.0,
+            pe=1.3, gat=1.56)
+LEAN = {}
+ORDER = ['0002040c061a100o0y0u0m0q0s0w1o36141v1w5r3i3k1618321c1y0e20242y4g224t4e3m26281i3o383q2a0a1k3s3a3076341e3u2c4i3w3y5o4k6q1q5u5s081g521s3c6g6i3e74722e0g6k6m4u7g7i4y7k2g6o2m0i7w2s2i7u7y4m2k2o2q805w628i2u2w5c8k4a6s848682881m4w500k567m8a8e8m908q8o403g8c8g94927o8s8u8w7q9a4496988y7s684c9c9g9e669i9k12469m6c9o9q9s9u9w6e9ya06a42584o5aa2a4aa7aa6a848aqacaeamakauawascg78caagaib0ci4qckayccao7ccocmb2b4bmb6cs54cucebobq5ybeb8bubgba64bwbibsbcbkbyc1606uc2cycwc46yd06w70c6cqd27eda5ed4c8dedidgd8d65gdmdkdcdqdo5kdsdue6e4e8dweaegeceeeieseudyewfae0eoekeqemf0eyfcfef4fgf2f6fifke2f8fm5ifofsfqfu5mgyfwfyg0h1h4g2g4g6g8h7gagegcgggigkgugmhugohahcgqh2hwgshehghyhihki0i2h8hmhoi4hqi6hsgwi8ikimieibisioihiuiciqiwiiiyj6j2j0j4',
+         '0002040c061a0o0y0m0q0u0s0w101o141v1w1i5r3i16181c1y1k3k0a3m1q3o20081g3q242y38323s1s223u3a1e3c3w2630283y0g2a34363e5o6q5u4t2c5s521m6g6i74720k566k6m4c403g546o2e5w626s442g7g7i2m7k7m2s760i4w7w2i2k7u7y2o687o2q2u808i2w66508k4u7q848682884y128m5c908a8e7s6c4a8q8o8c8g94926e8s8u8w4m96989a8y489c9g9e9i9k469m9o9q9s9u9w9y0ea06a42a2a4a6a8aa60akacae78ao6u6yauagawai584o7a5aay4ib2b04eb64gb87c5e4k4qaqas5y64bcbabe6w70bg7ebobib45g5k5i5mambsbwbubmbkgyc0bybqc4h4h1c2c6c8ckcicmh7cacocucqcscwd6d8ccdadoced2cyd4d0dedcdqdsdidudgdkdydwcgdme0e2e6e4e8eaeceeegeiekemeoeseqeueweyfef0f2hafgfifkhufaf4f8hwf6hcfmfohyi0h2fchefqi2fshgi4h8gafugci6g2fwgei8gig4fyg6gggkhig0gmg8gpgqhkhmhogshqguhsgwiaimioigidiuiqijiwieisiyikj0j8j4j6j2',
+         '0002040c061a100o0y0m0q0u0s0w1o36141v1w5n3i16181c1y3k320e20242y4g224t4e3m26281i3o383q2a0a1k3s3a303u341e3w2c4i3y5k4k6m1q5q5o081g4y1s3c6c6e3e706y2e0g6g6i4u7c7e4w727g2g6k2m0i7s2s2i7q7u4m2k2o2q7w827y84805y5s8e2u2w581m0k527i868g4a6o8i8w8m8k90888a8c403g7k8y8s8o8q7m964492947o8u644c989a9c629e9g46129i9k689m9o9q9s6a9u9w6642544o9ya0a2a4a648ama8aaaiaqasao74c6agcc7656acawaece4qcgauc8akck78aycib0bib250cocabkbab4cqbm5ubqbcb660bsbebob8bgbubx6q5wbycucsc06ucw6s6wc2cmcy7ad65ad0c4dadedcd4d25cdidgd8dmdk5gdodqe2e0e4dseoeqdue6ece8eaeeesf6dwekegemeieuewf8faf0fceyf2fefgdyf4fi5efkfofmfq5igufsfufwgxh0fyg0g2g4h3g6gag8gegcgggqgihqgkh6h8gmhsgohahchuhwgyhehghyi0h4hihki2hmi4hogsi6iiikici9iqimifisiaioiuigiwj4j0iyj2',
+         '0002040c061a0o0y0m0q0u0s0w101o141v1w1i5r3i3k0a16181y1c1k3m1q3o20081g3q24322y383s1s223u3a1e303c283w263y0g2a34363e5o6q5u4t2c5s521m6g6i74720k566k6m4c403g546o2e5w626s442g7g7i2m7k7m2s760i4w7w2i2k7u7y2o687o2q2u808i2w66508k4u7q868288844y128m5c908a8e7s6c4a8q8o8c8g94926e8s8u8w4m96989a8y489c9g9e9i9k469m9o9q9s9u9w9y0ea06a42a2a4a6a8aa60akacae78ao6u6yauagawai584o7a5aay4ib2b04eb64gb87c5e4k4qaqas5y64bcbabe6w70bg7ebobib45g5k5i5mambsbwbmbkbuh0bqc0byc4h6h3c2c6c8ckcicmh9cacocucqcscwd6d8ccdadoced2cyd4d0dedcdqdsdidudgdkdwdycgdme0e2e6e4e8eaeceeegeiekemeoeseqeueweyfefgf0fahwf2hcf4fifkfmf8hyhefofqf6h4i2hgi0fcfsfuhii4gci6hafwgei8g4fyggiagkg6g0gmg8gihkg2gogagrgshmhohqguhsgwhugyicioiqiiifiwisiliyigiuj0imj2jaj6j4j8']
 
 F, B, I, U16, CODES = "float32", "bfloat16", "int32", "uint16", "float8_e4m3fn_x4"
 SCRATCH, LOG, _TOP = {}, {}, {}
@@ -40,36 +41,31 @@ def _slab(slab, dtype, **kw):
         SCRATCH[slab] = ("sbuf", [128, _TOP[slab]], dtype)
 
 
-_own(B, onb=516, tbt=1040, ut=512, wt=1024, eb=516, ub0=512, ub1=512, h0=512, h1=512, mp=1024)
-for _n, _c in dict(tq=256, tw=512, tx=768, uq=128, uc=128, ug=128, eq=512, wq=256, tz=256, sla=64, slb=64,
-                   laa=128, lab=128, psa=128, psb=128, ou=256).items():
+_own(B, ut=532, tbt=1024, wt=1024, eb=516, em=516, ub0=512, ub1=512, h0=512, h1=512, mp=1024)
+for _n, _c in dict(tq=672, uq=128, uc=128, ug=128, eq=512, wq=256, sla=64, slb=64, laa=128, lab=128, psa=192, psb=192, en=128, ou=256).items():
     _own(CODES, **{_n: _c})
     _own("uint8", **{_n + "_s": _c})
 for _n in ("pa", "pu"):
     SCRATCH[_n] = ("psum", [128, 2048], F)
     LOG[_n] = (_n, 0, 2048, F)
-_own(F, l0=16, l1=16, l2=15, xs=256, xd=128, yb0=1024, yb1=1024, winc=192, wing=192, uf=8)
-_cube(F, row0=(4, 64), row1=(4, 64), kt=(4, 32), mm0=(4, 64), mm1=(4, 64))
+_own(F, l0=328, l1=32, l2=8, l3=8, xs=256, xd=128, yb0=1024, yb1=1024, winc=192, wing=192, uf=8)
+_cube(F, row0=(4, 64), row1=(4, 64), kt=(4, 32), mm0=(4, 64), mm1=(4, 64), sc=(4, 112))
 _cube(B, md=(16, 32))
-_slab("fs", F, jc=2, jp0=2, jp2=2, jpb=2, cf=12, rh=8, wm=16, ca=4, cb=4, c1=4, c2=4, c3=4, c4=4,
-      s1=4, s2=4, s4=4, s5=4, wl=4, wa=3, wb=1, wc=1, wd=3, wl1=3, mb=4, mk=64, rho=4, gm=40, mrow=32,
-      kf=16, kg=16, ofrf=4, kk=10, o1f=8, sra=2, srb=2, src1=2, cg=224, gg=96, gs=144,
-      fa=16, fb=16, fc=16, yn=256, lr=128, bsf=256, ga=12, r6=12, cq=12, cap=12, gy=12, d0m=12, gx=12,
-      sq=82, sc=448, d0c=97)
+_slab("fs", F, jc=2, jp0=2, jp2=2, jp3=2, cf=12, wm=4, ca=1, cb=1, c1=1, c0=1, none=1, minus=1, wa=2, wb=1, wl1=1, i1m=2, kgm=16,
+      mb=4, mk=64, rho=4, gm=40, mrow=32, kf=16, kg=16, ofrf=4, kk=10, o1f=8, src1=2, cg=224, gg=96, gs=144,
+      fa=16, fb=16, fc=16, yn=256, lr=128, bsf=256, ga=12, d0m=12, gx=12, d0c=97)
 _slab("hs", B, i16=160, dg=160, d0g=160, va=64, vb=64, mg=160, ms=160, fn=512)
 for _t in "01":
-    _slab("fs", F, **{n + _t: c for n, c in dict(rw=64, sa=2, mx=2, th=80, mt=256, zz=256, ac=4, ng=10, dv=10, pay=10,
-                                                 er=64, po=128, pe=2).items()})
+    _slab("fs", F, **{n + _t: c for n, c in dict(rw=64, sa=4, th=80, mt=256, zz=256, ac=4, ng=10, dv=10, pay=10, er=64, po=128, pe=2).items()})
     _slab("hs", B, **{n + _t: c for n, c in dict(cm=512, cj=256).items()})
     _slab("is_", I, **{n + _t: c for n, c in dict(wj=4, wk=2, rk=6, fi=4).items()})
     _slab("us", U16, **{n + _t: c for n, c in dict(off=4, rfo=6, ofs=4).items()})
 _slab("is_", I, bi=128, bk=64, bj=256, pi=4, ci=12, csi=8, csj=8, csk=8, dj=64, dk=64)
 _slab("us", U16, ofr=4, fou=16, ko=10, o1=8, o2=6, hm=8)
 
-SEMAPHORES = ["sv", "ss", "st", "sg", "dl_u", "dl_t0", "dl_t1", "dl_t2", "dl_w", "dl_z", "dl_x", "dl_x_s", "dl_m", "dl_m_s", "dl_n", "dl_n_s",
-              "dl_p", "dl_p_s", "dl_k", "dl_k_s", "dbs", "dy0", "dy1", "doc", "dos", "ls", "a0", "a1", "ha0", "ha1", "hb0", "hb1"]
+SEMAPHORES = ["sv", "ss", "st", "sg", "dl_u", "dl_t0", "dl_w", "dl_l", "dl_p", "dl_p_s", "dl_k", "dl_k_s", "dbs", "dy0", "dy1", "doc", "dos",
+              "ls", "a0", "ha0", "ha1", "hb0", "hb1"]
 _QS = {"v": "sv", "s": "ss", "t": "st", "g": "sg"}
-_PLANS = {}
 
 
 def W(name, c0=0, c1=None, step=1, p0=0, p1=128):
@@ -105,9 +101,9 @@ def calls(r, cores, topo):
     nodes = []
     cyc = 0.83 * TUNE["fac"]
 
-    def node(rd, wr, fns, cost, sem=None, by=1, lag=0.0, after=(), to=(), cast=False):
+    def node(rd, wr, fns, cost, sem=None, by=1, lag=0.0, to=(), cast=False, busy=0.0):
         kind = 2 if len(rd) > 1 and rd[0][4] != rd[1][4] else 1 if rd else 0
-        nodes.append(dict(kind=kind, rd=rd, wr=wr, fns=fns, cost=cost, sem=sem, by=by, lag=lag, after=list(after), to=to, cast=cast, i=len(nodes)))
+        nodes.append(dict(kind=kind, busy=busy, rd=rd, wr=wr, fns=fns, cost=cost, sem=sem, by=by, lag=lag, to=to, cast=cast, i=len(nodes)))
         return nodes[-1]
 
     def small(n, *ws):
@@ -165,7 +161,7 @@ def calls(r, cores, topo):
                     {"v": small(width(out), out, d0, d1)})
 
     def spread(out, s):
-        a = W("onb", 0, width(out))
+        a = W("ut", 16, 16 + width(out))
         return node([a, s], [out], {"s": lambda e: e["s"].activation(e["ap"](out), e["ap"](a), Act.Copy, scale=e["ap"](s))}, {"s": small(width(out))})
 
     def act(out, a, f, off=None):
@@ -186,10 +182,11 @@ def calls(r, cores, topo):
         q, s, x = W(name, c0, c0 + n), W(name + "_s", c0, c0 + n), W(src, s0, s0 + 4 * n)
         return node([x], [q, s], {"v": lambda e: e["v"].quantize_mx(e["ap"](q), e["ap"](s), e["ap"](x))}, {"v": (12 + 0.88 * n) * TUNE["fac"]})
 
-    def mm(bank, lhs, l0, rhs, r0, n=128):
+    def mm(bank, lhs, l0, rhs, r0, n=128, start=True, stop=True):
         rd = [W(lhs, l0, l0 + 128), W(lhs + "_s", l0, l0 + 128), W(rhs, r0, r0 + n), W(rhs + "_s", r0, r0 + n)]
         o = W("pu" if bank > 3 else "pa", 512 * (bank % 4), 512 * (bank % 4) + n)
-        return node(rd, [o], {"t": lambda e: e["t"].matmul_mx(e["ap"](o), e["ap"](rd[0]), e["ap"](rd[1]), e["ap"](rd[2]), e["ap"](rd[3]), True, True)},
+        return node(rd, [o] if start or stop else [],
+                    {"t": lambda e: e["t"].matmul_mx(e["ap"](o), e["ap"](rd[0]), e["ap"](rd[1]), e["ap"](rd[2]), e["ap"](rd[3]), start, stop)},
                     {"t": TUNE["pe"] * (n + 16) * cyc})
 
     def pick(dst, d0, src, width_, off, o0, n):
@@ -201,16 +198,22 @@ def calls(r, cores, topo):
     def raw(e, w):
         return e["ap"](w).bitcast(dt.uint8) if LOG[w[0]][3] == CODES else e["ap"](w)
 
+    def rows(w, n=1.0):
+        return n * max(1, (w[5] - w[4]) // 16) * (TUNE["row"] + TUNE["byte"] * width(w) * {F: 4, CODES: 4, B: 2}.get(LOG[w[0]][3], 1))
+
     def load(q, w, tensor, c0, c1, sem, first=()):
-        return node(list(first), [w], {q: lambda e: e[q].dma_start(e["ap"](w), e["T"][tensor][:, c0:c1])}, {q: TUNE["issue"]}, sem, 16, TUNE["load"])
+        return node(list(first), [w], {q: lambda e: e[q].dma_start(e["ap"](w), e["T"][tensor][:, c0:c1])}, {q: TUNE["issue"]}, sem, 16, TUNE["load"],
+                    busy=rows(w))
 
-    def move(q, out, a, sem, first=()):
-        return node([a] + list(first), [out], {q: lambda e: e[q].dma_start(raw(e, out), raw(e, a))}, {q: TUNE["issue"]}, sem, 16, TUNE["load"])
+    def move(q, out, a, sem, first):
+        return node([a, first], [out], {q: lambda e: e[q].dma_start(raw(e, out), raw(e, a))}, {q: TUNE["issue"]}, sem, 16, TUNE["load"], busy=rows(a))
 
-    def store(q, dst, a, sem, more=0.0):
-        return node([a], [], {q: lambda e: e[q].dma_start(dst(e["T"]), raw(e, a))}, {q: TUNE["issue"]}, sem, 16, TUNE["load"] + more)
+    def store(q, dst, a, sem, first=()):
+        return node([a] + list(first), [], {q: lambda e: e[q].dma_start(dst(e["T"]), raw(e, a))}, {q: TUNE["issue"]}, sem, 16, TUNE["load"],
+                    busy=rows(a))
 
     peers = [c for c in cores if c != core]
+    used = set()
 
     def mask(engs):
         m = 0
@@ -218,7 +221,7 @@ def calls(r, cores, topo):
             m |= 1 << e
         return m
 
-    def send(parts, sem, after=()):
+    def send(parts, sem):
         def did(c):
             a = topo.addr(c)
             return DstId(rid=a[0], pnc=a[1])
@@ -227,30 +230,27 @@ def calls(r, cores, topo):
             return e["g"].remote_dma_fused([RemoteDMATransfer(dst_ids=[did(c) for c in cs], dma_engine_mask=mask(es), remote_sem=e["T"].sem[sem],
                                                               srcs=[raw(e, a)], dsts=[raw(e, b)] * len(cs)) for a, b, cs, es in parts],
                                            local_sem=e["T"].sem["ls"])
-        lag = 0.0
-        for a, b, cs, es in parts:
-            row = width(a) * {F: 4, CODES: 4}.get(LOG[a[0]][3], 1)
-            lag = max(lag, TUNE["hop"] + 128 // len(es) * len(cs) * (TUNE["row"] + row * TUNE["byte"]))
-        return node([p[0] for p in parts], [], {"g": f}, {"g": TUNE["rissue"]}, "ls", sum(len(p[3]) for p in parts), lag, after,
-                    [(cores.index(c), sem) for p in parts for c in p[2]], True)
+        new = {x for p in parts for x in p[3]} - used
+        used.update(new)
+        return node([p[0] for p in parts], [], {"g": f}, {"g": TUNE["rissue"]}, "ls", sum(len(p[3]) for p in parts),
+                    TUNE["hop"] + TUNE["first"] * (sem == "a0") + TUNE["eng"] * len(new),
+                    [(cores.index(c), sem) for p in parts for c in p[2]], True, max(rows(a, 16 / len(es) * len(cs)) for a, b, cs, es in parts))
 
     def lands(sem, count, views):
         return node([], views, {"r": None}, {"r": 0.0}, sem, count)
 
     alle = topo.engines(core, peers[0])
 
-    load("y", W("ut", 0, 8), "u", 0, 8, "dl_u")
-    load("y", W("tbt", 0, 512), "tb", 0, 512, "dl_t0")
-    load("s", W("tbt", 512, 1024), "tb", 512, 1024, "dl_t1")
+    load("y", W("ut", 4, 12), "u", 0, 8, "dl_u")
+    load("s", W("tbt"), "tb", 0, 1024, "dl_t0")
 
     iota(W("pi", 0, 2), [[1, 2]], 0, 1)
     iota(W("pi", 2, 4), [[128, 2]], r, 1)
     iota(W("jc"), [[128, 2]], 0, 1)
-    iota(W("rh"), [[1, 4], [0, 2]])
     iota(W("mrow"), [[1, 32]])
-    fill(W("ut", 8, 512), 0.0)
-    fill(W("onb"), 1.0)
-    node([W("onb")], [W("eb")], {"g": lambda e: e["g"].affine_select(e["ap"](W("eb")), e["ap"](W("onb")), [[-1, 516]], Op.is_equal, 0.0, 3, 4)},
+    ones = W("ut", 16, 532)
+    fill(ones, 1.0)
+    node([ones], [W("eb")], {"g": lambda e: e["g"].affine_select(e["ap"](W("eb")), e["ap"](ones), [[-1, 516]], Op.is_equal, 0.0, 3, 4)},
          {"g": 170 * TUNE["fac"] + 1032 * cyc})
     iota(C("kt", 0, 4, 0, 32), [[16, 4], [0, 2], [1, 16]])
     iota(W("kf"), [[16, 16]])
@@ -268,71 +268,58 @@ def calls(r, cores, topo):
     fill(W("d0c", 16, 17), -1.0, "g")
     cp(W("cf", 0, 9), W("ci", 0, 9))
     q0, q1, xf, gf, i1 = W("cf", 0, 1), W("cf", 1, 2), W("cf", 2, 3), W("cf", 3, 4), W("cf", 4, 6)
-    ts(W("wm", 0, 8), W("rh"), q0, Op.is_equal)
-    ts(W("wm", 8, 16), W("rh"), q0, Op.not_equal)
+    two = W("d0c", 0, 2)
+    ts(W("wm", 0, 1), q0, float(r), Op.is_equal)
+    ts(W("wm", 1, 3), two, q0, Op.mult, float(r), Op.not_equal)
+    fill(W("wm", 3, 4), 1.0, "g")
     ts(W("gm", 0, 2), W("cf", 7, 9), -STEP, Op.mult, STEP, Op.add)
     ts(W("gm", 2, 34), W("mrow"), W("cf", 6, 7), Op.is_ge, STEP, Op.mult)
-    fill(W("sq", 16, 80), 0.0, "g")
-    fill(W("sq", 80, 82), -TINY)
-    iota(W("r6"), [[0, 2], [1, 6]])
-    ts(W("cq"), W("r6"), q0, Op.is_equal, -2 * HUGE, Op.mult)
-    ts(W("cap"), W("cq"), HUGE, Op.add)
-    fill(W("cap", 4, 12, 6), 0.0, "g")
-    fill(W("ga"), HUGE)
+    fill(W("l0", 0, 16), 0.0, "g")
+    fill(W("l0", 48, 328), 0.0, "g")
+    fill(W("l0", 305, 312, 4), -TINY)
+    fill(W("ga", 4, 12, 6), 0.0, "g")
+    fill(W("ga", 5, 12, 6), HUGE)
     fill(W("d0m"), 1.0, "g")
     fill(W("d0m", 0, 12, 6), -1.0, "g")
 
+    for x in (0, 12):
+        cp(W("ut", x, x + 4), W("ut", 4 + x // 3, 8 + x // 3), "vs")
     quant("uq", 0, "ut", 0, 128)
     quant("tq", 0, "tbt", 0, 128)
     mm(0, "tq", 0, "uq", 0)
     quant("tq", 128, "tbt", 512, 128)
     mm(1, "tq", 128, "uq", 0)
 
-    def mine(l, bank, sem):
+    mine = W("l0", 16 + 8 * r, 24 + 8 * r)
+    for h in range(2):
+        tt(W("l0", mine[1] + 4 * h, mine[1] + 4 * h + 4), W("pa", 512 * h, 512 * h + 4), W("wm"), Op.mult)
+    send([(mine, mine, peers, alle)], "a0")
+    lands("a0", 3 * len(alle), [W("l0", 16 + 8 * o, 24 + 8 * o) for o in range(N) if o != r])
+    landed = W("l0", 16, 48)
+
+    for o in range(1, N):
+        at = 16 + 8 * o
+        move("y", W("l1", 8 * o, 8 * o + 8, 1, 0, 128 - o), W("l0", at, at + 8, 1, o, 128), "dl_l", landed)
         for h in range(2):
-            o = 512 * (bank + h)
-            cp(W(l, 4 * r + 2 * h, 4 * r + 2 * h + 2), W("pa", o, o + 2), "vs")
-        v = W(l, 4 * r, 4 * r + 4)
-        send([(v, v, peers, alle)], sem)
-
-    mine("l0", 0, "a0")
-    lands("a0", 3 * len(alle), [W("l0", 4 * o, 4 * o + 4) for o in range(N) if o != r])
-
-    if r:
-        load("y", W("tbt", 1024, 1040), "tb", 0, 16, "dl_t2")
-        quant("tz", 0, "tbt", 4 * r, 256)
-        mm(2, "tz", 0, "uq", 0)
-        mm(3, "tz", 128, "uq", 0)
-        mine("l1", 2, "a1")
-    lands("a1", len(alle) * (3 if r == 0 else 2), [W("l1", 4 * o, 4 * o + 4) for o in range(1, N) if o != r])
+            move("y", W("l1", 8 * o + 4 * h, 8 * o + 4 * h + 4, 1, 128 - o, 128), W("l0", at + 4 - 4 * h, at + 8 - 4 * h, 1, 0, o), "dl_l", landed)
 
     u1, u2, u3, uj = 4096 / UNIT, 4 / UNIT, 1 / UNIT, 16 / UNIT
-    rk = W("mrow", 0, 4)
-    ts(W("ca"), rk, q0, Op.min)
-    ts(W("cb"), rk, q0, Op.max)
-    ts(W("s4"), rk, u1, Op.mult, 3 * u3, Op.add)
-    ts(W("c1"), W("ca"), 0.0, Op.is_equal, u2, Op.mult)
-    ts(W("c2"), W("cb"), 1.0, Op.is_equal, 1.0, Op.add)
-    ts(W("c3"), W("cb"), 3.0, Op.is_equal, -u3, Op.mult)
-    ts(W("c4"), W("ca"), 2.0, Op.is_equal, 1.0, Op.add)
-    tt(W("s1"), W("c1"), W("c2"), Op.mult)
-    tt(W("s2"), W("c3"), W("c4"), Op.mult)
-    tt(W("s5"), W("s1"), W("s2"), Op.add)
-    tt(W("wl"), W("s5"), W("s4"), Op.add)
-    ts(W("jp0"), W("jc"), 1.0 + uj, Op.mult)
+    ts(W("c0"), q0, 0.0, Op.not_equal, u2 - u1, Op.mult)
+    ts(W("dv0", 0, 10, 6), two, W("c0"), Op.mult)
+    ts(W("c1"), q0, 2.0, Op.is_ge, u3 - u2, Op.mult)
+    ts(W("dv0", 1, 10, 6), two, u2 - u1, Op.mult, W("c1"), Op.add)
+    fill(W("dv0", 2, 10, 6), u3 - u1)
+    ts(W("ca"), q0, 0.0, Op.is_equal, 3 * u3, Op.mult)
+    ts(W("cb"), q0, -u3, Op.mult)
+    ts(W("jp0"), W("jc"), 1.0 + uj, Op.mult, 3 * u1 + 3 * u3, Op.add)
+    ts(W("dv0", 3, 10, 6), W("jp0"), W("ca"), Op.add, W("cb"), Op.add)
     fill(W("dv0", 4, 6), 0.0, "g")
-    for h in range(2):
-        tt(W("dv0", 6 * h, 6 * h + 3), W("wl", 0, 3), W("wl", 1, 4), Op.subtract)
-    ts(W("dv0", 3, 10, 6), W("jp0"), W("wl", 3, 4), Op.add)
 
-    cp(W("uf"), W("ut", 0, 8), "s")
+    cp(W("uf"), W("ut", 4, 12), "s")
     for x in range(8):
         spread(W("ub%d" % (x // 4), x % 4, 512, 4), W("uf", x, x + 1))
-    before = r == BUILD[1][1]
-    old = R2 - 64 if before else R2 + 64
-    lift = old - M0
     iota(W("va"), [[1, 64]], M0)
-    iota(W("vb"), [[1, 64]], R2 - lift)
+    iota(W("vb"), [[1, 64]], M0 + 64)
     iota(W("i16"), [[0, 10], [1, 16]])
     ts(W("dg"), W("i16"), xf, Op.is_equal)
     ts(W("d0g"), W("i16"), 0.0, Op.not_equal)
@@ -341,18 +328,23 @@ def calls(r, cores, topo):
     when = 0 if r in BUILD[0] else 1
     for b in range(4):
         quant("eq", 128 * b, "eb", 3 - b, 128)
+    fill(W("minus"), -1.0, "g")
+    node([W("eb"), W("minus")], [W("em")], {"s": lambda e: e["s"].activation(e["ap"](W("em")), e["ap"](W("eb")), Act.Copy, scale=e["ap"](W("minus")))},
+         {"s": small(516)})
+    quant("en", 0, "em", 0, 128)
     cp(W(("h0", "h1")[when]), W("tbt", 0, 512), "vs")
+    side = [0 if r == BUILD[t][1] else 64 for t in range(2)]
     for x in ("", "_s"):
-        move("y", W(("psa", "psb")[when] + x, 96, 128), W("tq" + x, 0, 32), "dl_p" + x, [W("l0")])
-        move("y", W("tw" + x, 0, 256), W("tq" + x), "dl_m" + x, [W("l0")])
-        move("y", W("tw" + x, 288, 352), W("tq" + x, 0, 64), "dl_k" + x, [W("l0")])
+        move("y", W(("psa", "psb")[when] + x, 96, 192), W("uq" + x, 0, 96), "dl_p" + x, landed)
+        if when or r == BUILD[0][0]:
+            c = (R2, R1)[when]
+            move("y", W("tq" + x, c - 64, c), W("uq" + x, 0, 64), "dl_k" + x, landed)
     quant("uc", 0, "ub0", 0, 128)
     quant("ug", 0, "ub1", 0, 128)
-    for a, b in ((0, 504), (504, 1008), (1008, 1024)):
-        load("y", W("mp", a, b), "u", 8, 8 + b - a, "dl_z", [W("l0")])
-    load("y", W("wt"), "w", 0, 1024, "dl_w", [W("l0")])
-    for x in ("", "_s"):
-        move("y", W("tx" + x, 0, 256), W("tq" + x), "dl_n" + x, [W("l0")])
+    fill(W("none"), -256.0, "g")
+    for a in (0, 512):
+        spread(W("mp", a, a + 512), W("none"))
+    load("y", W("wt"), "w", 0, 1024, "dl_w", [landed])
     quant("wq", 0, "wt", 0, 256)
     for o in range(2):
         mm(2 + o, "wq", 128 * o, "tq", 0, 256)
@@ -362,16 +354,13 @@ def calls(r, cores, topo):
     cp(W("rho", 0, 1), q1, "vs")
     tt(W("rho", 1, 4), W("mrow", 0, 3), W("mb", 0, 3), Op.add)
     r1, r2, r3 = W("rho", 1, 2), W("rho", 2, 3), W("rho", 3, 4)
-    ts(W("wa"), W("rho", 1, 4), u1, Op.mult)
-    ts(W("wb"), r1, u2, Op.mult)
-    ts(W("wc"), r3, u3, Op.mult)
-    ts(W("wd", 0, 1), r2, u2, Op.mult, W("wa", 0, 1), Op.add)
-    ts(W("wd", 1, 3), W("wa", 1, 3), W("wb"), Op.add)
-    ts(W("wl1", 0, 2), W("wd", 0, 2), W("wc"), Op.add)
-    ts(W("wl1", 2, 3), r2, u3, Op.mult, W("wd", 2, 3), Op.add)
+    ts(W("wa"), W("mrow", 1, 3), q1, Op.is_equal, 1.0, Op.add)
+    for x in range(2):
+        ts(W("dv1", x, 10, 5), two, W("wa", x, x + 1), Op.mult, (u2, u3)[x] - u1, Op.mult)
+    ts(W("wb"), r3, u1, Op.mult, float(R1 - M0), Op.add)
+    ts(W("wl1"), r1, u2 / u3, Op.mult, r2, Op.add)
     fill(W("dv1", 3, 5), 0.0, "g")
     for h in range(2):
-        tt(W("dv1", 5 * h, 5 * h + 2), W("wl1", 0, 2), W("wl1", 1, 3), Op.subtract)
         fill(W("cg", 112 * h + 64, 112 * h + 96), 0.0, "g")
     fill(W("cg", 96, 224, 112), -TINY)
     fill(W("gs", 63, 144, 80), -1.0, "g")
@@ -383,33 +372,33 @@ def calls(r, cores, topo):
     tt(W("kk", 0, 8), W("csj"), W("csk"), Op.add)
     ts(W("kk", 8, 10), i1, 256.0 * r, Op.add)
     cp(W("ko"), W("kk"))
-    ts(W("jp2"), i1, uj, Op.mult)
+    ts(W("jp3"), i1, uj / u3, Op.mult, W("wl1"), Op.add)
+    ts(W("jp2"), W("jp3"), u3, Op.mult, W("wb"), Op.add)
+    ts(W("i1m"), i1, float(M0 - R1), Op.add)
+    ts(W("kgm"), W("kg"), float(M0 - R1), Op.add)
     for h in range(2):
-        ts(W("hm", 4 * h, 4 * h + 4), W("rho"), 4.0, Op.mult, 2.0 * h, Op.add)
-    cp(W("l1", 0, 4), W("l0", 0, 4), "vs")
-    cp(W("l2"), W("l1", 1, 16), "s")
-    own(W("winc", 0, M0), W("l1"), W("hm"))
-    own(W("wing", 0, M0), W("l2"), W("hm"))
+        ts(W("hm", 4 * h, 4 * h + 4), W("rho"), 2.0, Op.mult, float(h), Op.add)
+    cp(W("l1", 0, 8), W("l0", 16, 24), "s")
+    tt(W("l2"), W("l1", 0, 32, 4), W("l1", 1, 32, 4), Op.add)
+    cp(W("l3"), W("l1", 3, 32, 4), "s")
+    own(W("winc", 0, M0), W("l2"), W("hm"))
+    own(W("wing", 0, M0), W("l3"), W("hm"))
 
     def count(t):
         n = str(t)
         rw, rn, th, cm = "rw" + n, "row" + n, "th" + n, "cm" + n
-        at = 224 * t + 64
-        sa = [W("sa" + n, h, h + 1) for h in range(2)]
-        act(W("sa" + n), W("sc", at, at + 160, 112), Act.Abs)
-        act(W("mx" + n), W("sc", at + 32, at + 160, 112), Act.Abs)
+        sa = [W("sa" + n, 2 * h, 2 * h + 1) for h in range(2)]
+        act(W("sa" + n), C("sc", 2 * t, 2 * t + 2, 95, 97), Act.Abs)
         for h in range(2):
-            o = 112 * h + at
-            turn(W(rw, 32 * h, 32 * h + 32), W("sc", o, o + 32))
+            turn(W(rw, 32 * h, 32 * h + 32), C("sc", 2 * t + h, 2 * t + h + 1, 64, 96))
         act(C(rn, 0, 1, 0, 64), W(rw), Act.Abs)
-        for x in (1, 3):
-            for a in range(4):
-                b = a ^ x
-                act(C(rn, x, x + 1, 0, 64, 32 * a, 32 * a + 32), W(rw, 0, 64, 1, 32 * b, 32 * b + 32), Act.Abs)
+        for a in range(4):
+            act(C(rn, 1, 2, 0, 64, 32 * a, 32 * a + 32), W(rw, 0, 64, 1, 32 * (a ^ 1), 32 * (a ^ 1) + 32), Act.Abs)
         for a in range(2):
-            cp(C(rn, 2, 3, 0, 64, 64 * a, 64 * a + 64), C(rn, 0, 1, 0, 64, 64 - 64 * a, 128 - 64 * a), "vs")
+            act(C(rn, 2, 3, 0, 64, 64 * a, 64 * a + 64), W(rw, 0, 64, 1, 64 - 64 * a, 128 - 64 * a), Act.Abs)
+            cp(C(rn, 3, 4, 0, 64, 64 * a, 64 * a + 64), C(rn, 1, 2, 0, 64, 64 - 64 * a, 128 - 64 * a), "s")
         for h in range(2):
-            ts(W(th, 40 * h, 40 * h + 34), W("gm", 0, 34), W("mx" + n, h, h + 1), Op.mult, sa[h], Op.add)
+            ts(W(th, 40 * h, 40 * h + 34), W("gm", 0, 34), W("sa" + n, 2 * h + 1, 2 * h + 2), Op.mult, sa[h], Op.add)
         for h in range(2):
             o = 256 * h
             tt(W(cm, o, o + 32), C(rn, 0, 1, 32 * h, 32 * h + 32), W(th, 40 * h + 2, 40 * h + 34), Op.is_ge)
@@ -446,7 +435,7 @@ def calls(r, cores, topo):
 
     def gather(t):
         n = "ab"[t]
-        src, width_ = (("tq", 256), ("tw", 448))[t]
+        src, width_ = "tq", (P, R1 + 64)[t]
         off = "off%d" % t
         sl, la = "sl" + n, "la" + n
         bs = BUILD[t]
@@ -489,24 +478,27 @@ def calls(r, cores, topo):
         s, n, d = str(t), "ab"[t], BUILD[t].index(r)
         la, ps, hh = "la" + n, "ps" + n, "h" + s
         pick(ps, 0, la, 128, "rfo" + s, 0, 96)
-        for b in range(4):
-            mm(4 + b, "eq", 128 * b, ps, 0)
         at = 96 if d == 0 else 0
-        for b in range(4):
+        for b in range(3):
+            last = mm(4 + b, "eq", 128 * b, ps, 0)
             cp(W("xs", 64 * b, 64 * b + 64), W("pu", 512 * b + 32, 512 * b + 96), "s")
             tt(W("xd", 32 * b, 32 * b + 32), W("pu", 512 * b, 512 * b + 32), W("xs", 64 * b, 64 * b + 32), Op.subtract)
             tt(W(hh, 4 * at + b, 4 * at + 128, 4), W("xd", 32 * b, 32 * b + 32), W("xs", 64 * b + 32, 64 * b + 64), Op.subtract)
-        dst, base = ("tw", 256) if t == 0 else ("tx", 512)
-        quant(dst, base + 128 * d, hh, 0, 128)
-        c = base + 96 + 32 * d
+        for x in range(3):
+            n = mm(7, ("eq", "en")[x > 0], 0 if x else 384, ps, 32 * x, 128, x == 0, x == 2)
+            n["chain"] = last
+            last = n
+        cp(W(hh, 4 * at + 3, 4 * at + 128, 4), W("pu", 1536, 1568), "vs")
+        c = (R1, R2)[t] + 32 * d
+        quant("tq", c - at, hh, 0, 128)
         for x in ("", "_s"):
-            v = W(dst + x, c, c + 32)
+            v = W("tq" + x, c, c + 32)
             send([(v, v, peers, alle)], "hb%d" % t)
 
     def built(t):
-        dst, base = ("tw", 256) if t == 0 else ("tx", 512)
+        c = (R1, R2)[t]
         lands("hb%d" % t, sum(2 * len(topo.engines(cores[b], core)) for b in BUILD[t] if b != r),
-              [W(dst + x, base + 96 + 32 * d, base + 128 + 32 * d) for x in ("", "_s") for d in range(2) if BUILD[t][d] != r])
+              [W("tq" + x, c + 32 * d, c + 32 + 32 * d) for x in ("", "_s") for d in range(2) if BUILD[t][d] != r])
 
     def mapped(t):
         s = str(t)
@@ -514,17 +506,12 @@ def calls(r, cores, topo):
         cp(W("ofs" + s), W("fi" + s))
         strew(W("mp"), W("ofs" + s), W("va" if t == 0 else "vb"))
 
-    def placed(out, a, b, m, up, home):
-        ts(a, m, 1000.0, Op.mult, float(up), Op.min)
-        tt(b, a, m, Op.add)
-        tt(out, b, home, Op.max)
-
-    def products(t, src, c0, at):
+    def products(t):
         for o in range(2):
             bank = 2 - 2 * t + o
-            mm(bank, "wq", 128 * o, src, c0)
+            mm(bank, "wq", 128 * o, "tq", (R1, R2)[t] - side[t])
             v = W("yn", 128 * t + 64 * o, 128 * t + 64 * o + 64)
-            cp(v, W("pa", 512 * bank + at, 512 * bank + at + 64), "vs")
+            cp(v, W("pa", 512 * bank + side[t], 512 * bank + side[t] + 64), "vs")
             strew(W("yb%d" % o), W("ofs%d" % t), v)
 
     def stripes(t, w):
@@ -542,13 +529,10 @@ def calls(r, cores, topo):
         ts(W("bj", o + 64, o + 128, 1, 0, top), b, 12, Op.arith_shift_right, 3, Op.bitwise_and)
         cp(W("bsf", o, o + 128, 1, 0, 1), W("bj", o, o + 128, 1, 0, 1))
 
-    for m in range(2):
-        tt(W("sq", 8 * m, 8 * m + 8), W("l0", 0, 16, 2), W("wm", 8 * m, 8 * m + 8), Op.mult)
     for h in range(2):
-        scan(W("sc", 112 * h + 56, 112 * h + 97), W("d0c", 12, 53), W("sq", h, 82, 2))
-        act(W("ga", 6 * h, 6 * h + 4), W("l0", 2 * h + 1, 16, 4), Act.Abs)
-    tt(W("gy"), W("ga"), W("cap"), Op.min)
-    scan(W("gx"), W("d0m"), W("gy"), Op.max, Op.mult, HUGE)
+        scan(C("sc", h, h + 1, 58, 97), W("l0", 16 + 4 * h, 328, 8), W("l0", 1 + 4 * h, 312, 8), Op.subtract, Op.add)
+        act(W("ga", 6 * h, 6 * h + 4), W("l0", 18 + 4 * h, 48, 8), Act.Abs)
+    scan(W("gx"), W("d0m"), W("ga"), Op.max, Op.mult, HUGE)
     lost(0, W("gx", 1, 11), W("gx", 0, 10))
     count(0)
     w0 = listed(0)
@@ -569,17 +553,15 @@ def calls(r, cores, topo):
     cp(W("o1"), W("o1f"))
     for h in range(2):
         cp(W("o2", 3 * h, 3 * h + 3), W("o1f", 4 * h + 1, 4 * h + 4))
-    placed(W("src1"), W("sra"), W("srb"), W("ms", 143, 160, 16), R1 - M0, i1)
-    tt(W("jpb"), W("src1"), W("jp2"), Op.add)
-    ts(W("dv1", 2, 10, 5), W("jpb"), W("wl1", 2, 3), Op.add)
+    tt(W("src1"), W("ms", 143, 160, 16), W("i1m"), Op.max)
+    tt(W("dv1", 2, 10, 5), W("src1"), W("jp2"), Op.add)
 
-    mm(0, "uc", 0, "tw", 288)
-    mm(1, "ug", 0, "tw", 288)
-    tt(W("winc", M0, M0 + 64), W("pa", 64, 128), W("mk"), Op.mult)
-    tt(W("wing", M0, M0 + 64), W("pa", 576, 640), W("mk"), Op.mult)
+    for b in range(2):
+        mm(b, ("uc", "ug")[b], 0, "tq", R1 - side[0])
+        tt(W(("winc", "wing")[b], M0, M0 + 64), W("pa", 512 * b + side[0], 512 * b + side[0] + 64), W("mk"), Op.mult)
     for h in range(2):
         take(W("cg", 112 * h, 112 * h + 64), W("winc"), W("o1", 4 * h, 4 * h + 4), "vs"[h])
-        scan(W("sc", 112 * h + 224, 112 * h + 321), W("d0c"), W("cg", 112 * h, 112 * h + 97))
+        scan(C("sc", 2 + h, 3 + h, 0, 97), W("d0c"), W("cg", 112 * h, 112 * h + 97))
     act(W("gg"), W("wing"), Act.Abs, off=W("o2"))
     for h in range(2):
         scan(W("gs", 80 * h, 80 * h + 48), W("d0c", 17, 65), W("gg", 48 * h, 48 * h + 48), Op.max)
@@ -592,140 +574,36 @@ def calls(r, cores, topo):
         buildlist(1, w1)
         build(1)
     built(1)
-    for x in ("", "_s"):
-        move("y", W("tx" + x, old, old + 64), W("tw" + x, R1, R1 + 64), "dl_x" + x)
-    products(0, "tw", 288, 64)
+    products(0)
     mapped(1)
     for x in (0, 16):
         cp(C("md", 0, 16, x, x + 16), W("mp", 256 * r, 256 * r + 256), "s")
     turn(W("fn"), C("md", 0, 16, 0, 32))
-    placed(W("fc"), W("fa"), W("fb"), W("fn", 0, 512, 32), lift, W("kg"))
-    cp(W("fou"), W("fc"))
+    m = W("fn", 0, 512, 32)
+    ts(W("fa"), m, M0 + 64.0, Op.is_ge, R2 - R1 - 64.0, Op.mult)
+    tt(W("fb"), W("fa"), m, Op.add)
+    tt(W("fc"), W("fb"), W("kgm"), Op.max)
+    ts(W("fou"), W("fc"), float(R1 - M0), Op.add)
     stripes(1, w1)
     store("y", lambda T: T.bs[:, :], W("bsf", 0, 256, 1, 0, 1), "dbs")
 
-    products(1, "tx", min(old, R2), 64 if before else 0)
+    products(1)
     for c in range(2):
-        pick("ou", 128 * c, "tx", max(old, R2) + 64, "fou", 8 * c, 128)
+        pick("ou", 128 * c, "tq", R2 + 64, "fou", 8 * c, 128)
 
     def scales(k):
-        store("ys"[k % 2], lambda T: T.osc[4 * k:4 * k + 4, 0:256], W("ou_s", 0, 256, 1, 32 * k, 32 * k + 4), ("doc", "dos")[k % 2])
+        store("ys"[k % 2], lambda T: T.osc[4 * k:4 * k + 4, 0:256], W("ou_s", 0, 256, 1, 32 * k, 32 * k + 4), ("doc", "dos")[k % 2], [W("yb1")])
 
     def block(o):
-        store("ys"[o], lambda T: T.y[:, 256 * o:256 * o + 256], W("yb%d" % o, 256 * r, 256 * r + 256), "dy%d" % o, 200.0 - 200.0 * o)
+        store("ys"[o], lambda T: T.y[:, 256 * o:256 * o + 256], W("yb%d" % o, 256 * r, 256 * r + 256), "dy%d" % o)
 
-    store("y", lambda T: T.oc[:, 0:1024], W("ou"), "doc", 100.0)
+    store("y", lambda T: T.oc[:, 0:512], W("ou", 0, 128), "doc")
+    store("y", lambda T: T.oc[:, 512:1024], W("ou", 128, 256), "doc")
     block(0)
+    block(1)
     for k in range(4):
         scales(k)
-    block(1)
     return nodes
-
-
-def tag(r, n):
-    w = (n["wr"] + n["rd"])[0]
-    return "%d%s%d.%d.%d" % (r % 2, w[0], w[1], w[4], sum(w[6]) if len(w) > 6 else 0)
-
-
-def graph(plans):
-    flat, base = [], []
-    for r, ns in enumerate(plans):
-        base.append(len(flat))
-        for n in ns:
-            flat.append((r, n))
-    pred = [set() for _ in flat]
-    for r, ns in enumerate(plans):
-        log = {}
-        for n in ns:
-            me = base[r] + n["i"]
-            qs = list(n["fns"])
-            for ws, isw in ((n["rd"], False), (n["wr"], True)):
-                for w in ws:
-                    for w2, isw2, j, qs2 in log.get(w[0], ()):
-                        if (isw or isw2 or (w[0] in ("pa", "pu") and (len(qs) > 1 or qs != qs2))) and meet(w, w2):
-                            pred[me].add(j)
-            for ws, isw in ((n["rd"], False), (n["wr"], True)):
-                for w in ws:
-                    log.setdefault(w[0], []).append((w, isw, me, qs))
-            for a in n["after"]:
-                pred[me].add(base[r] + a["i"])
-            pred[me].discard(me)
-    sends = {}
-    for k, (r, n) in enumerate(flat):
-        for to in n["to"]:
-            sends.setdefault(to, []).append(k)
-    for k, (r, n) in enumerate(flat):
-        if "r" in n["fns"]:
-            pred[k].update(sends.get((r, n["sem"]), ()))
-    succ = [[] for _ in flat]
-    for k, ps in enumerate(pred):
-        for j in ps:
-            succ[j].append(k)
-    return flat, pred, succ, [tag(r, n) for r, n in flat]
-
-
-def arrange(g, lean):
-    flat, pred, succ, tags = g
-    wake = TUNE["wake"]
-
-    def after(j, k):
-        return flat[j][1]["lag"] + (0.0 if "r" in flat[k][1]["fns"] else wake)
-    left = [len(s) for s in succ]
-    way = [0.0] * len(flat)
-    todo = [k for k in range(len(flat)) if not left[k]]
-    while todo:
-        k = todo.pop()
-        n = flat[k][1]
-        way[k] = min(n["cost"].values()) + max([n["lag"]] + [after(k, j) + way[j] for j in succ[k]])
-        for j in pred[k]:
-            left[j] -= 1
-            if not left[j]:
-                todo.append(j)
-
-    way = [x + lean.get(t, 0) for x, t in zip(way, tags)]
-    count = [len(p) for p in pred]
-    when, free, ready, best, out, cross = [0.0] * len(flat), {}, {}, {}, [], {}
-
-    def choose(q):
-        f = free.get(q, 0.0)
-        top, at = None, 0.0
-        for k in sorted(ready[q], key=lambda k: (-way[k], k)):
-            s = max(f, when[k], cross.get(q, 0.0) if flat[k][1]["kind"] == 1 else 0.0)
-            if top is None or (s < at and s + flat[k][1]["cost"][q[1]] <= at + TUNE["tol"]):
-                top, at = k, s
-        best[q] = (at, top)
-        if top is None:
-            del best[q]
-
-    def put(k):
-        for q in flat[k][1]["fns"]:
-            ready.setdefault((flat[k][0], q), set()).add(k)
-            choose((flat[k][0], q))
-    for k in range(len(flat)):
-        if not count[k]:
-            put(k)
-
-    def ends(q):
-        n = flat[best[q][1]][1]
-        return best[q][0] + n["cost"][q[1]] + (TUNE["bias"] if q[1] == "v" and len(n["fns"]) > 1 else 0.0), best[q][1]
-    while best:
-        q = min(best, key=ends)
-        at, k = best[q]
-        r, n = flat[k]
-        out.append((r, n, q[1]))
-        end = at + n["cost"][q[1]]
-        free[q] = end if q[1] != "r" else 0.0
-        if q[1] == "v" and n["kind"] == 2:
-            cross[q] = end + wake
-        for x in n["fns"]:
-            ready[(r, x)].discard(k)
-            choose((r, x))
-        for j in succ[k]:
-            when[j] = max(when[j], end + after(k, j))
-            count[j] -= 1
-            if not count[j]:
-                put(j)
-    return out
 
 
 def viewer(T):
@@ -744,9 +622,7 @@ def rank_program(g, core, T, topo):
     r = T.rank_of(core)
     if r is None:
         return
-    cores = list(T.cores)
-    if "order" not in _PLANS:
-        _PLANS["order"] = arrange(graph([calls(i, cores, topo) for i in range(N)]), LEAN)
+    nodes = calls(r, list(T.cores), topo)
     queue = {"v": g.vector, "s": g.scalar, "t": g.tensor, "g": g, "y": g.sync}
     total, known, snap, log = {}, {q: {} for q in queue}, {}, {}
     env = dict(queue, T=T, ap=viewer(T))
@@ -761,10 +637,11 @@ def rank_program(g, core, T, topo):
             if known[q].get(a, 0) < b:
                 known[q][a] = b
 
-    tokens, cross = {}, 0
-    for rank, n, q in _PLANS["order"]:
-        if rank != r:
-            continue
+    cross = 0
+    for i in range(0, len(ORDER[r]), 2):
+        v = int(ORDER[r][i:i + 2], 36)
+        n = nodes[v // 2]
+        q = "vs"[v % 2] if len(n["fns"]) > 1 else list(n["fns"])[0]
         s = n["sem"] or _QS[q]
         if q != "r":
             need = {}
@@ -773,9 +650,8 @@ def rank_program(g, core, T, topo):
                     for w2, isw2, tok, q2 in log.get(w[0], ()):
                         if (isw or isw2 or (w[0] in ("pa", "pu") and q != q2)) and meet(w, w2):
                             need[tok[0]] = max(need.get(tok[0], 0), tok[1])
-            for a in n["after"]:
-                tok = tokens[a["i"]]
-                need[tok[0]] = max(need.get(tok[0], 0), tok[1])
+            if n.get("chain"):
+                need.pop("st", None)
             if q == "v" and n["kind"] == 1 and cross:
                 need["sv"] = max(need.get("sv", 0), cross)
             for x in sorted(need):
@@ -789,9 +665,8 @@ def rank_program(g, core, T, topo):
                 snap[(s, total[s])] = dict(known[q])
         else:
             total[s] = n["by"]
-        tok = tokens[n["i"]] = (s, total[s])
         for ws, isw in ((n["rd"], False), (n["wr"], True)):
             for w in ws:
-                log.setdefault(w[0], []).append((w, isw, tok, q))
-    for s in sorted(total):
+                log.setdefault(w[0], []).append((w, isw, (s, total[s]), q))
+    for s in sorted(total, key=lambda s: (s in ("doc", "dos", "dy0", "dy1"), s)):
         wait("g", (s, total[s]))

from concourse.bass import DstId, RemoteDMATransfer
from concourse.mybir import dt, AluOpType as Op, ActivationFunctionType as Act

N, P, K = 4, 256, 64
R1, R2 = 352, 512
M0 = 128
BUILD = ((0, 2), (1, 3))
STEP = 1.5 * 2.0 ** -24
TINY = 2.0 ** -100
HUGE = 2.0 ** 90
UNIT = 32768.0
TUNE = dict(wake=165.0, fac=1.25, load=800.0, issue=60.0, rissue=250.0, hop=500.0, row=15.0, byte=0.03, first=0.0, eng=15.0, tol=0.0, bias=20.0,
            pe=1.3, gat=1.56)
LEAN = {}
ORDER = ['0002040c061a100o0y0u0m0q0s0w1o36141v1w5r3i3k1618321c1y0e20242y4g224t4e3m26281i3o383q2a0a1k3s3a3076341e3u2c4i3w3y5o4k6q1q5u5s081g521s3c6g6i3e74722e0g6k6m4u7g7i4y7k2g6o2m0i7w2s2i7u7y4m2k2o2q805w628i2u2w5c8k4a6s848682881m4w500k567m8a8e8m908q8o403g8c8g94927o8s8u8w7q9a4496988y7s684c9c9g9e669i9k12469m6c9o9q9s9u9w6e9ya06a42584o5aa2a4aa7aa6a848aqacaeamakauawascg78caagaib0ci4qckayccao7ccocmb2b4bmb6cs54cucebobq5ybeb8bubgba64bwbibsbcbkbyc1606uc2cycwc46yd06w70c6cqd27eda5ed4c8dedidgd8d65gdmdkdcdqdo5kdsdue6e4e8dweaegeceeeieseudyewfae0eoekeqemf0eyfcfef4fgf2f6fifke2f8fm5ifofsfqfu5mgyfwfyg0h1h4g2g4g6g8h7gagegcgggigkgugmhugohahcgqh2hwgshehghyhihki0i2h8hmhoi4hqi6hsgwi8ikimieibisioihiuiciqiwiiiyj6j2j0j4',
         '0002040c061a0o0y0m0q0u0s0w101o141v1w1i5r3i16181c1y1k3k0a3m1q3o20081g3q242y38323s1s223u3a1e3c3w2630283y0g2a34363e5o6q5u4t2c5s521m6g6i74720k566k6m4c403g546o2e5w626s442g7g7i2m7k7m2s760i4w7w2i2k7u7y2o687o2q2u808i2w66508k4u7q848682884y128m5c908a8e7s6c4a8q8o8c8g94926e8s8u8w4m96989a8y489c9g9e9i9k469m9o9q9s9u9w9y0ea06a42a2a4a6a8aa60akacae78ao6u6yauagawai584o7a5aay4ib2b04eb64gb87c5e4k4qaqas5y64bcbabe6w70bg7ebobib45g5k5i5mambsbwbubmbkgyc0bybqc4h4h1c2c6c8ckcicmh7cacocucqcscwd6d8ccdadoced2cyd4d0dedcdqdsdidudgdkdydwcgdme0e2e6e4e8eaeceeegeiekemeoeseqeueweyfef0f2hafgfifkhufaf4f8hwf6hcfmfohyi0h2fchefqi2fshgi4h8gafugci6g2fwgei8gig4fyg6gggkhig0gmg8gpgqhkhmhogshqguhsgwiaimioigidiuiqijiwieisiyikj0j8j4j6j2',
         '0002040c061a100o0y0m0q0u0s0w1o36141v1w5n3i16181c1y3k320e20242y4g224t4e3m26281i3o383q2a0a1k3s3a303u341e3w2c4i3y5k4k6m1q5q5o081g4y1s3c6c6e3e706y2e0g6g6i4u7c7e4w727g2g6k2m0i7s2s2i7q7u4m2k2o2q7w827y84805y5s8e2u2w581m0k527i868g4a6o8i8w8m8k90888a8c403g7k8y8s8o8q7m964492947o8u644c989a9c629e9g46129i9k689m9o9q9s6a9u9w6642544o9ya0a2a4a648ama8aaaiaqasao74c6agcc7656acawaece4qcgauc8akck78aycib0bib250cocabkbab4cqbm5ubqbcb660bsbebob8bgbubx6q5wbycucsc06ucw6s6wc2cmcy7ad65ad0c4dadedcd4d25cdidgd8dmdk5gdodqe2e0e4dseoeqdue6ece8eaeeesf6dwekegemeieuewf8faf0fceyf2fefgdyf4fi5efkfofmfq5igufsfufwgxh0fyg0g2g4h3g6gag8gegcgggqgihqgkh6h8gmhsgohahchuhwgyhehghyi0h4hihki2hmi4hogsi6iiikici9iqimifisiaioiuigiwj4j0iyj2',
         '0002040c061a0o0y0m0q0u0s0w101o141v1w1i5r3i3k0a16181y1c1k3m1q3o20081g3q24322y383s1s223u3a1e303c283w263y0g2a34363e5o6q5u4t2c5s521m6g6i74720k566k6m4c403g546o2e5w626s442g7g7i2m7k7m2s760i4w7w2i2k7u7y2o687o2q2u808i2w66508k4u7q868288844y128m5c908a8e7s6c4a8q8o8c8g94926e8s8u8w4m96989a8y489c9g9e9i9k469m9o9q9s9u9w9y0ea06a42a2a4a6a8aa60akacae78ao6u6yauagawai584o7a5aay4ib2b04eb64gb87c5e4k4qaqas5y64bcbabe6w70bg7ebobib45g5k5i5mambsbwbmbkbuh0bqc0byc4h6h3c2c6c8ckcicmh9cacocucqcscwd6d8ccdadoced2cyd4d0dedcdqdsdidudgdkdwdycgdme0e2e6e4e8eaeceeegeiekemeoeseqeueweyfefgf0fahwf2hcf4fifkfmf8hyhefofqf6h4i2hgi0fcfsfuhii4gci6hafwgei8g4fyggiagkg6g0gmg8gihkg2gogagrgshmhohqguhsgwhugyicioiqiiifiwisiliyigiuj0imj2jaj6j4j8']

F, B, I, U16, CODES = "float32", "bfloat16", "int32", "uint16", "float8_e4m3fn_x4"
SCRATCH, LOG, _TOP = {}, {}, {}


def _own(dtype, **kw):
    for n, c in kw.items():
        SCRATCH[n] = ("sbuf", [128, c], dtype)
        LOG[n] = (n, 0, c, dtype)


def _cube(dtype, **kw):
    for n, (a, b) in kw.items():
        SCRATCH[n] = ("sbuf", [128, a, b], dtype)
        LOG[n] = (n, 0, a * b, dtype)


def _slab(slab, dtype, **kw):
    for n, c in kw.items():
        at = _TOP.get(slab, 0)
        LOG[n] = (slab, at, c, dtype)
        _TOP[slab] = at + (c + 15) // 16 * 16
        SCRATCH[slab] = ("sbuf", [128, _TOP[slab]], dtype)


_own(B, ut=532, tbt=1024, wt=1024, eb=516, em=516, ub0=512, ub1=512, h0=512, h1=512, mp=1024)
for _n, _c in dict(tq=672, uq=128, uc=128, ug=128, eq=512, wq=256, sla=64, slb=64, laa=128, lab=128, psa=192, psb=192, en=128, ou=256).items():
    _own(CODES, **{_n: _c})
    _own("uint8", **{_n + "_s": _c})
for _n in ("pa", "pu"):
    SCRATCH[_n] = ("psum", [128, 2048], F)
    LOG[_n] = (_n, 0, 2048, F)
_own(F, l0=328, l1=32, l2=8, l3=8, xs=256, xd=128, yb0=1024, yb1=1024, winc=192, wing=192, uf=8)
_cube(F, row0=(4, 64), row1=(4, 64), kt=(4, 32), mm0=(4, 64), mm1=(4, 64), sc=(4, 112))
_cube(B, md=(16, 32))
_slab("fs", F, jc=2, jp0=2, jp2=2, jp3=2, cf=12, wm=4, ca=1, cb=1, c1=1, c0=1, none=1, minus=1, wa=2, wb=1, wl1=1, i1m=2, kgm=16,
      mb=4, mk=64, rho=4, gm=40, mrow=32, kf=16, kg=16, ofrf=4, kk=10, o1f=8, src1=2, cg=224, gg=96, gs=144,
      fa=16, fb=16, fc=16, yn=256, lr=128, bsf=256, ga=12, d0m=12, gx=12, d0c=97)
_slab("hs", B, i16=160, dg=160, d0g=160, va=64, vb=64, mg=160, ms=160, fn=512)
for _t in "01":
    _slab("fs", F, **{n + _t: c for n, c in dict(rw=64, sa=4, th=80, mt=256, zz=256, ac=4, ng=10, dv=10, pay=10, er=64, po=128, pe=2).items()})
    _slab("hs", B, **{n + _t: c for n, c in dict(cm=512, cj=256).items()})
    _slab("is_", I, **{n + _t: c for n, c in dict(wj=4, wk=2, rk=6, fi=4).items()})
    _slab("us", U16, **{n + _t: c for n, c in dict(off=4, rfo=6, ofs=4).items()})
_slab("is_", I, bi=128, bk=64, bj=256, pi=4, ci=12, csi=8, csj=8, csk=8, dj=64, dk=64)
_slab("us", U16, ofr=4, fou=16, ko=10, o1=8, o2=6, hm=8)

SEMAPHORES = ["sv", "ss", "st", "sg", "dl_u", "dl_t0", "dl_w", "dl_l", "dl_p", "dl_p_s", "dl_k", "dl_k_s", "dbs", "dy0", "dy1", "doc", "dos",
              "ls", "a0", "ha0", "ha1", "hb0", "hb1"]
_QS = {"v": "sv", "s": "ss", "t": "st", "g": "sg"}


def W(name, c0=0, c1=None, step=1, p0=0, p1=128):
    return (name, c0, LOG[name][2] if c1 is None else c1, step, p0, p1)


def C(name, a0, a1, b0, b1, p0=0, p1=128):
    return (name, 0, LOG[name][2], 1, p0, p1, (a0, a1, b0, b1))


def width(w):
    if len(w) > 6:
        a0, a1, b0, b1 = w[6]
        return (a1 - a0) * (b1 - b0)
    return len(range(w[1], w[2], w[3]))


def meet(a, b):
    if a[4] >= b[5] or b[4] >= a[5]:
        return False
    if a[0] in ("pa", "pu"):
        return a[1] // 512 <= (b[2] - 1) // 512 and b[1] // 512 <= (a[2] - 1) // 512
    if len(a) > 6 and len(b) > 6:
        x, y = a[6], b[6]
        return x[0] < y[1] and y[0] < x[1] and x[2] < y[3] and y[2] < x[3]
    if a[1] >= b[2] or b[1] >= a[2]:
        return False
    return not (a[3] == b[3] and a[3] > 1 and (a[1] - b[1]) % a[3])


def calls(r, cores, topo):
    core = cores[r]
    nodes = []
    cyc = 0.83 * TUNE["fac"]

    def node(rd, wr, fns, cost, sem=None, by=1, lag=0.0, to=(), cast=False, busy=0.0):
        kind = 2 if len(rd) > 1 and rd[0][4] != rd[1][4] else 1 if rd else 0
        nodes.append(dict(kind=kind, busy=busy, rd=rd, wr=wr, fns=fns, cost=cost, sem=sem, by=by, lag=lag, to=to, cast=cast, i=len(nodes)))
        return nodes[-1]

    def small(n, *ws):
        if ws and all(LOG[w[0]][3] in (B, U16) for w in ws):
            n = n / 2
        return max(64, n) * cyc

    def tt(out, a, b, op):
        both = a[0] not in ("pa", "pu") and b[0] not in ("pa", "pu")
        return node([a, b], [out], {"v": lambda e: e["v"].tensor_tensor(e["ap"](out), e["ap"](a), e["ap"](b), op)},
                    {"v": small(width(out) * (2 if both else 1))})

    def own(out, win, off):
        n = width(out)
        b = W("dg", 0, n)
        return node([win, off, b], [out], {"v": lambda e: e["v"].tensor_tensor(e["ap"](out), e["ap"](win).indirect(e["ap"](off)), e["ap"](b), Op.mult)},
                    {"v": (50 + max(2, TUNE["gat"]) * 0.83 * n) * TUNE["fac"]})

    def take(out, win, off, q):
        n = TUNE["gat"] * 0.83 * width(out)
        fns = {"v": lambda e: e["v"].tensor_copy(e["ap"](out), e["ap"](win).indirect(e["ap"](off))),
               "s": lambda e: e["s"].activation(e["ap"](out), e["ap"](win).indirect(e["ap"](off)), Act.Copy)}
        return node([win, off], [out], {x: fns[x] for x in q}, {x: (n + (50 if x == "v" else 65)) * TUNE["fac"] for x in q})

    def strew(win, off, src):
        node([off, src], [win], {"v": lambda e: e["v"].tensor_copy(e["ap"](win).indirect(e["ap"](off)), e["ap"](src))},
             {"v": (50 + TUNE["gat"] * 2.3 * 0.83 * width(src)) * TUNE["fac"]})

    def ts(out, a, s1, op0, s2=None, op1=None):
        rd = [a] + [s for s in (s1, s2) if isinstance(s, tuple)]

        def f(e):
            x1, x2 = [e["ap"](s) if isinstance(s, tuple) else s for s in (s1, s2)]
            if op1 is not None:
                return e["v"].tensor_scalar(e["ap"](out), e["ap"](a), x1, x2, op0, op1)
            return e["v"].tensor_scalar(e["ap"](out), e["ap"](a), x1, None, op0)
        return node(rd, [out], {"v": f}, {"v": small(width(out), out, a)})

    def cp(out, a, q="v"):
        fns = {"v": lambda e: e["v"].tensor_copy(e["ap"](out), e["ap"](a)), "s": lambda e: e["s"].activation(e["ap"](out), e["ap"](a), Act.Copy)}
        return node([a], [out], {x: fns[x] for x in q}, {x: small(width(out)) for x in q})

    def fill(out, c, q="v"):
        fns = {"v": lambda e: e["v"].memset(e["ap"](out), c),
               "g": lambda e: e["g"].iota(e["ap"](out), [[0, width(out)]], int(c), 0, allow_small_or_imprecise_dtypes=True)}
        return node([], [out], {x: fns[x] for x in q}, {x: small(width(out), out) if x == "v" else 130 * TUNE["fac"] + 2 * cyc * width(out) for x in q})

    def turn(out, a):
        return node([a], [out], {"v": lambda e: e["v"].transpose(e["ap"](out), e["ap"](a))}, {"v": small(width(a), out, a)})

    def scan(out, d0, d1, op=Op.subtract, op0=Op.mult, first=0.0):
        col = isinstance(first, tuple)
        return node([d0, d1] + [first] * col, [out],
                    {"v": lambda e: e["v"].tensor_tensor_scan(e["ap"](out), e["ap"](d0), e["ap"](d1), e["ap"](first) if col else first, op0, op)},
                    {"v": small(width(out), out, d0, d1)})

    def spread(out, s):
        a = W("ut", 16, 16 + width(out))
        return node([a, s], [out], {"s": lambda e: e["s"].activation(e["ap"](out), e["ap"](a), Act.Copy, scale=e["ap"](s))}, {"s": small(width(out))})

    def act(out, a, f, off=None):
        rd = [a] + [w for w in (off,) if w is not None]
        n = width(out)
        return node(rd, [out], {"s": lambda e: e["s"].activation(e["ap"](out), e["ap"](a) if off is None else e["ap"](a).indirect(e["ap"](off)), f)},
                    {"s": small(n) if off is None else (65 + TUNE["gat"] * 0.83 * n) * TUNE["fac"]})

    def total(out, a, spare):
        return node([a], [out, spare], {"s": lambda e: e["s"].activation(e["ap"](spare), e["ap"](a), Act.Copy, accum_out=e["ap"](out))},
                    {"s": small(width(a)) + 20})

    def iota(out, pattern, base=0, cm=0):
        kw = {} if LOG[out[0]][3] == I else {"allow_small_or_imprecise_dtypes": True}
        return node([], [out], {"g": lambda e: e["g"].iota(e["ap"](out), pattern, base, cm, **kw)}, {"g": 130 * TUNE["fac"] + 2 * cyc * width(out)})

    def quant(name, c0, src, s0, n):
        q, s, x = W(name, c0, c0 + n), W(name + "_s", c0, c0 + n), W(src, s0, s0 + 4 * n)
        return node([x], [q, s], {"v": lambda e: e["v"].quantize_mx(e["ap"](q), e["ap"](s), e["ap"](x))}, {"v": (12 + 0.88 * n) * TUNE["fac"]})

    def mm(bank, lhs, l0, rhs, r0, n=128, start=True, stop=True):
        rd = [W(lhs, l0, l0 + 128), W(lhs + "_s", l0, l0 + 128), W(rhs, r0, r0 + n), W(rhs + "_s", r0, r0 + n)]
        o = W("pu" if bank > 3 else "pa", 512 * (bank % 4), 512 * (bank % 4) + n)
        return node(rd, [o] if start or stop else [],
                    {"t": lambda e: e["t"].matmul_mx(e["ap"](o), e["ap"](rd[0]), e["ap"](rd[1]), e["ap"](rd[2]), e["ap"](rd[3]), start, stop)},
                    {"t": TUNE["pe"] * (n + 16) * cyc})

    def pick(dst, d0, src, width_, off, o0, n):
        o, a, f = W(dst, d0, d0 + n), W(src, 0, width_), W(off, o0, o0 + n // 16)
        node([a, f], [o], {"v": lambda e: e["v"].tensor_copy(e["ap"](o).bitcast(dt.uint32), e["ap"](a).bitcast(dt.uint32).indirect(e["ap"](f)))},
             {"v": (50 + TUNE["gat"] * 0.83 * n) * TUNE["fac"]})
        act(W(dst + "_s", d0, d0 + n), W(src + "_s", 0, width_), Act.Copy, off=f)

    def raw(e, w):
        return e["ap"](w).bitcast(dt.uint8) if LOG[w[0]][3] == CODES else e["ap"](w)

    def rows(w, n=1.0):
        return n * max(1, (w[5] - w[4]) // 16) * (TUNE["row"] + TUNE["byte"] * width(w) * {F: 4, CODES: 4, B: 2}.get(LOG[w[0]][3], 1))

    def load(q, w, tensor, c0, c1, sem, first=()):
        return node(list(first), [w], {q: lambda e: e[q].dma_start(e["ap"](w), e["T"][tensor][:, c0:c1])}, {q: TUNE["issue"]}, sem, 16, TUNE["load"],
                    busy=rows(w))

    def move(q, out, a, sem, first):
        return node([a, first], [out], {q: lambda e: e[q].dma_start(raw(e, out), raw(e, a))}, {q: TUNE["issue"]}, sem, 16, TUNE["load"], busy=rows(a))

    def store(q, dst, a, sem, first=()):
        return node([a] + list(first), [], {q: lambda e: e[q].dma_start(dst(e["T"]), raw(e, a))}, {q: TUNE["issue"]}, sem, 16, TUNE["load"],
                    busy=rows(a))

    peers = [c for c in cores if c != core]
    used = set()

    def mask(engs):
        m = 0
        for e in engs:
            m |= 1 << e
        return m

    def send(parts, sem):
        def did(c):
            a = topo.addr(c)
            return DstId(rid=a[0], pnc=a[1])

        def f(e):
            return e["g"].remote_dma_fused([RemoteDMATransfer(dst_ids=[did(c) for c in cs], dma_engine_mask=mask(es), remote_sem=e["T"].sem[sem],
                                                              srcs=[raw(e, a)], dsts=[raw(e, b)] * len(cs)) for a, b, cs, es in parts],
                                           local_sem=e["T"].sem["ls"])
        new = {x for p in parts for x in p[3]} - used
        used.update(new)
        return node([p[0] for p in parts], [], {"g": f}, {"g": TUNE["rissue"]}, "ls", sum(len(p[3]) for p in parts),
                    TUNE["hop"] + TUNE["first"] * (sem == "a0") + TUNE["eng"] * len(new),
                    [(cores.index(c), sem) for p in parts for c in p[2]], True, max(rows(a, 16 / len(es) * len(cs)) for a, b, cs, es in parts))

    def lands(sem, count, views):
        return node([], views, {"r": None}, {"r": 0.0}, sem, count)

    alle = topo.engines(core, peers[0])

    load("y", W("ut", 4, 12), "u", 0, 8, "dl_u")
    load("s", W("tbt"), "tb", 0, 1024, "dl_t0")

    iota(W("pi", 0, 2), [[1, 2]], 0, 1)
    iota(W("pi", 2, 4), [[128, 2]], r, 1)
    iota(W("jc"), [[128, 2]], 0, 1)
    iota(W("mrow"), [[1, 32]])
    ones = W("ut", 16, 532)
    fill(ones, 1.0)
    node([ones], [W("eb")], {"g": lambda e: e["g"].affine_select(e["ap"](W("eb")), e["ap"](ones), [[-1, 516]], Op.is_equal, 0.0, 3, 4)},
         {"g": 170 * TUNE["fac"] + 1032 * cyc})
    iota(C("kt", 0, 4, 0, 32), [[16, 4], [0, 2], [1, 16]])
    iota(W("kf"), [[16, 16]])
    iota(W("ofrf"), [[2, 2], [0, 2]])

    pp = W("pi", 0, 1)
    ts(W("ci", 0, 2), W("pi", 0, 2), 3, Op.bitwise_and)
    ts(W("ci", 2, 3), pp, 15, Op.bitwise_and)
    ts(W("ci", 3, 4), pp, 4, Op.arith_shift_right, 1, Op.bitwise_and)
    ts(W("ci", 4, 6), W("pi", 2, 4), 255, Op.bitwise_and)
    ts(W("ci", 6, 7), pp, 31, Op.bitwise_and)
    ts(W("ci", 7, 8), pp, 5, Op.arith_shift_right, 1, Op.bitwise_and)
    ts(W("ci", 8, 9), pp, 6, Op.arith_shift_right)
    fill(W("d0c"), 1.0)
    fill(W("d0c", 16, 17), -1.0, "g")
    cp(W("cf", 0, 9), W("ci", 0, 9))
    q0, q1, xf, gf, i1 = W("cf", 0, 1), W("cf", 1, 2), W("cf", 2, 3), W("cf", 3, 4), W("cf", 4, 6)
    two = W("d0c", 0, 2)
    ts(W("wm", 0, 1), q0, float(r), Op.is_equal)
    ts(W("wm", 1, 3), two, q0, Op.mult, float(r), Op.not_equal)
    fill(W("wm", 3, 4), 1.0, "g")
    ts(W("gm", 0, 2), W("cf", 7, 9), -STEP, Op.mult, STEP, Op.add)
    ts(W("gm", 2, 34), W("mrow"), W("cf", 6, 7), Op.is_ge, STEP, Op.mult)
    fill(W("l0", 0, 16), 0.0, "g")
    fill(W("l0", 48, 328), 0.0, "g")
    fill(W("l0", 305, 312, 4), -TINY)
    fill(W("ga", 4, 12, 6), 0.0, "g")
    fill(W("ga", 5, 12, 6), HUGE)
    fill(W("d0m"), 1.0, "g")
    fill(W("d0m", 0, 12, 6), -1.0, "g")

    for x in (0, 12):
        cp(W("ut", x, x + 4), W("ut", 4 + x // 3, 8 + x // 3), "vs")
    quant("uq", 0, "ut", 0, 128)
    quant("tq", 0, "tbt", 0, 128)
    mm(0, "tq", 0, "uq", 0)
    quant("tq", 128, "tbt", 512, 128)
    mm(1, "tq", 128, "uq", 0)

    mine = W("l0", 16 + 8 * r, 24 + 8 * r)
    for h in range(2):
        tt(W("l0", mine[1] + 4 * h, mine[1] + 4 * h + 4), W("pa", 512 * h, 512 * h + 4), W("wm"), Op.mult)
    send([(mine, mine, peers, alle)], "a0")
    lands("a0", 3 * len(alle), [W("l0", 16 + 8 * o, 24 + 8 * o) for o in range(N) if o != r])
    landed = W("l0", 16, 48)

    for o in range(1, N):
        at = 16 + 8 * o
        move("y", W("l1", 8 * o, 8 * o + 8, 1, 0, 128 - o), W("l0", at, at + 8, 1, o, 128), "dl_l", landed)
        for h in range(2):
            move("y", W("l1", 8 * o + 4 * h, 8 * o + 4 * h + 4, 1, 128 - o, 128), W("l0", at + 4 - 4 * h, at + 8 - 4 * h, 1, 0, o), "dl_l", landed)

    u1, u2, u3, uj = 4096 / UNIT, 4 / UNIT, 1 / UNIT, 16 / UNIT
    ts(W("c0"), q0, 0.0, Op.not_equal, u2 - u1, Op.mult)
    ts(W("dv0", 0, 10, 6), two, W("c0"), Op.mult)
    ts(W("c1"), q0, 2.0, Op.is_ge, u3 - u2, Op.mult)
    ts(W("dv0", 1, 10, 6), two, u2 - u1, Op.mult, W("c1"), Op.add)
    fill(W("dv0", 2, 10, 6), u3 - u1)
    ts(W("ca"), q0, 0.0, Op.is_equal, 3 * u3, Op.mult)
    ts(W("cb"), q0, -u3, Op.mult)
    ts(W("jp0"), W("jc"), 1.0 + uj, Op.mult, 3 * u1 + 3 * u3, Op.add)
    ts(W("dv0", 3, 10, 6), W("jp0"), W("ca"), Op.add, W("cb"), Op.add)
    fill(W("dv0", 4, 6), 0.0, "g")

    cp(W("uf"), W("ut", 4, 12), "s")
    for x in range(8):
        spread(W("ub%d" % (x // 4), x % 4, 512, 4), W("uf", x, x + 1))
    iota(W("va"), [[1, 64]], M0)
    iota(W("vb"), [[1, 64]], M0 + 64)
    iota(W("i16"), [[0, 10], [1, 16]])
    ts(W("dg"), W("i16"), xf, Op.is_equal)
    ts(W("d0g"), W("i16"), 0.0, Op.not_equal)
    ts(W("kg"), W("kf"), xf, Op.add)
    ts(W("ofr"), W("ofrf"), gf, Op.add)
    when = 0 if r in BUILD[0] else 1
    for b in range(4):
        quant("eq", 128 * b, "eb", 3 - b, 128)
    fill(W("minus"), -1.0, "g")
    node([W("eb"), W("minus")], [W("em")], {"s": lambda e: e["s"].activation(e["ap"](W("em")), e["ap"](W("eb")), Act.Copy, scale=e["ap"](W("minus")))},
         {"s": small(516)})
    quant("en", 0, "em", 0, 128)
    cp(W(("h0", "h1")[when]), W("tbt", 0, 512), "vs")
    side = [0 if r == BUILD[t][1] else 64 for t in range(2)]
    for x in ("", "_s"):
        move("y", W(("psa", "psb")[when] + x, 96, 192), W("uq" + x, 0, 96), "dl_p" + x, landed)
        if when or r == BUILD[0][0]:
            c = (R2, R1)[when]
            move("y", W("tq" + x, c - 64, c), W("uq" + x, 0, 64), "dl_k" + x, landed)
    quant("uc", 0, "ub0", 0, 128)
    quant("ug", 0, "ub1", 0, 128)
    fill(W("none"), -256.0, "g")
    for a in (0, 512):
        spread(W("mp", a, a + 512), W("none"))
    load("y", W("wt"), "w", 0, 1024, "dl_w", [landed])
    quant("wq", 0, "wt", 0, 256)
    for o in range(2):
        mm(2 + o, "wq", 128 * o, "tq", 0, 256)
        cp(W("yb%d" % o, 256 * r, 256 * r + 256), W("pa", 512 * (2 + o), 512 * (2 + o) + 256), "s")

    ts(W("mb", 0, 3), W("mrow", 0, 3), q1, Op.is_ge)
    cp(W("rho", 0, 1), q1, "vs")
    tt(W("rho", 1, 4), W("mrow", 0, 3), W("mb", 0, 3), Op.add)
    r1, r2, r3 = W("rho", 1, 2), W("rho", 2, 3), W("rho", 3, 4)
    ts(W("wa"), W("mrow", 1, 3), q1, Op.is_equal, 1.0, Op.add)
    for x in range(2):
        ts(W("dv1", x, 10, 5), two, W("wa", x, x + 1), Op.mult, (u2, u3)[x] - u1, Op.mult)
    ts(W("wb"), r3, u1, Op.mult, float(R1 - M0), Op.add)
    ts(W("wl1"), r1, u2 / u3, Op.mult, r2, Op.add)
    fill(W("dv1", 3, 5), 0.0, "g")
    for h in range(2):
        fill(W("cg", 112 * h + 64, 112 * h + 96), 0.0, "g")
    fill(W("cg", 96, 224, 112), -TINY)
    fill(W("gs", 63, 144, 80), -1.0, "g")
    fill(W("gs", 79, 80), 1.0, "g")
    for h in range(2):
        ts(W("csi", 4 * h, 4 * h + 4), W("rho"), 4097.0, Op.mult, W("jc", h, h + 1), Op.add)
    ts(W("csj"), W("csi"), 255, Op.bitwise_and)
    ts(W("csk"), W("csi"), 4, Op.arith_shift_right, 768, Op.bitwise_and)
    tt(W("kk", 0, 8), W("csj"), W("csk"), Op.add)
    ts(W("kk", 8, 10), i1, 256.0 * r, Op.add)
    cp(W("ko"), W("kk"))
    ts(W("jp3"), i1, uj / u3, Op.mult, W("wl1"), Op.add)
    ts(W("jp2"), W("jp3"), u3, Op.mult, W("wb"), Op.add)
    ts(W("i1m"), i1, float(M0 - R1), Op.add)
    ts(W("kgm"), W("kg"), float(M0 - R1), Op.add)
    for h in range(2):
        ts(W("hm", 4 * h, 4 * h + 4), W("rho"), 2.0, Op.mult, float(h), Op.add)
    cp(W("l1", 0, 8), W("l0", 16, 24), "s")
    tt(W("l2"), W("l1", 0, 32, 4), W("l1", 1, 32, 4), Op.add)
    cp(W("l3"), W("l1", 3, 32, 4), "s")
    own(W("winc", 0, M0), W("l2"), W("hm"))
    own(W("wing", 0, M0), W("l3"), W("hm"))

    def count(t):
        n = str(t)
        rw, rn, th, cm = "rw" + n, "row" + n, "th" + n, "cm" + n
        sa = [W("sa" + n, 2 * h, 2 * h + 1) for h in range(2)]
        act(W("sa" + n), C("sc", 2 * t, 2 * t + 2, 95, 97), Act.Abs)
        for h in range(2):
            turn(W(rw, 32 * h, 32 * h + 32), C("sc", 2 * t + h, 2 * t + h + 1, 64, 96))
        act(C(rn, 0, 1, 0, 64), W(rw), Act.Abs)
        for a in range(4):
            act(C(rn, 1, 2, 0, 64, 32 * a, 32 * a + 32), W(rw, 0, 64, 1, 32 * (a ^ 1), 32 * (a ^ 1) + 32), Act.Abs)
        for a in range(2):
            act(C(rn, 2, 3, 0, 64, 64 * a, 64 * a + 64), W(rw, 0, 64, 1, 64 - 64 * a, 128 - 64 * a), Act.Abs)
            cp(C(rn, 3, 4, 0, 64, 64 * a, 64 * a + 64), C(rn, 1, 2, 0, 64, 64 - 64 * a, 128 - 64 * a), "s")
        for h in range(2):
            ts(W(th, 40 * h, 40 * h + 34), W("gm", 0, 34), W("sa" + n, 2 * h + 1, 2 * h + 2), Op.mult, sa[h], Op.add)
        for h in range(2):
            o = 256 * h
            tt(W(cm, o, o + 32), C(rn, 0, 1, 32 * h, 32 * h + 32), W(th, 40 * h + 2, 40 * h + 34), Op.is_ge)
            ts(W(cm, o + 32, o + 64), C(rn, 1, 2, 32 * h, 32 * h + 32), W(th, 40 * h, 40 * h + 1), Op.is_ge)
            for x in (0, 2):
                ts(W(cm, o + 64 + 32 * x, o + 128 + 32 * x), C(rn, x, x + 2, 32 - 32 * h, 64 - 32 * h), sa[h], (Op.is_gt, Op.is_ge)[h])
            ts(W(cm, o + 192, o + 256), C(rn, 2, 4, 32 * h, 32 * h + 32), W(th, 40 * h + 1, 40 * h + 2), Op.is_ge)
            near = W("pe" + n, h, h + 1)
            total(near, W(cm, o, o + 128), W("cj" + n, 128 * h, 128 * h + 128))
            scan(W("po" + n, 64 * h, 64 * h + 64), W(cm, o + 128, o + 192), W(cm, o + 192, o + 256), Op.add, Op.add, near)

    def listed(t):
        m, mt, z, c, po, pay = [x + str(t) for x in ("mm", "mt", "zz", "ac", "po", "pay")]
        for h in range(2):
            at = (3 + 6 * h, 2 + 5 * h)[t]
            for y in (0, 2):
                ts(C(m, y, y + 2, 32 * h, 32 * h + 32), C("kt", y, y + 2, 0, 32), W(po, 64 * h + 63, 64 * h + 64), Op.is_equal, W(pay, at, at + 1), Op.mult)
        for y in range(4):
            turn(W(mt, 64 * y, 64 * y + 64), C(m, y, y + 1, 0, 64))
        for y in range(4):
            o = 64 * y
            scan(W(z, o, o + 64, 1, 0, 64), W(mt, o, o + 64, 1, 0, 64), W(mt, o, o + 64, 1, 64, 128), Op.add, Op.add)
        for k in range(2):
            tt(W(c, 0, 4, 1, 32 * k, 32 * k + 32), W(z, 63, 256, 64, 0, 32), W(z, 63, 256, 64, 32, 64), Op.add)
        for k in range(2):
            cp(W("off%d" % t, 0, 4, 1, 64 * k, 64 * k + 64), W(c, 0, 4, 1, 0, 64))
        cp(W(c, 0, 4, 1, 64, 128), W(c, 0, 4, 1, 0, 64), "s")
        return W(c, 0, 4)

    def lost(t, later, sooner):
        n, s = width(later), str(t)
        tt(W("ng" + s, 0, n), later, sooner, Op.is_le)
        scan(W("pay" + s, 0, n), W("dv" + s, 0, n), W("ng" + s, 0, n), Op.mult, Op.add)

    def gather(t):
        n = "ab"[t]
        src, width_ = "tq", (P, R1 + 64)[t]
        off = "off%d" % t
        sl, la = "sl" + n, "la" + n
        bs = BUILD[t]
        if r in bs:
            d = bs.index(r)
            o = 1 - d
            pick(sl, 32 * o, src, width_, off, 2 * o, 32)
            to = cores[bs[o]]
            for s in ("", "_s"):
                send([(W(sl + s, 32 * o, 32 * o + 32), W(la + s, 32 * r, 32 * r + 32), [to], topo.engines(core, to))], "ha%d" % t)
            pick(la, 32 * r, src, width_, off, 2 * d, 32)
            cnt = 0
            for i in range(N):
                if i != r:
                    cnt += 2 * len(topo.engines(cores[i], core)) // (1 if i in bs else 2)
            lands("ha%d" % t, cnt, [W(la + s, 32 * i, 32 * i + 32) for s in ("", "_s") for i in range(N) if i != r])
        else:
            pick(sl, 0, src, width_, off, 0, 64)
            for s in ("", "_s"):
                send([(W(sl + s, 32 * d, 32 * d + 32), W(la + s, 32 * r, 32 * r + 32), [cores[bs[d]]], topo.engines(core, cores[bs[d]])[d::2])
                      for d in range(2)], "ha%d" % t)

    def numbers(t, w):
        ts(W("wj%d" % t), w, UNIT, Op.mult)

    def buildlist(t, w):
        s, d = str(t), BUILD[t].index(r)
        v = vq = W("wj" + s, 2 * d, 2 * d + 2)
        up = t * (1 - r) % N
        if up:
            vq = W("wk" + s)
            ts(vq, W(w[0], 2 * d, 2 * d + 2), UNIT, Op.mult, 16.0 * up, Op.add)
        ts(W("rk" + s, 0, 2), vq, 4, Op.arith_shift_right, 3, Op.bitwise_and)
        ts(W("rk" + s, 2, 4), v, 2, Op.arith_shift_right, 3, Op.bitwise_and)
        ts(W("rk" + s, 4, 6), v, 3, Op.bitwise_and)
        for y in range(2):
            ts(W("rfo" + s, y, 6, 2), W("rk" + s, y, 6, 2), 32.0, Op.mult, W("kg", y, y + 1), Op.add)

    def build(t):
        s, n, d = str(t), "ab"[t], BUILD[t].index(r)
        la, ps, hh = "la" + n, "ps" + n, "h" + s
        pick(ps, 0, la, 128, "rfo" + s, 0, 96)
        at = 96 if d == 0 else 0
        for b in range(3):
            last = mm(4 + b, "eq", 128 * b, ps, 0)
            cp(W("xs", 64 * b, 64 * b + 64), W("pu", 512 * b + 32, 512 * b + 96), "s")
            tt(W("xd", 32 * b, 32 * b + 32), W("pu", 512 * b, 512 * b + 32), W("xs", 64 * b, 64 * b + 32), Op.subtract)
            tt(W(hh, 4 * at + b, 4 * at + 128, 4), W("xd", 32 * b, 32 * b + 32), W("xs", 64 * b + 32, 64 * b + 64), Op.subtract)
        for x in range(3):
            n = mm(7, ("eq", "en")[x > 0], 0 if x else 384, ps, 32 * x, 128, x == 0, x == 2)
            n["chain"] = last
            last = n
        cp(W(hh, 4 * at + 3, 4 * at + 128, 4), W("pu", 1536, 1568), "vs")
        c = (R1, R2)[t] + 32 * d
        quant("tq", c - at, hh, 0, 128)
        for x in ("", "_s"):
            v = W("tq" + x, c, c + 32)
            send([(v, v, peers, alle)], "hb%d" % t)

    def built(t):
        c = (R1, R2)[t]
        lands("hb%d" % t, sum(2 * len(topo.engines(cores[b], core)) for b in BUILD[t] if b != r),
              [W("tq" + x, c + 32 * d, c + 32 + 32 * d) for x in ("", "_s") for d in range(2) if BUILD[t][d] != r])

    def mapped(t):
        s = str(t)
        ts(W("fi" + s), W("wj" + s), 4, Op.arith_shift_right, 1023, Op.bitwise_and)
        cp(W("ofs" + s), W("fi" + s))
        strew(W("mp"), W("ofs" + s), W("va" if t == 0 else "vb"))

    def products(t):
        for o in range(2):
            bank = 2 - 2 * t + o
            mm(bank, "wq", 128 * o, "tq", (R1, R2)[t] - side[t])
            v = W("yn", 128 * t + 64 * o, 128 * t + 64 * o + 64)
            cp(v, W("pa", 512 * bank + side[t], 512 * bank + side[t] + 64), "vs")
            strew(W("yb%d" % o), W("ofs%d" % t), v)

    def stripes(t, w):
        s, o = str(t), 128 * t
        act(W("er" + s), w, Act.Copy, off=W("ofr"))
        turn(W("lr", 64 * t, 64 * t + 64), W("er" + s))
        top = 1 if t else 128
        a = W("lr", 64 * t, 64 * t + 64, 1, 0, top)
        b = c = W("bi", 64 * t, 64 * t + 64, 1, 0, top)
        ts(b, a, UNIT, Op.mult)
        if t * r:
            c = W("bk", 0, 64, 1, 0, 1)
            ts(c, a, UNIT, Op.mult, 16.0 * (256 - r), Op.add)
        ts(W("bj", o, o + 64, 1, 0, top), c, 4, Op.arith_shift_right, 255, Op.bitwise_and)
        ts(W("bj", o + 64, o + 128, 1, 0, top), b, 12, Op.arith_shift_right, 3, Op.bitwise_and)
        cp(W("bsf", o, o + 128, 1, 0, 1), W("bj", o, o + 128, 1, 0, 1))

    for h in range(2):
        scan(C("sc", h, h + 1, 58, 97), W("l0", 16 + 4 * h, 328, 8), W("l0", 1 + 4 * h, 312, 8), Op.subtract, Op.add)
        act(W("ga", 6 * h, 6 * h + 4), W("l0", 18 + 4 * h, 48, 8), Act.Abs)
    scan(W("gx"), W("d0m"), W("ga"), Op.max, Op.mult, HUGE)
    lost(0, W("gx", 1, 11), W("gx", 0, 10))
    count(0)
    w0 = listed(0)
    gather(0)
    numbers(0, w0)
    if r in BUILD[0]:
        buildlist(0, w0)
        build(0)
    built(0)
    mapped(0)
    stripes(0, w0)
    tt(W("dj"), W("bj", 0, 64), W("bj", 64, 128), Op.subtract)
    ts(W("dk"), W("dj"), 127, Op.bitwise_and)
    ts(W("mk"), W("dk"), W("jc", 0, 1), Op.is_equal)
    own(W("mg"), W("mp"), W("ko"))
    scan(W("ms"), W("d0g", 0, 160), W("mg"), Op.add)
    tt(W("o1f"), W("ms", 15, 128, 16), W("kg", 0, 8), Op.max)
    cp(W("o1"), W("o1f"))
    for h in range(2):
        cp(W("o2", 3 * h, 3 * h + 3), W("o1f", 4 * h + 1, 4 * h + 4))
    tt(W("src1"), W("ms", 143, 160, 16), W("i1m"), Op.max)
    tt(W("dv1", 2, 10, 5), W("src1"), W("jp2"), Op.add)

    for b in range(2):
        mm(b, ("uc", "ug")[b], 0, "tq", R1 - side[0])
        tt(W(("winc", "wing")[b], M0, M0 + 64), W("pa", 512 * b + side[0], 512 * b + side[0] + 64), W("mk"), Op.mult)
    for h in range(2):
        take(W("cg", 112 * h, 112 * h + 64), W("winc"), W("o1", 4 * h, 4 * h + 4), "vs"[h])
        scan(C("sc", 2 + h, 3 + h, 0, 97), W("d0c"), W("cg", 112 * h, 112 * h + 97))
    act(W("gg"), W("wing"), Act.Abs, off=W("o2"))
    for h in range(2):
        scan(W("gs", 80 * h, 80 * h + 48), W("d0c", 17, 65), W("gg", 48 * h, 48 * h + 48), Op.max)
    lost(1, W("gs", 31, 144, 16), W("gs", 15, 128, 16))
    count(1)
    w1 = listed(1)
    gather(1)
    numbers(1, w1)
    if r in BUILD[1]:
        buildlist(1, w1)
        build(1)
    built(1)
    products(0)
    mapped(1)
    for x in (0, 16):
        cp(C("md", 0, 16, x, x + 16), W("mp", 256 * r, 256 * r + 256), "s")
    turn(W("fn"), C("md", 0, 16, 0, 32))
    m = W("fn", 0, 512, 32)
    ts(W("fa"), m, M0 + 64.0, Op.is_ge, R2 - R1 - 64.0, Op.mult)
    tt(W("fb"), W("fa"), m, Op.add)
    tt(W("fc"), W("fb"), W("kgm"), Op.max)
    ts(W("fou"), W("fc"), float(R1 - M0), Op.add)
    stripes(1, w1)
    store("y", lambda T: T.bs[:, :], W("bsf", 0, 256, 1, 0, 1), "dbs")

    products(1)
    for c in range(2):
        pick("ou", 128 * c, "tq", R2 + 64, "fou", 8 * c, 128)

    def scales(k):
        store("ys"[k % 2], lambda T: T.osc[4 * k:4 * k + 4, 0:256], W("ou_s", 0, 256, 1, 32 * k, 32 * k + 4), ("doc", "dos")[k % 2], [W("yb1")])

    def block(o):
        store("ys"[o], lambda T: T.y[:, 256 * o:256 * o + 256], W("yb%d" % o, 256 * r, 256 * r + 256), "dy%d" % o)

    store("y", lambda T: T.oc[:, 0:512], W("ou", 0, 128), "doc")
    store("y", lambda T: T.oc[:, 512:1024], W("ou", 128, 256), "doc")
    block(0)
    block(1)
    for k in range(4):
        scales(k)
    return nodes


def viewer(T):
    def ap(w):
        n, c0, c1, st, p0, p1 = w[:6]
        if len(w) > 6:
            a0, a1, b0, b1 = w[6]
            return T[n][p0:p1, a0, b0:b1] if a1 == a0 + 1 else T[n][p0:p1, a0:a1, b0:b1]
        n, at = LOG[n][:2]
        c0, c1 = c0 + at, c1 + at
        return T[n][p0:p1, c0:c1] if st == 1 else T[n][p0:p1, c0:c1:st]
    return ap


def rank_program(g, core, T, topo):
    r = T.rank_of(core)
    if r is None:
        return
    nodes = calls(r, list(T.cores), topo)
    queue = {"v": g.vector, "s": g.scalar, "t": g.tensor, "g": g, "y": g.sync}
    total, known, snap, log = {}, {q: {} for q in queue}, {}, {}
    env = dict(queue, T=T, ap=viewer(T))

    def wait(q, tok):
        s, v = tok
        if known[q].get(s, 0) >= v:
            return
        queue[q].wait_ge(T.sem[s], v)
        known[q][s] = v
        for a, b in snap.get(tok, {}).items():
            if known[q].get(a, 0) < b:
                known[q][a] = b

    cross = 0
    for i in range(0, len(ORDER[r]), 2):
        v = int(ORDER[r][i:i + 2], 36)
        n = nodes[v // 2]
        q = "vs"[v % 2] if len(n["fns"]) > 1 else list(n["fns"])[0]
        s = n["sem"] or _QS[q]
        if q != "r":
            need = {}
            for ws, isw in ((n["rd"], False), (n["wr"], True)):
                for w in ws:
                    for w2, isw2, tok, q2 in log.get(w[0], ()):
                        if (isw or isw2 or (w[0] in ("pa", "pu") and q != q2)) and meet(w, w2):
                            need[tok[0]] = max(need.get(tok[0], 0), tok[1])
            if n.get("chain"):
                need.pop("st", None)
            if q == "v" and n["kind"] == 1 and cross:
                need["sv"] = max(need.get("sv", 0), cross)
            for x in sorted(need):
                wait(q, (x, need[x]))
            ins = n["fns"][q](env)
            total[s] = total.get(s, 0) + n["by"]
            if q == "v" and n["kind"] == 2:
                cross = total[s]
            if not n["cast"]:
                ins.then_inc(T.sem[s], n["by"])
                snap[(s, total[s])] = dict(known[q])
        else:
            total[s] = n["by"]
        for ws, isw in ((n["rd"], False), (n["wr"], True)):
            for w in ws:
                log.setdefault(w[0], []).append((w, isw, (s, total[s]), q))
    for s in sorted(total, key=lambda s: (s in ("doc", "dos", "dy0", "dy1"), s)):
        wait("g", (s, total[s]))
